import numpy as np
import ml_dtypes


def mxq(x, axis, fmt="e4m3"):
    dtype, down = {"e4m3": (ml_dtypes.float8_e4m3fn, 7), "e5m2": (ml_dtypes.float8_e5m2, 14)}[fmt]
    v = np.moveaxis(np.asarray(x, np.float32).astype(ml_dtypes.bfloat16).astype(np.float64), axis, -1)
    blocks = v.reshape(v.shape[:-1] + (-1, 32))
    amax = np.abs(blocks).max(-1, keepdims=True)
    byte = np.maximum(np.where(amax > 0, np.frexp(amax)[1] - 1 + 127, 0) - down, 1)
    scale = np.exp2(byte - 127.0)
    codes = (blocks / scale).astype(np.float32).astype(dtype).astype(np.float64)
    return np.moveaxis((codes * scale).reshape(v.shape), -1, axis)


WIDE = False


def mx_kscale(k):
    if not WIDE:
        return np.ones(k)
    levels = np.array([10, -10, 5, -5, 0])
    if k % 512:
        return np.exp2(np.random.permutation(np.resize(levels, k // 32))).repeat(32)
    a = np.empty((k // 512, 16))
    for p in range(k // 512):
        a[p, :8] = np.random.permutation(np.resize(levels, 8))
        for g in range(8):
            far = levels[np.abs(levels - a[p, g]) >= 10]
            a[p, g + 8] = far[np.random.randint(len(far))]
    return np.exp2(a.ravel()).repeat(32)


def f64(x):
    return np.asarray(x).astype(np.float64)


def striped(idx):
    return np.tile(idx.reshape(-1, 16).T, (8, 1)).astype(np.uint16)


def unstriped(offs):
    return offs[:16].T.reshape(-1).astype(np.int64)


E2M1 = np.array([0.0, 0.5, 1.0, 1.5, 2.0, 3.0, 4.0, 6.0, -0.0, -0.5, -1.0, -1.5, -2.0, -3.0, -4.0, -6.0])


def pack_weight(w, fmt):
    k, n = w.shape
    w = f64(np.asarray(w, np.float32).astype(ml_dtypes.bfloat16)).reshape(k // 32, 32, n)
    amax = np.abs(w).max(1)
    if fmt == "e4m3":
        byte = np.frexp(amax)[1] - 1 + 127 - 7
    else:
        mant, ex = np.frexp(amax / 6.0)
        byte = np.where(mant > 0.5, ex, ex - 1) + 127
    byte = np.clip(np.where(amax > 0, byte, 1), 1, 254)
    scaled = (w * np.exp2(127.0 - byte)[:, None, :]).reshape(k, n).astype(np.float32)
    by_word = np.ascontiguousarray(scaled.reshape(k // 512, 128, 4, n).transpose(0, 1, 3, 2))
    if fmt == "e4m3":
        words = by_word.astype(ml_dtypes.float8_e4m3fn).view(np.uint8)
    else:
        c = by_word.astype(ml_dtypes.float4_e2m1fn).view(np.uint8) & 0xF
        words = (c[..., 0::2] | (c[..., 1::2] << 4)).reshape(k // 512, 128, 2 * n)
    return np.ascontiguousarray(words), np.ascontiguousarray(byte.astype(np.uint8).reshape(k // 512, 16, n))


def unpack_weight(words, scales, fmt):
    g, _, n = scales.shape
    words = np.ascontiguousarray(words).reshape(g, 128, n, -1)
    if fmt == "e4m3":
        vals = words.view(ml_dtypes.float8_e4m3fn).astype(np.float64)
    else:
        nib = np.empty((g, 128, n, 4), np.uint8)
        nib[..., 0::2] = words & 0xF
        nib[..., 1::2] = words >> 4
        vals = E2M1[nib]
    vals = vals * np.repeat(np.exp2(scales.astype(np.float64) - 127.0), 8, axis=1)[..., None]
    return vals.transpose(0, 1, 3, 2).reshape(g * 512, n)


def gelu(v):
    return 0.5 * v * (1.0 + np.tanh(np.sqrt(2.0 / np.pi) * (v + 0.044715 * v**3)))


def striped8(idx):
    return np.concatenate([v.reshape(-1, 16).T for v in idx]).astype(np.uint16)


def unstriped8(offs):
    return np.stack([offs[16 * g:16 * g + 16].T.reshape(-1) for g in range(8)]).astype(np.int64)


def heads(h, wgt, idx8):
    r = np.arange(h.shape[0])
    return wgt[r // 4 % 128] * h[r[:, None], idx8[r % 512 // 64]]


K, T, S, H, P, N = 1024, 2048, 1024, 1536, 512, 768

def setup_inputs():
    n = np.random.standard_normal
    s = mx_kscale(K)[:, None]
    u = mx_kscale(H)[:, None]
    tab_words, tab_scales = pack_weight(n((K, T)) * s, "e4m3")
    w1_words, w1_scales = pack_weight(n((K, H)) / np.sqrt(K) / s, "e2m1")
    return {
        "tab_words": tab_words, "tab_scales": tab_scales,
        "offs": striped(np.random.permutation(T)[:S]),
        "w1_words": w1_words, "w1_scales": w1_scales,
        "b1": (0.4 * n(H)).astype(np.float32),
        "offs2": striped8(np.stack([np.random.permutation(S)[:P] for _ in range(8)])),
        "wgt": np.repeat(np.random.uniform(0.5, 2.0, (8, P)), 16, axis=0).astype(np.float32),
        "gain": (np.exp(0.3 * n(H)) * u[:, 0]).astype(np.float32),
        "ws": (n((H, N)) / np.sqrt(H) / u).astype(np.float32),
    }

def reference(tab_words, tab_scales, offs, w1_words, w1_scales, b1, offs2, wgt, gain, ws):
    v = unpack_weight(tab_words, tab_scales, "e4m3")[:, unstriped(offs)]
    w1 = unpack_weight(w1_words, w1_scales, "e2m1")
    h = (w1.T @ v) + f64(b1)[:, None]
    x = heads(h, f64(wgt), unstriped8(offs2))
    silu = x / (1.0 + np.exp(-x))
    z = (silu + x) * f64(gain)[:, None]
    out = mxq(f64(ws), 0, "e4m3").T @ mxq(z, 0, "e4m3")
    return out

@@ -1,0 +1,226 @@
+from contextlib import ExitStack
+
+import concourse.mybir as mybir
+
+K, T, S, H, SLOTS, N = 1024, 2048, 1024, 1536, 512, 768
+FLOPS = 2 * K * H * S + 2 * H * N * SLOTS
+
+F32 = mybir.dt.float32
+BF16 = mybir.dt.bfloat16
+I32 = mybir.dt.int32
+U32 = mybir.dt.uint32
+U16 = mybir.dt.uint16
+U8 = mybir.dt.uint8
+FP8X4 = mybir.dt.float8_e4m3fn_x4
+FP4X4 = mybir.dt.float4_e2m1fn_x4
+ACT = mybir.ActivationFunctionType
+ALU = mybir.AluOpType
+
+P = 128
+PACK = 4
+PASS = P * PACK
+K_PASSES = K // PASS
+H_PASSES = H // PASS
+BANK = 512
+HALF = SLOTS // 2
+RUN = 4
+WS_PIECE = 256
+SHIFT_ROWS = 112
+
+
+def tile_list_draft_tree_sketch_kernel(tc, tab_words, tab_scales, offs, w1_words, w1_scales, b1, offs2, wgt, gain, ws, out):
+    nc = tc.nc
+    with ExitStack() as ctx:
+        keep = ctx.enter_context(tc.tile_pool(name="keep", bufs=1))
+        ring = ctx.enter_context(tc.tile_pool(name="ring", bufs=8))
+        psum = ctx.enter_context(tc.psum_pool(name="psum", bufs=8))
+
+        def tile(shape, dtype, name):
+            return keep.tile(shape, dtype, name=name, align_bytes=64)
+
+        live = tile([P, S // 16], U16, "live")
+        picks = tile([P, SLOTS // 16], U16, "picks")
+        w1s_raw = tile([P, H], U8, "w1s_raw")
+        ts_raw = tile([P, T], U8, "ts_raw")
+        w1s = [tile([P, H], U8, "w1s%d" % a) for a in range(K_PASSES)]
+        ts = [tile([P, S], U8, "ts%d" % a) for a in range(K_PASSES)]
+        w1_first = tile([P, K_PASSES, PASS // 2], I32, "w1_first")
+        w1_rest = tile([P, K_PASSES, (H - PASS) // 2], I32, "w1_rest")
+        w1p = [tile([P, K_PASSES, PASS * 2], U8, "w1p%d" % b) for b in range(H_PASSES)]
+        tab = [tile([P, T], I32, "tab%d" % a) for a in range(K_PASSES)]
+        v = [[tile([P, BANK], U32, "v%d_%d" % (a, j)) for j in range(2)] for a in range(K_PASSES)]
+        bias = tile([P, H_PASSES, PACK], F32, "bias")
+        gains = tile([P, H_PASSES, PACK], F32, "gains")
+        strength = tile([P, SLOTS], F32, "strength")
+        ws_raw = [tile([P, PACK, N], F32, "ws_raw%d" % b) for b in range(H_PASSES)]
+        ws_bf = [tile([P, N, PACK], BF16, "ws_bf%d" % b) for b in range(H_PASSES)]
+        ws_q = [tile([P, N], U32, "ws_q%d" % b) for b in range(H_PASSES)]
+        ws_s = [tile([P, N], U8, "ws_s%d" % b) for b in range(H_PASSES)]
+        h = {}
+        warm = tile([P, 2], F32, "warm")
+
+        nc.vector.memset(w1s_raw[:].bitcast(I32), 0)
+        nc.vector.memset(ts_raw[:].bitcast(I32), 0)
+        nc.vector.memset(warm[:], 0.0)
+        nc.scalar.activation(warm[:, 1:2], warm[:, 0:1], ACT.Sigmoid)
+        nc.vector.memset(w1s[1][:].bitcast(I32), 0)
+        nc.vector.memset(ts[1][:].bitcast(I32), 0)
+
+        w1_i32 = w1_words.bitcast(I32).rearrange("a p c -> p a c")
+        nc.sync.dma_start(w1_first[:], w1_i32[:, :, 0 : PASS // 2])
+        for q in range(4):
+            nc.sync.dma_start(w1s_raw[32 * q : 32 * q + 8, :].bitcast(I32), w1_scales[:, 4 * q : 4 * q + 4, :].bitcast(I32))
+        nc.sync.dma_start(live[:], offs)
+        for q in range(4):
+            nc.sync.dma_start(ts_raw[32 * q : 32 * q + 8, :].bitcast(I32), tab_scales[:, 4 * q : 4 * q + 4, :].bitcast(I32))
+        for a in range(K_PASSES):
+            nc.sync.dma_start(tab[a][:], tab_words[a].rearrange("p t i -> p (t i)").bitcast(I32))
+        nc.sync.dma_start(bias[:], b1.rearrange("(b p t) -> p b t", p=P, t=PACK))
+        nc.sync.dma_start(picks[:], offs2)
+        nc.sync.dma_start(w1_rest[:], w1_i32[:, :, PASS // 2 : H // 2])
+        nc.sync.dma_start(strength[:], wgt)
+        nc.sync.dma_start(gains[:], gain.rearrange("(b p t) -> p b t", p=P, t=PACK))
+        for b in range(H_PASSES):
+            nc.sync.dma_start(ws_raw[b][:], ws[PASS * b : PASS * (b + 1), :].rearrange("(p t) n -> p t n", t=PACK))
+
+        def order_w1(b):
+            src = w1_first[:] if b == 0 else w1_rest[:, :, (b - 1) * PASS // 2 : b * PASS // 2]
+            nc.vector.tensor_copy(
+                w1p[b][:].bitcast(U16).rearrange("p a (t m) -> p a t m", t=PACK),
+                src.bitcast(U16).rearrange("p a (m t) -> p a t m", t=PACK),
+            )
+
+        def shift_rows(dst, src):
+            nc.scalar.dma_start(dst[0:SHIFT_ROWS, :].bitcast(I32), src[4 : 4 + SHIFT_ROWS, :].bitcast(I32))
+
+        order_w1(0)
+        nc.vector.tensor_copy(
+            w1s[0][:].rearrange("p (b t m) -> p b t m", t=PACK, m=P),
+            w1s_raw[:].rearrange("p (b m t) -> p b t m", t=PACK, m=P),
+        )
+        shift_rows(w1s[1], w1s[0])
+        nc.vector.tensor_copy(ts[0][:], ts_raw[:].indirect(live[:]))
+        shift_rows(ts[1], ts[0])
+        for j in range(2):
+            for a in range(K_PASSES):
+                nc.vector.tensor_copy(v[a][j][:], tab[a][:].bitcast(U32).indirect(live[:, 32 * j : 32 * (j + 1)]))
+        order_w1(1)
+        order_w1(2)
+
+        def project(r, j):
+            b, t = divmod(r, PACK)
+            if j == 0:
+                h[r] = ring.tile([P, S], F32, name="h", tag="h")
+            acc = psum.tile([P, BANK], F32, name="acc", tag="bank")
+            for a in range(K_PASSES):
+                nc.tensor.matmul_mx(
+                    acc[:],
+                    lhsT=w1p[b][:, a, 2 * P * t : 2 * P * (t + 1)].bitcast(FP4X4),
+                    lhsT_scale=w1s[a][:, P * r : P * (r + 1)],
+                    rhs=v[a][j][:].bitcast(FP8X4),
+                    rhs_scale=ts[a][:, BANK * j : BANK * (j + 1)],
+                    start=(a == 0),
+                    stop=(a == K_PASSES - 1),
+                )
+            nc.scalar.activation(h[r][:, BANK * j : BANK * (j + 1)], acc[:], ACT.Identity, bias=bias[:, b, t : t + 1])
+
+        def weave_ws(b, i):
+            cols = slice(WS_PIECE * i, WS_PIECE * (i + 1))
+            nc.scalar.copy(
+                ws_bf[b][:, cols, :].rearrange("p (c i) t -> p c t i", i=RUN),
+                ws_raw[b][:, :, cols].rearrange("p t (c i) -> p c t i", i=RUN),
+            )
+
+        def quantize_ws(b, lo, hi):
+            nc.vector.quantize_mx(ws_q[b][:, lo:hi].bitcast(FP8X4), ws_s[b][:, lo:hi], ws_bf[b][:, lo:hi, :].rearrange("p n t -> p (n t)"))
+
+        units = [(0, 0, SLOTS), (1, 0, SLOTS), (2, 0, HALF), (2, HALF, HALF)]
+        x = [tile([P, PACK, w], F32, "x%d" % u) for u, (b, c, w) in enumerate(units)]
+        f = [tile([P, PACK, w], F32, "f%d" % u) for u, (b, c, w) in enumerate(units)]
+        z = [tile([P, w, PACK], BF16, "z%d" % u) for u, (b, c, w) in enumerate(units)]
+        z_q = [tile([P, w], U32, "z_q%d" % u) for u, (b, c, w) in enumerate(units)]
+        z_s = [tile([P, w], U8, "z_s%d" % u) for u, (b, c, w) in enumerate(units)]
+
+        def pick(u, t):
+            b, c, w = units[u]
+            nc.vector.tensor_tensor(x[u][:, t, :], h[PACK * b + t][:].indirect(picks[:, c // 16 : (c + w) // 16]), strength[:, c : c + w], ALU.mult)
+            nc.scalar.activation(f[u][:, t, :], x[u][:, t, :], ACT.Sigmoid)
+
+        def factor(u, t):
+            g = gains[:, units[u][0], t : t + 1]
+            nc.vector.tensor_scalar(f[u][:, t, :], f[u][:, t, :], g, g, ALU.mult, ALU.add)
+
+        def weave_z(u):
+            nc.vector.tensor_tensor(
+                z[u][:].rearrange("p (c i) t -> p c t i", i=RUN),
+                x[u][:].rearrange("p t (c i) -> p c t i", i=RUN),
+                f[u][:].rearrange("p t (c i) -> p c t i", i=RUN),
+                ALU.mult,
+            )
+
+        def quantize_z(u):
+            nc.vector.quantize_mx(z_q[u][:].bitcast(FP8X4), z_s[u][:], z[u][:].rearrange("p m t -> p (m t)"))
+
+        scores = {}
+
+        def score(half, b):
+            u, c = (b, HALF * half) if b < 2 else (2 + half, 0)
+            for j in range(3):
+                if b == 0:
+                    scores[half, j] = psum.tile([P, 2, HALF], F32, name="score", tag="bank")
+                for e in range(2):
+                    n = 2 * j + e
+                    nc.tensor.matmul_mx(
+                        scores[half, j][:, e, :],
+                        lhsT=ws_q[b][:, P * n : P * (n + 1)].bitcast(FP8X4),
+                        lhsT_scale=ws_s[b][:, P * n : P * (n + 1)],
+                        rhs=z_q[u][:, c : c + HALF].bitcast(FP8X4),
+                        rhs_scale=z_s[u][:, c : c + HALF],
+                        start=(b == 0 and e == 0),
+                        stop=(b == H_PASSES - 1 and e == 1),
+                    )
+
+        def store(half, j, on_vector):
+            res = tile([P, 2, HALF], F32, "res%d_%d" % (half, j))
+            if on_vector:
+                nc.vector.tensor_copy(res[:], scores[half, j][:])
+            else:
+                nc.scalar.copy(res[:], scores[half, j][:])
+            nc.sync.dma_start(out[2 * P * j : 2 * P * (j + 1), HALF * half : HALF * (half + 1)].rearrange("(e p) m -> p e m", p=P), res[:])
+
+        for j in range(2):
+            for r in range(PACK):
+                project(r, j)
+
+        steps = [(u, t) for u in range(len(units)) for t in range(PACK)]
+        for s, (u, t) in enumerate(steps):
+            pick(u, t)
+            if s + PACK < H_PASSES * PACK:
+                project(s + PACK, 0)
+                project(s + PACK, 1)
+            if s < 9:
+                weave_ws(*divmod(s, 3))
+            if s > 0:
+                factor(*steps[s - 1])
+            if u > 0 and t == 1:
+                weave_z(u - 1)
+            if u > 0 and t == 2:
+                quantize_z(u - 1)
+            if s in (3, 6, 9):
+                quantize_ws(s // 3 - 1, 0, 512)
+            if s in (4, 7, 10):
+                quantize_ws(s // 3 - 1, 512, N)
+            if s == 11:
+                for b in range(2):
+                    for half in range(2):
+                        score(half, b)
+            if s == 14:
+                score(0, 2)
+        factor(*steps[-1])
+        for j in range(3):
+            store(0, j, False)
+        weave_z(3)
+        quantize_z(3)
+        score(1, 2)
+        for j in range(3):
+            store(1, j, j != 1)

@@ -23,68 +23,77 @@ K_PASSES = K // PASS
 H_PASSES = H // PASS
 BANK = 512
 HALF = SLOTS // 2
-RUN = 4
+RUN = 2
 WS_PIECE = 256
 SHIFT_ROWS = 112
+WS_BYTES = PACK * N * 4
+TAB_BYTES = T * 4
+AT_WS = (WS_BYTES + S, 0, WS_BYTES + S)
+AT_TAB = (WS_BYTES + S, WS_BYTES - TAB_BYTES)
+AT_TS = WS_BYTES
+AT_W1_FIRST = WS_BYTES - 512
+AT_TS_RAW = 2 * WS_BYTES + S
+AT_W1S = AT_TS_RAW
+AT_W1_REST = AT_W1S + H
+AT_W1S_RAW = AT_W1_REST + 4 * (H - PASS)
+AT_CONSTS = AT_W1S_RAW
 
 
 def tile_list_draft_tree_sketch_kernel(tc, tab_words, tab_scales, offs, w1_words, w1_scales, b1, offs2, wgt, gain, ws, out):
     nc = tc.nc
     with ExitStack() as ctx:
         keep = ctx.enter_context(tc.tile_pool(name="keep", bufs=1))
-        ring = ctx.enter_context(tc.tile_pool(name="ring", bufs=8))
+        ring = ctx.enter_context(tc.tile_pool(name="ring", bufs=12))
+        stage = ctx.enter_context(tc.tile_pool(name="stage", bufs=1))
         psum = ctx.enter_context(tc.psum_pool(name="psum", bufs=8))
 
         def tile(shape, dtype, name):
             return keep.tile(shape, dtype, name=name, align_bytes=64)
 
+        def staged(shape, dtype, name, offset):
+            return stage.tile(shape, dtype, name=name, align_bytes=64, offset=offset)
+
         live = tile([P, S // 16], U16, "live")
         picks = tile([P, SLOTS // 16], U16, "picks")
-        w1s_raw = tile([P, H], U8, "w1s_raw")
-        ts_raw = tile([P, T], U8, "ts_raw")
-        w1s = [tile([P, H], U8, "w1s%d" % a) for a in range(K_PASSES)]
-        ts = [tile([P, S], U8, "ts%d" % a) for a in range(K_PASSES)]
-        w1_first = tile([P, K_PASSES, PASS // 2], I32, "w1_first")
-        w1_rest = tile([P, K_PASSES, (H - PASS) // 2], I32, "w1_rest")
+        w1s_raw = staged([P, H], U8, "w1s_raw", AT_W1S_RAW)
+        ts_raw = staged([P, T], U8, "ts_raw", AT_TS_RAW)
+        w1s = {1: tile([P, H], U8, "w1s1")}
+        ts = {1: tile([P, S], U8, "ts1")}
         w1p = [tile([P, K_PASSES, PASS * 2], U8, "w1p%d" % b) for b in range(H_PASSES)]
-        tab = [tile([P, T], I32, "tab%d" % a) for a in range(K_PASSES)]
+        tab = {}
         v = [[tile([P, BANK], U32, "v%d_%d" % (a, j)) for j in range(2)] for a in range(K_PASSES)]
-        bias = tile([P, H_PASSES, PACK], F32, "bias")
-        gains = tile([P, H_PASSES, PACK], F32, "gains")
-        strength = tile([P, SLOTS], F32, "strength")
-        ws_raw = [tile([P, PACK, N], F32, "ws_raw%d" % b) for b in range(H_PASSES)]
+        ws_raw = {}
         ws_bf = [tile([P, N, PACK], BF16, "ws_bf%d" % b) for b in range(H_PASSES)]
         ws_q = [tile([P, N], U32, "ws_q%d" % b) for b in range(H_PASSES)]
         ws_s = [tile([P, N], U8, "ws_s%d" % b) for b in range(H_PASSES)]
         h = {}
-        warm = tile([P, 2], F32, "warm")
 
-        nc.vector.memset(w1s_raw[:].bitcast(I32), 0)
         nc.vector.memset(ts_raw[:].bitcast(I32), 0)
+        nc.vector.memset(w1s_raw[:].bitcast(I32), 0)
+        warm = tile([P, 2], F32, "warm")
         nc.vector.memset(warm[:], 0.0)
         nc.scalar.activation(warm[:, 1:2], warm[:, 0:1], ACT.Sigmoid)
         nc.vector.memset(w1s[1][:].bitcast(I32), 0)
         nc.vector.memset(ts[1][:].bitcast(I32), 0)
 
         w1_i32 = w1_words.bitcast(I32).rearrange("a p c -> p a c")
-        nc.sync.dma_start(w1_first[:], w1_i32[:, :, 0 : PASS // 2])
-        for q in range(4):
-            nc.sync.dma_start(w1s_raw[32 * q : 32 * q + 8, :].bitcast(I32), w1_scales[:, 4 * q : 4 * q + 4, :].bitcast(I32))
-        nc.sync.dma_start(live[:], offs)
-        for q in range(4):
-            nc.sync.dma_start(ts_raw[32 * q : 32 * q + 8, :].bitcast(I32), tab_scales[:, 4 * q : 4 * q + 4, :].bitcast(I32))
-        for a in range(K_PASSES):
-            nc.sync.dma_start(tab[a][:], tab_words[a].rearrange("p t i -> p (t i)").bitcast(I32))
-        nc.sync.dma_start(bias[:], b1.rearrange("(b p t) -> p b t", p=P, t=PACK))
-        nc.sync.dma_start(picks[:], offs2)
-        nc.sync.dma_start(w1_rest[:], w1_i32[:, :, PASS // 2 : H // 2])
-        nc.sync.dma_start(strength[:], wgt)
-        nc.sync.dma_start(gains[:], gain.rearrange("(b p t) -> p b t", p=P, t=PACK))
-        for b in range(H_PASSES):
-            nc.sync.dma_start(ws_raw[b][:], ws[PASS * b : PASS * (b + 1), :].rearrange("(p t) n -> p t n", t=PACK))
 
-        def order_w1(b):
-            src = w1_first[:] if b == 0 else w1_rest[:, :, (b - 1) * PASS // 2 : b * PASS // 2]
+        def load_scale_rows(dst, scales):
+            for q in range(4):
+                nc.sync.dma_start(dst[32 * q : 32 * q + 8, :].bitcast(I32), scales[:, 4 * q : 4 * q + 4, :].bitcast(I32))
+
+        def load_table(a):
+            tab[a] = staged([P, T], I32, "tab%d" % a, AT_TAB[a])
+            nc.sync.dma_start(tab[a][:], tab_words[a].rearrange("p t i -> p (t i)").bitcast(I32))
+
+        w1_first = staged([P, K_PASSES, PASS // 2], I32, "w1_first", AT_W1_FIRST)
+        nc.sync.dma_start(w1_first[:], w1_i32[:, :, 0 : PASS // 2])
+        nc.sync.dma_start(live[:], offs)
+        nc.sync.dma_start(picks[:], offs2)
+        load_scale_rows(ts_raw, tab_scales)
+        load_scale_rows(w1s_raw, w1_scales)
+
+        def order_w1(b, src):
             nc.vector.tensor_copy(
                 w1p[b][:].bitcast(U16).rearrange("p a (t m) -> p a t m", t=PACK),
                 src.bitcast(U16).rearrange("p a (m t) -> p a t m", t=PACK),
@@ -93,36 +102,75 @@ def tile_list_draft_tree_sketch_kernel(tc, tab_words, tab_scales, offs, w1_words
         def shift_rows(dst, src):
             nc.scalar.dma_start(dst[0:SHIFT_ROWS, :].bitcast(I32), src[4 : 4 + SHIFT_ROWS, :].bitcast(I32))
 
-        order_w1(0)
+        def gather_words(a, j):
+            nc.vector.tensor_copy(v[a][j][:], tab[a][:].bitcast(U32).indirect(live[:, 32 * j : 32 * (j + 1)]))
+
+        acc = {}
+
+        def project_pass(r, j, a):
+            b, t = divmod(r, PACK)
+            if a == 0:
+                acc[r, j] = psum.tile([P, BANK], F32, name="acc", tag="bank")
+            nc.tensor.matmul_mx(
+                acc[r, j][:],
+                lhsT=w1p[b][:, a, 2 * P * t : 2 * P * (t + 1)].bitcast(FP4X4),
+                lhsT_scale=w1s[a][:, P * r : P * (r + 1)],
+                rhs=v[a][j][:].bitcast(FP8X4),
+                rhs_scale=ts[a][:, BANK * j : BANK * (j + 1)],
+                start=(a == 0),
+                stop=(a == K_PASSES - 1),
+            )
+
+        def add_bias(r, j):
+            b, t = divmod(r, PACK)
+            if j == 0:
+                h[r] = ring.tile([P, S], F32, name="h", tag="h")
+            nc.scalar.activation(h[r][:, BANK * j : BANK * (j + 1)], acc[r, j][:], ACT.Identity, bias=bias[:, b, t : t + 1])
+
+        def project(r, j):
+            for a in range(K_PASSES):
+                project_pass(r, j, a)
+            add_bias(r, j)
+
+        order_w1(0, w1_first[:])
+        load_table(0)
+        load_table(1)
+        ts[0] = staged([P, S], U8, "ts0", AT_TS)
+        nc.vector.tensor_copy(ts[0][:], ts_raw[:].indirect(live[:]))
+        shift_rows(ts[1], ts[0])
+        w1_rest = staged([P, K_PASSES, (H - PASS) // 2], I32, "w1_rest", AT_W1_REST)
+        w1s[0] = staged([P, H], U8, "w1s0", AT_W1S)
+        nc.sync.dma_start(w1_rest[:], w1_i32[:, :, PASS // 2 : H // 2])
         nc.vector.tensor_copy(
             w1s[0][:].rearrange("p (b t m) -> p b t m", t=PACK, m=P),
             w1s_raw[:].rearrange("p (b m t) -> p b t m", t=PACK, m=P),
         )
         shift_rows(w1s[1], w1s[0])
-        nc.vector.tensor_copy(ts[0][:], ts_raw[:].indirect(live[:]))
-        shift_rows(ts[1], ts[0])
-        for j in range(2):
-            for a in range(K_PASSES):
-                nc.vector.tensor_copy(v[a][j][:], tab[a][:].bitcast(U32).indirect(live[:, 32 * j : 32 * (j + 1)]))
-        order_w1(1)
-        order_w1(2)
+        consts = staged([P, 32 + SLOTS], F32, "consts", AT_CONSTS)
+        bias = consts[:, 0:12].rearrange("p (b t) -> p b t", t=PACK)
+        gains = consts[:, 16:28].rearrange("p (b t) -> p b t", t=PACK)
+        strength = consts[:, 32 : 32 + SLOTS]
+        nc.sync.dma_start(bias, b1.rearrange("(b p t) -> p b t", p=P, t=PACK))
+        nc.sync.dma_start(strength, wgt)
+        nc.sync.dma_start(gains, gain.rearrange("(b p t) -> p b t", p=P, t=PACK))
+        for a in range(K_PASSES):
+            for j in range(2):
+                gather_words(a, j)
+                for r in range(2):
+                    project_pass(r, j, a)
+        order_w1(1, w1_rest[:, :, 0 : PASS // 2])
+        for r in range(2):
+            for j in range(2):
+                add_bias(r, j)
+        project(2, 0)
+        project(2, 1)
 
-        def project(r, j):
-            b, t = divmod(r, PACK)
-            if j == 0:
-                h[r] = ring.tile([P, S], F32, name="h", tag="h")
-            acc = psum.tile([P, BANK], F32, name="acc", tag="bank")
-            for a in range(K_PASSES):
-                nc.tensor.matmul_mx(
-                    acc[:],
-                    lhsT=w1p[b][:, a, 2 * P * t : 2 * P * (t + 1)].bitcast(FP4X4),
-                    lhsT_scale=w1s[a][:, P * r : P * (r + 1)],
-                    rhs=v[a][j][:].bitcast(FP8X4),
-                    rhs_scale=ts[a][:, BANK * j : BANK * (j + 1)],
-                    start=(a == 0),
-                    stop=(a == K_PASSES - 1),
-                )
-            nc.scalar.activation(h[r][:, BANK * j : BANK * (j + 1)], acc[:], ACT.Identity, bias=bias[:, b, t : t + 1])
+        def load_ws(b):
+            ws_raw[b] = staged([P, PACK, N], F32, "ws_raw%d" % b, AT_WS[b])
+            nc.sync.dma_start(ws_raw[b][:], ws[PASS * b : PASS * (b + 1), :].rearrange("(p t) n -> p t n", t=PACK))
+
+        load_ws(0)
+        load_ws(1)
 
         def weave_ws(b, i):
             cols = slice(WS_PIECE * i, WS_PIECE * (i + 1))
@@ -144,6 +192,8 @@ def tile_list_draft_tree_sketch_kernel(tc, tab_words, tab_scales, offs, w1_words
         def pick(u, t):
             b, c, w = units[u]
             nc.vector.tensor_tensor(x[u][:, t, :], h[PACK * b + t][:].indirect(picks[:, c // 16 : (c + w) // 16]), strength[:, c : c + w], ALU.mult)
+
+        def gate(u, t):
             nc.scalar.activation(f[u][:, t, :], x[u][:, t, :], ACT.Sigmoid)
 
         def factor(u, t):
@@ -188,34 +238,35 @@ def tile_list_draft_tree_sketch_kernel(tc, tab_words, tab_scales, offs, w1_words
                 nc.scalar.copy(res[:], scores[half, j][:])
             nc.sync.dma_start(out[2 * P * j : 2 * P * (j + 1), HALF * half : HALF * (half + 1)].rearrange("(e p) m -> p e m", p=P), res[:])
 
-        for j in range(2):
-            for r in range(PACK):
-                project(r, j)
-
         steps = [(u, t) for u in range(len(units)) for t in range(PACK)]
         for s, (u, t) in enumerate(steps):
             pick(u, t)
-            if s + PACK < H_PASSES * PACK:
-                project(s + PACK, 0)
-                project(s + PACK, 1)
-            if s < 9:
-                weave_ws(*divmod(s, 3))
-            if s > 0:
-                factor(*steps[s - 1])
-            if u > 0 and t == 1:
-                weave_z(u - 1)
+            if s + 3 < H_PASSES * PACK:
+                project(s + 3, 0)
+                project(s + 3, 1)
+            gate(u, t)
+            if s == 1:
+                order_w1(2, w1_rest[:, :, PASS // 2 : PASS])
+            if 2 <= s < 11:
+                weave_ws(*divmod(s - 2, 3))
+            if s == 4:
+                load_ws(2)
+            if s > 1:
+                factor(*steps[s - 2])
             if u > 0 and t == 2:
+                weave_z(u - 1)
+            if u > 0 and t == 3:
                 quantize_z(u - 1)
-            if s in (3, 6, 9):
-                quantize_ws(s // 3 - 1, 0, 512)
-            if s in (4, 7, 10):
-                quantize_ws(s // 3 - 1, 512, N)
+            if s in (5, 8, 11):
+                quantize_ws((s - 5) // 3, 0, 512)
+            if s in (6, 9, 12):
+                quantize_ws((s - 5) // 3, 512, N)
             if s == 11:
                 for b in range(2):
                     for half in range(2):
                         score(half, b)
-            if s == 14:
-                score(0, 2)
+        score(0, 2)
+        factor(*steps[-2])
         factor(*steps[-1])
         for j in range(3):
             store(0, j, False)

@@ -26,17 +26,18 @@ HALF = SLOTS // 2
 RUN = 2
 WS_PIECE = 256
 SHIFT_ROWS = 112
+H_BANKS = 4
 WS_BYTES = PACK * N * 4
 TAB_BYTES = T * 4
-AT_WS = (WS_BYTES + S, 0, WS_BYTES + S)
-AT_TAB = (WS_BYTES + S, WS_BYTES - TAB_BYTES)
-AT_TS = WS_BYTES
-AT_W1_FIRST = WS_BYTES - 512
-AT_TS_RAW = 2 * WS_BYTES + S
-AT_W1S = AT_TS_RAW
-AT_W1_REST = AT_W1S + H
-AT_W1S_RAW = AT_W1_REST + 4 * (H - PASS)
-AT_CONSTS = AT_W1S_RAW
+AT_WS = (WS_BYTES + H, 0, WS_BYTES + H)
+AT_TAB = (WS_BYTES + H, WS_BYTES - TAB_BYTES)
+AT_W1S = WS_BYTES
+AT_W1_FIRST = WS_BYTES - 256
+AT_W1S_RAW = 2 * WS_BYTES + H
+AT_TS = AT_W1S_RAW
+AT_W1_REST = AT_W1S_RAW + H
+AT_CONSTS = AT_W1_REST + 4 * (H - PASS)
+AT_TS_RAW = AT_CONSTS - T // 2
 
 
 def tile_list_draft_tree_sketch_kernel(tc, tab_words, tab_scales, offs, w1_words, w1_scales, b1, offs2, wgt, gain, ws, out):
@@ -45,7 +46,7 @@ def tile_list_draft_tree_sketch_kernel(tc, tab_words, tab_scales, offs, w1_words
         keep = ctx.enter_context(tc.tile_pool(name="keep", bufs=1))
         ring = ctx.enter_context(tc.tile_pool(name="ring", bufs=12))
         stage = ctx.enter_context(tc.tile_pool(name="stage", bufs=1))
-        psum = ctx.enter_context(tc.psum_pool(name="psum", bufs=8))
+        psum = ctx.enter_context(tc.psum_pool(name="psum", bufs=1))
 
         def tile(shape, dtype, name):
             return keep.tile(shape, dtype, name=name, align_bytes=64)
@@ -68,8 +69,8 @@ def tile_list_draft_tree_sketch_kernel(tc, tab_words, tab_scales, offs, w1_words
         ws_s = [tile([P, N], U8, "ws_s%d" % b) for b in range(H_PASSES)]
         h = {}
 
-        nc.vector.memset(ts_raw[:].bitcast(I32), 0)
         nc.vector.memset(w1s_raw[:].bitcast(I32), 0)
+        nc.vector.memset(ts_raw[:].bitcast(I32), 0)
         warm = tile([P, 2], F32, "warm")
         nc.vector.memset(warm[:], 0.0)
         nc.scalar.activation(warm[:, 1:2], warm[:, 0:1], ACT.Sigmoid)
@@ -90,8 +91,10 @@ def tile_list_draft_tree_sketch_kernel(tc, tab_words, tab_scales, offs, w1_words
         nc.sync.dma_start(w1_first[:], w1_i32[:, :, 0 : PASS // 2])
         nc.sync.dma_start(live[:], offs)
         nc.sync.dma_start(picks[:], offs2)
-        load_scale_rows(ts_raw, tab_scales)
+        bias = tile([P, H_PASSES, 8], F32, "bias")
+        nc.scalar.dma_start(bias[:, :, 0:PACK], b1.rearrange("(b p t) -> p b t", p=P, t=PACK))
         load_scale_rows(w1s_raw, w1_scales)
+        load_scale_rows(ts_raw, tab_scales)
 
         def order_w1(b, src):
             nc.vector.tensor_copy(
@@ -100,7 +103,7 @@ def tile_list_draft_tree_sketch_kernel(tc, tab_words, tab_scales, offs, w1_words
             )
 
         def shift_rows(dst, src):
-            nc.scalar.dma_start(dst[0:SHIFT_ROWS, :].bitcast(I32), src[4 : 4 + SHIFT_ROWS, :].bitcast(I32))
+            nc.sync.dma_start(dst[0:SHIFT_ROWS, :].bitcast(I32), src[4 : 4 + SHIFT_ROWS, :].bitcast(I32))
 
         def gather_words(a, j):
             nc.vector.tensor_copy(v[a][j][:], tab[a][:].bitcast(U32).indirect(live[:, 32 * j : 32 * (j + 1)]))
@@ -110,7 +113,7 @@ def tile_list_draft_tree_sketch_kernel(tc, tab_words, tab_scales, offs, w1_words
         def project_pass(r, j, a):
             b, t = divmod(r, PACK)
             if a == 0:
-                acc[r, j] = psum.tile([P, BANK], F32, name="acc", tag="bank")
+                acc[r, j] = psum.tile([P, BANK], F32, name="acc", tag="bank%d" % (len(acc) % H_BANKS))
             nc.tensor.matmul_mx(
                 acc[r, j][:],
                 lhsT=w1p[b][:, a, 2 * P * t : 2 * P * (t + 1)].bitcast(FP4X4),
@@ -135,22 +138,20 @@ def tile_list_draft_tree_sketch_kernel(tc, tab_words, tab_scales, offs, w1_words
         order_w1(0, w1_first[:])
         load_table(0)
         load_table(1)
-        ts[0] = staged([P, S], U8, "ts0", AT_TS)
-        nc.vector.tensor_copy(ts[0][:], ts_raw[:].indirect(live[:]))
-        shift_rows(ts[1], ts[0])
-        w1_rest = staged([P, K_PASSES, (H - PASS) // 2], I32, "w1_rest", AT_W1_REST)
         w1s[0] = staged([P, H], U8, "w1s0", AT_W1S)
-        nc.sync.dma_start(w1_rest[:], w1_i32[:, :, PASS // 2 : H // 2])
         nc.vector.tensor_copy(
             w1s[0][:].rearrange("p (b t m) -> p b t m", t=PACK, m=P),
             w1s_raw[:].rearrange("p (b m t) -> p b t m", t=PACK, m=P),
         )
         shift_rows(w1s[1], w1s[0])
-        consts = staged([P, 32 + SLOTS], F32, "consts", AT_CONSTS)
-        bias = consts[:, 0:12].rearrange("p (b t) -> p b t", t=PACK)
-        gains = consts[:, 16:28].rearrange("p (b t) -> p b t", t=PACK)
-        strength = consts[:, 32 : 32 + SLOTS]
-        nc.sync.dma_start(bias, b1.rearrange("(b p t) -> p b t", p=P, t=PACK))
+        ts[0] = staged([P, S], U8, "ts0", AT_TS)
+        nc.vector.tensor_copy(ts[0][:], ts_raw[:].indirect(live[:]))
+        shift_rows(ts[1], ts[0])
+        w1_rest = staged([P, K_PASSES, (H - PASS) // 2], I32, "w1_rest", AT_W1_REST)
+        nc.sync.dma_start(w1_rest[:], w1_i32[:, :, PASS // 2 : H // 2])
+        consts = staged([P, 8 * H_PASSES + SLOTS], F32, "consts", AT_CONSTS)
+        gains = consts[:, 0 : 8 * H_PASSES].rearrange("p (b t) -> p b t", t=8)[:, :, 0:PACK]
+        strength = consts[:, 8 * H_PASSES : 8 * H_PASSES + SLOTS]
         nc.sync.dma_start(strength, wgt)
         nc.sync.dma_start(gains, gain.rearrange("(b p t) -> p b t", p=P, t=PACK))
         for a in range(K_PASSES):
@@ -158,12 +159,11 @@ def tile_list_draft_tree_sketch_kernel(tc, tab_words, tab_scales, offs, w1_words
                 gather_words(a, j)
                 for r in range(2):
                     project_pass(r, j, a)
-        order_w1(1, w1_rest[:, :, 0 : PASS // 2])
-        for r in range(2):
-            for j in range(2):
-                add_bias(r, j)
+        for r, j in [(0, 0), (1, 0), (0, 1), (1, 1)]:
+            add_bias(r, j)
         project(2, 0)
         project(2, 1)
+        order_w1(1, w1_rest[:, :, 0 : PASS // 2])
 
         def load_ws(b):
             ws_raw[b] = staged([P, PACK, N], F32, "ws_raw%d" % b, AT_WS[b])
@@ -200,43 +200,47 @@ def tile_list_draft_tree_sketch_kernel(tc, tab_words, tab_scales, offs, w1_words
             g = gains[:, units[u][0], t : t + 1]
             nc.vector.tensor_scalar(f[u][:, t, :], f[u][:, t, :], g, g, ALU.mult, ALU.add)
 
-        def weave_z(u):
+        def weave_z(u, lo, hi):
             nc.vector.tensor_tensor(
-                z[u][:].rearrange("p (c i) t -> p c t i", i=RUN),
-                x[u][:].rearrange("p t (c i) -> p c t i", i=RUN),
-                f[u][:].rearrange("p t (c i) -> p c t i", i=RUN),
+                z[u][:, lo:hi, :].rearrange("p (c i) t -> p c t i", i=RUN),
+                x[u][:, :, lo:hi].rearrange("p t (c i) -> p c t i", i=RUN),
+                f[u][:, :, lo:hi].rearrange("p t (c i) -> p c t i", i=RUN),
                 ALU.mult,
             )
 
-        def quantize_z(u):
-            nc.vector.quantize_mx(z_q[u][:].bitcast(FP8X4), z_s[u][:], z[u][:].rearrange("p m t -> p (m t)"))
+        def quantize_z(u, lo, hi):
+            nc.vector.quantize_mx(z_q[u][:, lo:hi].bitcast(FP8X4), z_s[u][:, lo:hi], z[u][:, lo:hi, :].rearrange("p m t -> p (m t)"))
 
         scores = {}
+        parts = [(0, HALF, 2), (HALF, HALF // 2, 3), (HALF + HALF // 2, HALF // 2, 3)]
 
-        def score(half, b):
-            u, c = (b, HALF * half) if b < 2 else (2 + half, 0)
-            for j in range(3):
-                if b == 0:
-                    scores[half, j] = psum.tile([P, 2, HALF], F32, name="score", tag="bank")
-                for e in range(2):
-                    n = 2 * j + e
-                    nc.tensor.matmul_mx(
-                        scores[half, j][:, e, :],
-                        lhsT=ws_q[b][:, P * n : P * (n + 1)].bitcast(FP8X4),
-                        lhsT_scale=ws_s[b][:, P * n : P * (n + 1)],
-                        rhs=z_q[u][:, c : c + HALF].bitcast(FP8X4),
-                        rhs_scale=z_s[u][:, c : c + HALF],
-                        start=(b == 0 and e == 0),
-                        stop=(b == H_PASSES - 1 and e == 1),
-                    )
+        def score(part, b):
+            c, w, per_bank = parts[part]
+            u = b if b < 2 else 2 + c // HALF
+            lo = c - units[u][1]
+            for n in range(N // P):
+                j, e = divmod(n, per_bank)
+                if b == 0 and e == 0:
+                    scores[part, j] = psum.tile([P, per_bank, w], F32, name="score", tag="bank%d" % ((H_BANKS + len(scores)) % 8))
+                nc.tensor.matmul_mx(
+                    scores[part, j][:, e, :],
+                    lhsT=ws_q[b][:, P * n : P * (n + 1)].bitcast(FP8X4),
+                    lhsT_scale=ws_s[b][:, P * n : P * (n + 1)],
+                    rhs=z_q[u][:, lo : lo + w].bitcast(FP8X4),
+                    rhs_scale=z_s[u][:, lo : lo + w],
+                    start=(b == 0 and e == 0),
+                    stop=(b == H_PASSES - 1 and e == per_bank - 1),
+                )
 
-        def store(half, j, on_vector):
-            res = tile([P, 2, HALF], F32, "res%d_%d" % (half, j))
+        def store(part, j, on_vector):
+            c, w, per_bank = parts[part]
+            res = tile([P, per_bank, w], F32, "res%d_%d" % (part, j))
             if on_vector:
-                nc.vector.tensor_copy(res[:], scores[half, j][:])
+                nc.vector.tensor_copy(res[:], scores[part, j][:])
             else:
-                nc.scalar.copy(res[:], scores[half, j][:])
-            nc.sync.dma_start(out[2 * P * j : 2 * P * (j + 1), HALF * half : HALF * (half + 1)].rearrange("(e p) m -> p e m", p=P), res[:])
+                nc.scalar.copy(res[:], scores[part, j][:])
+            rows = per_bank * P
+            nc.sync.dma_start(out[rows * j : rows * (j + 1), c : c + w].rearrange("(e p) m -> p e m", p=P), res[:])
 
         steps = [(u, t) for u in range(len(units)) for t in range(PACK)]
         for s, (u, t) in enumerate(steps):
@@ -254,24 +258,27 @@ def tile_list_draft_tree_sketch_kernel(tc, tab_words, tab_scales, offs, w1_words
             if s > 1:
                 factor(*steps[s - 2])
             if u > 0 and t == 2:
-                weave_z(u - 1)
+                weave_z(u - 1, 0, units[u - 1][2])
             if u > 0 and t == 3:
-                quantize_z(u - 1)
+                quantize_z(u - 1, 0, units[u - 1][2])
             if s in (5, 8, 11):
                 quantize_ws((s - 5) // 3, 0, 512)
             if s in (6, 9, 12):
                 quantize_ws((s - 5) // 3, 512, N)
             if s == 11:
                 for b in range(2):
-                    for half in range(2):
-                        score(half, b)
+                    for part in range(len(parts)):
+                        score(part, b)
         score(0, 2)
         factor(*steps[-2])
         factor(*steps[-1])
         for j in range(3):
             store(0, j, False)
-        weave_z(3)
-        quantize_z(3)
-        score(1, 2)
-        for j in range(3):
-            store(1, j, j != 1)
+        for lo in (0, HALF // 2):
+            weave_z(3, lo, lo + HALF // 2)
+        for lo in (0, HALF // 2):
+            quantize_z(3, lo, lo + HALF // 2)
+        for part in (1, 2):
+            score(part, 2)
+            for j in range(2):
+                store(part, j, part == 2)

@@ -71,9 +71,6 @@ def tile_list_draft_tree_sketch_kernel(tc, tab_words, tab_scales, offs, w1_words
 
         nc.vector.memset(w1s_raw[:].bitcast(I32), 0)
         nc.vector.memset(ts_raw[:].bitcast(I32), 0)
-        warm = tile([P, 2], F32, "warm")
-        nc.vector.memset(warm[:], 0.0)
-        nc.scalar.activation(warm[:, 1:2], warm[:, 0:1], ACT.Sigmoid)
         nc.vector.memset(w1s[1][:].bitcast(I32), 0)
         nc.vector.memset(ts[1][:].bitcast(I32), 0)
 
@@ -154,6 +151,8 @@ def tile_list_draft_tree_sketch_kernel(tc, tab_words, tab_scales, offs, w1_words
         strength = consts[:, 8 * H_PASSES : 8 * H_PASSES + SLOTS]
         nc.sync.dma_start(strength, wgt)
         nc.sync.dma_start(gains, gain.rearrange("(b p t) -> p b t", p=P, t=PACK))
+        slope = tile([P, H_PASSES, PACK], F32, "slope")
+        level = tile([P, H_PASSES, PACK], F32, "level")
         for a in range(K_PASSES):
             for j in range(2):
                 gather_words(a, j)
@@ -172,9 +171,9 @@ def tile_list_draft_tree_sketch_kernel(tc, tab_words, tab_scales, offs, w1_words
         load_ws(0)
         load_ws(1)
 
-        def weave_ws(b, i):
-            cols = slice(WS_PIECE * i, WS_PIECE * (i + 1))
-            nc.scalar.copy(
+        def weave_ws(copy, b, lo, hi):
+            cols = slice(lo, hi)
+            copy(
                 ws_bf[b][:, cols, :].rearrange("p (c i) t -> p c t i", i=RUN),
                 ws_raw[b][:, :, cols].rearrange("p t (c i) -> p c t i", i=RUN),
             )
@@ -194,11 +193,11 @@ def tile_list_draft_tree_sketch_kernel(tc, tab_words, tab_scales, offs, w1_words
             nc.vector.tensor_tensor(x[u][:, t, :], h[PACK * b + t][:].indirect(picks[:, c // 16 : (c + w) // 16]), strength[:, c : c + w], ALU.mult)
 
         def gate(u, t):
-            nc.scalar.activation(f[u][:, t, :], x[u][:, t, :], ACT.Sigmoid)
+            nc.scalar.activation(f[u][:, t, :], x[u][:, t, :], ACT.Tanh, scale=0.5)
 
         def factor(u, t):
-            g = gains[:, units[u][0], t : t + 1]
-            nc.vector.tensor_scalar(f[u][:, t, :], f[u][:, t, :], g, g, ALU.mult, ALU.add)
+            b = units[u][0]
+            nc.vector.tensor_scalar(f[u][:, t, :], f[u][:, t, :], slope[:, b, t : t + 1], level[:, b, t : t + 1], ALU.mult, ALU.add)
 
         def weave_z(u, lo, hi):
             nc.vector.tensor_tensor(
@@ -251,20 +250,26 @@ def tile_list_draft_tree_sketch_kernel(tc, tab_words, tab_scales, offs, w1_words
             gate(u, t)
             if s == 1:
                 order_w1(2, w1_rest[:, :, PASS // 2 : PASS])
-            if 2 <= s < 11:
-                weave_ws(*divmod(s - 2, 3))
+            if s == 0:
+                nc.vector.tensor_scalar_mul(slope[:], gains, 0.5)
+                nc.vector.tensor_scalar_mul(level[:], gains, 1.5)
+            if s == 3:
+                weave_ws(nc.vector.tensor_copy, 0, 0, 512)
             if s == 4:
+                weave_ws(nc.vector.tensor_copy, 0, 512, N)
                 load_ws(2)
+            if s > 4 and s % 4 > 0 and s < 12:
+                weave_ws(nc.scalar.copy, s // 4, WS_PIECE * (s % 4 - 1), WS_PIECE * (s % 4))
             if s > 1:
                 factor(*steps[s - 2])
             if u > 0 and t == 2:
                 weave_z(u - 1, 0, units[u - 1][2])
             if u > 0 and t == 3:
                 quantize_z(u - 1, 0, units[u - 1][2])
-            if s in (5, 8, 11):
-                quantize_ws((s - 5) // 3, 0, 512)
-            if s in (6, 9, 12):
-                quantize_ws((s - 5) // 3, 512, N)
+            if s in (5, 8, 12):
+                quantize_ws((s - 4) // 4, 0, 512)
+            if s in (6, 9, 13):
+                quantize_ws((s - 5) // 4, 512, N)
             if s == 11:
                 for b in range(2):
                     for part in range(len(parts)):

@@ -21,21 +21,31 @@ PACK = 4
 PASS = P * PACK
 K_PASSES = K // PASS
 H_PASSES = H // PASS
+SLICES = H_PASSES * PACK
+LIST = 16
 BANK = 512
-HALF = SLOTS // 2
-RUN = 2
-WS_PIECE = 256
-SHIFT_ROWS = 112
+BANKS = 8
 H_BANKS = 4
+HALF = SLOTS // 2
+QUARTER = SLOTS // 4
+RUN = 2
+SCALE_ROWS = 4
+SHIFT_ROWS = 112
+PADDED = 8
+WS_PIECE = 256
+FIRST_WAVE = 2
+AHEAD = 3
+BEHIND = 2
+
 WS_BYTES = PACK * N * 4
-TAB_BYTES = T * 4
-AT_WS = (WS_BYTES + H, 0, WS_BYTES + H)
-AT_TAB = (WS_BYTES + H, WS_BYTES - TAB_BYTES)
+EDGE = 256
 AT_W1S = WS_BYTES
-AT_W1_FIRST = WS_BYTES - 256
-AT_W1S_RAW = 2 * WS_BYTES + H
+AT_TAB = (AT_W1S + H, AT_W1S - 4 * T)
+AT_W1_FIRST = (AT_TAB[0] + EDGE - 2 * PASS, AT_W1S - EDGE)
+AT_W1S_RAW = AT_TAB[0] + WS_BYTES
 AT_TS = AT_W1S_RAW
-AT_W1_REST = AT_W1S_RAW + H
+AT_WS = (AT_TAB[0], 0, AT_W1S_RAW + H)
+AT_W1_REST = AT_WS[2] + WS_BYTES - EDGE
 AT_CONSTS = AT_W1_REST + 4 * (H - PASS)
 AT_TS_RAW = AT_CONSTS - T // 2
 
@@ -44,7 +54,7 @@ def tile_list_draft_tree_sketch_kernel(tc, tab_words, tab_scales, offs, w1_words
     nc = tc.nc
     with ExitStack() as ctx:
         keep = ctx.enter_context(tc.tile_pool(name="keep", bufs=1))
-        ring = ctx.enter_context(tc.tile_pool(name="ring", bufs=12))
+        h_pool = ctx.enter_context(tc.tile_pool(name="h_pool", bufs=SLICES))
         stage = ctx.enter_context(tc.tile_pool(name="stage", bufs=1))
         psum = ctx.enter_context(tc.psum_pool(name="psum", bufs=1))
 
@@ -54,8 +64,8 @@ def tile_list_draft_tree_sketch_kernel(tc, tab_words, tab_scales, offs, w1_words
         def staged(shape, dtype, name, offset):
             return stage.tile(shape, dtype, name=name, align_bytes=64, offset=offset)
 
-        live = tile([P, S // 16], U16, "live")
-        picks = tile([P, SLOTS // 16], U16, "picks")
+        live = tile([P, S // LIST], U16, "live")
+        picks = tile([P, SLOTS // LIST], U16, "picks")
         w1s_raw = staged([P, H], U8, "w1s_raw", AT_W1S_RAW)
         ts_raw = staged([P, T], U8, "ts_raw", AT_TS_RAW)
         w1s = {1: tile([P, H], U8, "w1s1")}
@@ -77,21 +87,16 @@ def tile_list_draft_tree_sketch_kernel(tc, tab_words, tab_scales, offs, w1_words
         w1_i32 = w1_words.bitcast(I32).rearrange("a p c -> p a c")
 
         def load_scale_rows(dst, scales):
-            for q in range(4):
-                nc.sync.dma_start(dst[32 * q : 32 * q + 8, :].bitcast(I32), scales[:, 4 * q : 4 * q + 4, :].bitcast(I32))
+            for q in range(P // 32):
+                rows = scales[:, SCALE_ROWS * q : SCALE_ROWS * (q + 1), :]
+                nc.sync.dma_start(dst[32 * q : 32 * q + K_PASSES * SCALE_ROWS, :].bitcast(I32), rows.bitcast(I32))
+
+        def shift_rows(dst, src):
+            nc.scalar.dma_start(dst[0:SHIFT_ROWS, :].bitcast(I32), src[SCALE_ROWS : SCALE_ROWS + SHIFT_ROWS, :].bitcast(I32))
 
         def load_table(a):
             tab[a] = staged([P, T], I32, "tab%d" % a, AT_TAB[a])
             nc.sync.dma_start(tab[a][:], tab_words[a].rearrange("p t i -> p (t i)").bitcast(I32))
-
-        w1_first = staged([P, K_PASSES, PASS // 2], I32, "w1_first", AT_W1_FIRST)
-        nc.sync.dma_start(w1_first[:], w1_i32[:, :, 0 : PASS // 2])
-        nc.sync.dma_start(live[:], offs)
-        nc.sync.dma_start(picks[:], offs2)
-        bias = tile([P, H_PASSES, 8], F32, "bias")
-        nc.scalar.dma_start(bias[:, :, 0:PACK], b1.rearrange("(b p t) -> p b t", p=P, t=PACK))
-        load_scale_rows(w1s_raw, w1_scales)
-        load_scale_rows(ts_raw, tab_scales)
 
         def order_w1(b, src):
             nc.vector.tensor_copy(
@@ -99,11 +104,9 @@ def tile_list_draft_tree_sketch_kernel(tc, tab_words, tab_scales, offs, w1_words
                 src.bitcast(U16).rearrange("p a (m t) -> p a t m", t=PACK),
             )
 
-        def shift_rows(dst, src):
-            nc.sync.dma_start(dst[0:SHIFT_ROWS, :].bitcast(I32), src[4 : 4 + SHIFT_ROWS, :].bitcast(I32))
-
         def gather_words(a, j):
-            nc.vector.tensor_copy(v[a][j][:], tab[a][:].bitcast(U32).indirect(live[:, 32 * j : 32 * (j + 1)]))
+            columns = BANK // LIST
+            nc.vector.tensor_copy(v[a][j][:], tab[a][:].bitcast(U32).indirect(live[:, columns * j : columns * (j + 1)]))
 
         acc = {}
 
@@ -124,44 +127,64 @@ def tile_list_draft_tree_sketch_kernel(tc, tab_words, tab_scales, offs, w1_words
         def add_bias(r, j):
             b, t = divmod(r, PACK)
             if j == 0:
-                h[r] = ring.tile([P, S], F32, name="h", tag="h")
+                h[r] = h_pool.tile([P, S], F32, name="h", tag="h")
             nc.scalar.activation(h[r][:, BANK * j : BANK * (j + 1)], acc[r, j][:], ACT.Identity, bias=bias[:, b, t : t + 1])
 
-        def project(r, j):
-            for a in range(K_PASSES):
-                project_pass(r, j, a)
-            add_bias(r, j)
+        def project(r):
+            for j in range(2):
+                for a in range(K_PASSES):
+                    project_pass(r, j, a)
+                add_bias(r, j)
 
-        order_w1(0, w1_first[:])
-        load_table(0)
-        load_table(1)
+        w1_first = [staged([P, PASS // 2], I32, "w1_first%d" % a, AT_W1_FIRST[a]) for a in range(K_PASSES)]
+        for a in range(K_PASSES):
+            nc.sync.dma_start(w1_first[a][:], w1_i32[:, a, 0 : PASS // 2])
+        nc.sync.dma_start(live[:], offs)
+        nc.sync.dma_start(picks[:], offs2)
+        load_scale_rows(w1s_raw, w1_scales)
+        load_scale_rows(ts_raw, tab_scales)
+
+        for a in range(K_PASSES):
+            nc.vector.tensor_copy(
+                w1p[0][:, a, :].bitcast(U16).rearrange("p (t m) -> p t m", t=PACK),
+                w1_first[a][:].bitcast(U16).rearrange("p (m t) -> p t m", t=PACK),
+            )
+            load_table(a)
+
         w1s[0] = staged([P, H], U8, "w1s0", AT_W1S)
         nc.vector.tensor_copy(
-            w1s[0][:].rearrange("p (b t m) -> p b t m", t=PACK, m=P),
-            w1s_raw[:].rearrange("p (b m t) -> p b t m", t=PACK, m=P),
+            w1s[0][:].rearrange("p (b t m) -> p t b m", t=PACK, m=P),
+            w1s_raw[:].rearrange("p (b m t) -> p t b m", t=PACK, m=P),
         )
         shift_rows(w1s[1], w1s[0])
         ts[0] = staged([P, S], U8, "ts0", AT_TS)
         nc.vector.tensor_copy(ts[0][:], ts_raw[:].indirect(live[:]))
         shift_rows(ts[1], ts[0])
+
+        per_row_cols = 2 * H_PASSES * PADDED
+        consts = staged([P, per_row_cols + SLOTS], F32, "consts", AT_CONSTS)
+        per_row = consts[:, 0:per_row_cols].rearrange("p (v b t) -> p v b t", v=2, t=PADDED)
+        bias = per_row[:, 0, :, 0:PACK]
+        gains = per_row[:, 1, :, 0:PACK]
+        strength = consts[:, per_row_cols : per_row_cols + SLOTS]
+        nc.sync.dma_start(bias, b1.rearrange("(b p t) -> p b t", p=P, t=PACK))
         w1_rest = staged([P, K_PASSES, (H - PASS) // 2], I32, "w1_rest", AT_W1_REST)
         nc.sync.dma_start(w1_rest[:], w1_i32[:, :, PASS // 2 : H // 2])
-        consts = staged([P, 8 * H_PASSES + SLOTS], F32, "consts", AT_CONSTS)
-        gains = consts[:, 0 : 8 * H_PASSES].rearrange("p (b t) -> p b t", t=8)[:, :, 0:PACK]
-        strength = consts[:, 8 * H_PASSES : 8 * H_PASSES + SLOTS]
         nc.sync.dma_start(strength, wgt)
         nc.sync.dma_start(gains, gain.rearrange("(b p t) -> p b t", p=P, t=PACK))
         slope = tile([P, H_PASSES, PACK], F32, "slope")
         level = tile([P, H_PASSES, PACK], F32, "level")
+
         for a in range(K_PASSES):
             for j in range(2):
                 gather_words(a, j)
-                for r in range(2):
+                for r in range(FIRST_WAVE):
                     project_pass(r, j, a)
-        for r, j in [(0, 0), (1, 0), (0, 1), (1, 1)]:
-            add_bias(r, j)
-        project(2, 0)
-        project(2, 1)
+        for j in range(2):
+            for r in range(FIRST_WAVE):
+                add_bias(r, j)
+        for r in range(FIRST_WAVE, AHEAD):
+            project(r)
         order_w1(1, w1_rest[:, :, 0 : PASS // 2])
 
         def load_ws(b):
@@ -171,9 +194,9 @@ def tile_list_draft_tree_sketch_kernel(tc, tab_words, tab_scales, offs, w1_words
         load_ws(0)
         load_ws(1)
 
-        def weave_ws(copy, b, lo, hi):
-            cols = slice(lo, hi)
-            copy(
+        def weave_ws(b, i):
+            cols = slice(WS_PIECE * i, WS_PIECE * (i + 1))
+            nc.scalar.copy(
                 ws_bf[b][:, cols, :].rearrange("p (c i) t -> p c t i", i=RUN),
                 ws_raw[b][:, :, cols].rearrange("p t (c i) -> p c t i", i=RUN),
             )
@@ -190,7 +213,8 @@ def tile_list_draft_tree_sketch_kernel(tc, tab_words, tab_scales, offs, w1_words
 
         def pick(u, t):
             b, c, w = units[u]
-            nc.vector.tensor_tensor(x[u][:, t, :], h[PACK * b + t][:].indirect(picks[:, c // 16 : (c + w) // 16]), strength[:, c : c + w], ALU.mult)
+            looked_up = h[PACK * b + t][:].indirect(picks[:, c // LIST : (c + w) // LIST])
+            nc.vector.tensor_tensor(x[u][:, t, :], looked_up, strength[:, c : c + w], ALU.mult)
 
         def gate(u, t):
             nc.scalar.activation(f[u][:, t, :], x[u][:, t, :], ACT.Tanh, scale=0.5)
@@ -210,19 +234,19 @@ def tile_list_draft_tree_sketch_kernel(tc, tab_words, tab_scales, offs, w1_words
         def quantize_z(u, lo, hi):
             nc.vector.quantize_mx(z_q[u][:, lo:hi].bitcast(FP8X4), z_s[u][:, lo:hi], z[u][:, lo:hi, :].rearrange("p m t -> p (m t)"))
 
+        parts = [(0, HALF, 2), (HALF, QUARTER, 3), (HALF + QUARTER, QUARTER, 3)]
         scores = {}
-        parts = [(0, HALF, 2), (HALF, HALF // 2, 3), (HALF + HALF // 2, HALF // 2, 3)]
 
         def score(part, b):
             c, w, per_bank = parts[part]
-            u = b if b < 2 else 2 + c // HALF
+            u = b if b < H_PASSES - 1 else b + c // HALF
             lo = c - units[u][1]
             for n in range(N // P):
-                j, e = divmod(n, per_bank)
+                g, e = divmod(n, per_bank)
                 if b == 0 and e == 0:
-                    scores[part, j] = psum.tile([P, per_bank, w], F32, name="score", tag="bank%d" % ((H_BANKS + len(scores)) % 8))
+                    scores[part, g] = psum.tile([P, per_bank, w], F32, name="score", tag="bank%d" % ((H_BANKS + len(scores)) % BANKS))
                 nc.tensor.matmul_mx(
-                    scores[part, j][:, e, :],
+                    scores[part, g][:, e, :],
                     lhsT=ws_q[b][:, P * n : P * (n + 1)].bitcast(FP8X4),
                     lhsT_scale=ws_s[b][:, P * n : P * (n + 1)],
                     rhs=z_q[u][:, lo : lo + w].bitcast(FP8X4),
@@ -231,59 +255,56 @@ def tile_list_draft_tree_sketch_kernel(tc, tab_words, tab_scales, offs, w1_words
                     stop=(b == H_PASSES - 1 and e == per_bank - 1),
                 )
 
-        def store(part, j, on_vector):
+        def store(part, copy):
             c, w, per_bank = parts[part]
-            res = tile([P, per_bank, w], F32, "res%d_%d" % (part, j))
-            if on_vector:
-                nc.vector.tensor_copy(res[:], scores[part, j][:])
-            else:
-                nc.scalar.copy(res[:], scores[part, j][:])
             rows = per_bank * P
-            nc.sync.dma_start(out[rows * j : rows * (j + 1), c : c + w].rearrange("(e p) m -> p e m", p=P), res[:])
+            for g in range(N // rows):
+                res = tile([P, per_bank, w], F32, "res%d_%d" % (part, g))
+                copy(res[:], scores[part, g][:])
+                nc.sync.dma_start(out[rows * g : rows * (g + 1), c : c + w].rearrange("(e p) m -> p e m", p=P), res[:])
 
         steps = [(u, t) for u in range(len(units)) for t in range(PACK)]
+        last_projected = SLICES - 1 - AHEAD
+        pieces = N // WS_PIECE
+        weave_steps = list(range(AHEAD, last_projected, 2))
+        weave_steps.extend(range(last_projected, last_projected + H_PASSES * pieces - len(weave_steps)))
+        score_steps = [last_projected, 3 * PACK - 1]
         for s, (u, t) in enumerate(steps):
             pick(u, t)
-            if s + 3 < H_PASSES * PACK:
-                project(s + 3, 0)
-                project(s + 3, 1)
+            if s <= last_projected:
+                project(s + AHEAD)
             gate(u, t)
+            if s == 0:
+                nc.scalar.mul(slope[:], gains, 0.5)
+                nc.scalar.mul(level[:], gains, 1.5)
             if s == 1:
                 order_w1(2, w1_rest[:, :, PASS // 2 : PASS])
-            if s == 0:
-                nc.vector.tensor_scalar_mul(slope[:], gains, 0.5)
-                nc.vector.tensor_scalar_mul(level[:], gains, 1.5)
-            if s == 3:
-                weave_ws(nc.vector.tensor_copy, 0, 0, 512)
-            if s == 4:
-                weave_ws(nc.vector.tensor_copy, 0, 512, N)
                 load_ws(2)
-            if s > 4 and s % 4 > 0 and s < 12:
-                weave_ws(nc.scalar.copy, s // 4, WS_PIECE * (s % 4 - 1), WS_PIECE * (s % 4))
-            if s > 1:
-                factor(*steps[s - 2])
-            if u > 0 and t == 2:
+            if s in weave_steps:
+                weave_ws(*divmod(weave_steps.index(s), pieces))
+            if s >= BEHIND:
+                factor(*steps[s - BEHIND])
+            if u > 0 and t == BEHIND:
                 weave_z(u - 1, 0, units[u - 1][2])
-            if u > 0 and t == 3:
+            if u > 0 and t == BEHIND + 1:
                 quantize_z(u - 1, 0, units[u - 1][2])
-            if s in (5, 8, 12):
-                quantize_ws((s - 4) // 4, 0, 512)
-            if s in (6, 9, 13):
-                quantize_ws((s - 5) // 4, 512, N)
-            if s == 11:
-                for b in range(2):
-                    for part in range(len(parts)):
-                        score(part, b)
-        score(0, 2)
-        factor(*steps[-2])
-        factor(*steps[-1])
-        for j in range(3):
-            store(0, j, False)
-        for lo in (0, HALF // 2):
-            weave_z(3, lo, lo + HALF // 2)
-        for lo in (0, HALF // 2):
-            quantize_z(3, lo, lo + HALF // 2)
-        for part in (1, 2):
-            score(part, 2)
-            for j in range(2):
-                store(part, j, part == 2)
+            if s - 1 in weave_steps[1::pieces]:
+                quantize_ws(weave_steps.index(s - 1) // pieces, 0, 2 * WS_PIECE)
+            if s - 1 in weave_steps[2::pieces]:
+                quantize_ws(weave_steps.index(s - 1) // pieces, 2 * WS_PIECE, N)
+            if s in score_steps:
+                for part in range(len(parts)):
+                    score(part, score_steps.index(s))
+
+        last_pass, last_unit = H_PASSES - 1, len(units) - 1
+        score(0, last_pass)
+        for u, t in steps[-BEHIND:]:
+            factor(u, t)
+        store(0, nc.scalar.copy)
+        for lo in (0, QUARTER):
+            weave_z(last_unit, lo, lo + QUARTER)
+        for lo in (0, QUARTER):
+            quantize_z(last_unit, lo, lo + QUARTER)
+        for part, copy in ((1, nc.scalar.copy), (2, nc.vector.tensor_copy)):
+            score(part, last_pass)
+            store(part, copy)

@@ -29,32 +29,39 @@ H_BANKS = 4
 HALF = SLOTS // 2
 QUARTER = SLOTS // 4
 RUN = 2
+QUADRANT = 32
 SCALE_ROWS = 4
-SHIFT_ROWS = 112
+ROWS_AT = P - K_PASSES * 16
 PADDED = 8
 WS_PIECE = 256
 FIRST_WAVE = 2
 AHEAD = 3
-BEHIND = 2
+LARGEST = 3.0e38
 
 WS_BYTES = PACK * N * 4
-EDGE = 256
-AT_W1S = WS_BYTES
-AT_TAB = (AT_W1S + H, AT_W1S - 4 * T)
-AT_W1_FIRST = (AT_TAB[0] + EDGE - 2 * PASS, AT_W1S - EDGE)
-AT_W1S_RAW = AT_TAB[0] + WS_BYTES
-AT_TS = AT_W1S_RAW
-AT_WS = (AT_TAB[0], 0, AT_W1S_RAW + H)
-AT_W1_REST = AT_WS[2] + WS_BYTES - EDGE
-AT_CONSTS = AT_W1_REST + 4 * (H - PASS)
-AT_TS_RAW = AT_CONSTS - T // 2
+TAB_BYTES = 4 * T
+AT_WS = (0, WS_BYTES, 2 * WS_BYTES)
+AT_ROWS = AT_WS[0]
+AT_TS_RAW = AT_ROWS + S + H
+AT_W1S_RAW = AT_TS_RAW + T
+AT_TS_PICKED = AT_W1S_RAW + H
+W1P_BYTES = 2 * K_PASSES * PASS
+AT_TAB = (AT_WS[1], 3 * WS_BYTES - W1P_BYTES)
+AT_W1P = AT_TAB[1] + W1P_BYTES
+AT_INV = AT_W1P + 2 * W1P_BYTES
+AT_W1_FIRST = AT_TAB[1] + TAB_BYTES
+AT_W1_REST = AT_W1_FIRST
+AT_WEIGHTS = AT_W1_REST + 2 * K_PASSES * (H - PASS)
+AT_UNITS = AT_WEIGHTS + SLICES * SLOTS * 4
+UNIT_BYTES = PACK * SLOTS * 4
+AT_RES = AT_UNITS + 2 * UNIT_BYTES
+WOVEN_ON = 2
 
 
 def tile_list_draft_tree_sketch_kernel(tc, tab_words, tab_scales, offs, w1_words, w1_scales, b1, offs2, wgt, gain, ws, out):
     nc = tc.nc
     with ExitStack() as ctx:
         keep = ctx.enter_context(tc.tile_pool(name="keep", bufs=1))
-        h_pool = ctx.enter_context(tc.tile_pool(name="h_pool", bufs=SLICES))
         stage = ctx.enter_context(tc.tile_pool(name="stage", bufs=1))
         psum = ctx.enter_context(tc.psum_pool(name="psum", bufs=1))
 
@@ -66,43 +73,85 @@ def tile_list_draft_tree_sketch_kernel(tc, tab_words, tab_scales, offs, w1_words
 
         live = tile([P, S // LIST], U16, "live")
         picks = tile([P, SLOTS // LIST], U16, "picks")
-        w1s_raw = staged([P, H], U8, "w1s_raw", AT_W1S_RAW)
         ts_raw = staged([P, T], U8, "ts_raw", AT_TS_RAW)
-        w1s = {1: tile([P, H], U8, "w1s1")}
-        ts = {1: tile([P, S], U8, "ts1")}
-        w1p = [tile([P, K_PASSES, PASS * 2], U8, "w1p%d" % b) for b in range(H_PASSES)]
-        tab = {}
+        w1s_raw = staged([P, H], U8, "w1s_raw", AT_W1S_RAW)
+        ts_picked = staged([P, S], U8, "ts_picked", AT_TS_PICKED)
+        rows = staged([P, S + H], U8, "rows", AT_ROWS)
+        scales = tile([P, K_PASSES, S + H], U8, "scales")
+        w1p = {0: tile([P, K_PASSES, PASS * 2], U8, "w1p0")}
+        tab = [staged([P, T], I32, "tab%d" % a, AT_TAB[a]) for a in range(K_PASSES)]
         v = [[tile([P, BANK], U32, "v%d_%d" % (a, j)) for j in range(2)] for a in range(K_PASSES)]
         ws_raw = {}
-        ws_bf = [tile([P, N, PACK], BF16, "ws_bf%d" % b) for b in range(H_PASSES)]
+        ws_bf = {}
         ws_q = [tile([P, N], U32, "ws_q%d" % b) for b in range(H_PASSES)]
         ws_s = [tile([P, N], U8, "ws_s%d" % b) for b in range(H_PASSES)]
-        h = {}
+        h = [tile([P, S], F32, "h%d" % r) for r in range(SLICES)]
+        gains_pad = tile([P, H_PASSES, PADDED], F32, "gains")
+        bias_pad = tile([P, H_PASSES, PADDED], F32, "bias")
+        gains = gains_pad[:, :, 0:PACK]
+        bias = bias_pad[:, :, 0:PACK]
+        strength = tile([P, SLOTS], F32, "strength")
+        half_gain = tile([P, H_PASSES, PACK], F32, "half_gain")
+        inv_capped = tile([P, H_PASSES, PACK], F32, "inv_capped")
+        inv_gain = tile([P, H_PASSES, PACK], F32, "inv_gain")
+        weights = [staged([P, SLOTS], F32, "weights%d" % r, AT_WEIGHTS + 4 * SLOTS * r) for r in range(SLICES)]
 
-        nc.vector.memset(w1s_raw[:].bitcast(I32), 0)
-        nc.vector.memset(ts_raw[:].bitcast(I32), 0)
-        nc.vector.memset(w1s[1][:].bitcast(I32), 0)
-        nc.vector.memset(ts[1][:].bitcast(I32), 0)
+        nc.vector.memset(ts_raw[0:ROWS_AT, :].bitcast(I32), 0)
+        nc.vector.memset(w1s_raw[0:ROWS_AT, :].bitcast(I32), 0)
+        nc.vector.memset(scales[:].rearrange("p a c -> p (a c)").bitcast(I32), 0)
 
         w1_i32 = w1_words.bitcast(I32).rearrange("a p c -> p a c")
 
-        def load_scale_rows(dst, scales):
-            for q in range(P // 32):
-                rows = scales[:, SCALE_ROWS * q : SCALE_ROWS * (q + 1), :]
-                nc.sync.dma_start(dst[32 * q : 32 * q + K_PASSES * SCALE_ROWS, :].bitcast(I32), rows.bitcast(I32))
+        def load_scale_rows(dst, src):
+            nc.sync.dma_start(dst[ROWS_AT:P, :].bitcast(I32), src.bitcast(I32).rearrange("a j c -> j a c"))
 
-        def shift_rows(dst, src):
-            nc.scalar.dma_start(dst[0:SHIFT_ROWS, :].bitcast(I32), src[SCALE_ROWS : SCALE_ROWS + SHIFT_ROWS, :].bitcast(I32))
-
-        def load_table(a):
-            tab[a] = staged([P, T], I32, "tab%d" % a, AT_TAB[a])
+        w1_first = staged([P, K_PASSES, PASS // 2], I32, "w1_first", AT_W1_FIRST)
+        nc.sync.dma_start(live[:], offs)
+        load_scale_rows(ts_raw, tab_scales)
+        load_scale_rows(w1s_raw, w1_scales)
+        nc.sync.dma_start(gains, gain.rearrange("(b p t) -> p b t", p=P, t=PACK))
+        nc.sync.dma_start(strength[:], wgt)
+        nc.sync.dma_start(w1_first[:], w1_i32[:, :, 0 : PASS // 2])
+        for a in range(K_PASSES):
             nc.sync.dma_start(tab[a][:], tab_words[a].rearrange("p t i -> p (t i)").bitcast(I32))
+        nc.sync.dma_start(picks[:], offs2)
+        nc.sync.dma_start(bias, b1.rearrange("(b p t) -> p b t", p=P, t=PACK))
+
+        nc.vector.tensor_copy(ts_picked[:], ts_raw[:].indirect(live[:]))
+        nc.vector.tensor_copy(
+            rows[:, S : S + H].rearrange("p (b t m) -> p t b m", t=PACK, m=P),
+            w1s_raw[:].rearrange("p (b m t) -> p t b m", t=PACK, m=P),
+        )
+        nc.vector.tensor_copy(rows[ROWS_AT:P, 0:S].bitcast(I32), ts_picked[ROWS_AT:P, :].bitcast(I32))
+        per_quadrant = K_PASSES * SCALE_ROWS
+        for q in range(P // QUADRANT):
+            nc.sync.dma_start(
+                scales[QUADRANT * q : QUADRANT * q + SCALE_ROWS, :, :].rearrange("p a c -> p (a c)").bitcast(I32),
+                rows[ROWS_AT + per_quadrant * q : ROWS_AT + per_quadrant * (q + 1), :].bitcast(I32),
+            )
 
         def order_w1(b, src):
+            if b > 0:
+                w1p[b] = staged([P, K_PASSES, PASS * 2], U8, "w1p%d" % b, AT_W1P + W1P_BYTES * (b - 1))
             nc.vector.tensor_copy(
                 w1p[b][:].bitcast(U16).rearrange("p a (t m) -> p a t m", t=PACK),
                 src.bitcast(U16).rearrange("p a (m t) -> p a t m", t=PACK),
             )
+
+        order_w1(0, w1_first[:])
+        w1_rest = staged([P, K_PASSES, (H - PASS) // 2], I32, "w1_rest", AT_W1_REST)
+        nc.sync.dma_start(w1_rest[:], w1_i32[:, :, PASS // 2 : H // 2])
+
+        nc.scalar.mul(half_gain[:], gains, 0.5)
+        for r in range(SLICES):
+            b, t = divmod(r, PACK)
+            nc.scalar.activation(weights[r][:], strength[:], ACT.Identity, scale=half_gain[:, b, t : t + 1])
+
+        def load_ws(b):
+            ws_raw[b] = staged([P, PACK, N], F32, "ws_raw%d" % b, AT_WS[b])
+            nc.sync.dma_start(ws_raw[b][:], ws[PASS * b : PASS * (b + 1), :].rearrange("(p t) n -> p t n", t=PACK))
+
+        load_ws(0)
 
         def gather_words(a, j):
             columns = BANK // LIST
@@ -117,17 +166,15 @@ def tile_list_draft_tree_sketch_kernel(tc, tab_words, tab_scales, offs, w1_words
             nc.tensor.matmul_mx(
                 acc[r, j][:],
                 lhsT=w1p[b][:, a, 2 * P * t : 2 * P * (t + 1)].bitcast(FP4X4),
-                lhsT_scale=w1s[a][:, P * r : P * (r + 1)],
+                lhsT_scale=scales[:, a, S + P * r : S + P * (r + 1)],
                 rhs=v[a][j][:].bitcast(FP8X4),
-                rhs_scale=ts[a][:, BANK * j : BANK * (j + 1)],
+                rhs_scale=scales[:, a, BANK * j : BANK * (j + 1)],
                 start=(a == 0),
                 stop=(a == K_PASSES - 1),
             )
 
         def add_bias(r, j):
             b, t = divmod(r, PACK)
-            if j == 0:
-                h[r] = h_pool.tile([P, S], F32, name="h", tag="h")
             nc.scalar.activation(h[r][:, BANK * j : BANK * (j + 1)], acc[r, j][:], ACT.Identity, bias=bias[:, b, t : t + 1])
 
         def project(r):
@@ -135,45 +182,6 @@ def tile_list_draft_tree_sketch_kernel(tc, tab_words, tab_scales, offs, w1_words
                 for a in range(K_PASSES):
                     project_pass(r, j, a)
                 add_bias(r, j)
-
-        w1_first = [staged([P, PASS // 2], I32, "w1_first%d" % a, AT_W1_FIRST[a]) for a in range(K_PASSES)]
-        for a in range(K_PASSES):
-            nc.sync.dma_start(w1_first[a][:], w1_i32[:, a, 0 : PASS // 2])
-        nc.sync.dma_start(live[:], offs)
-        nc.sync.dma_start(picks[:], offs2)
-        load_scale_rows(w1s_raw, w1_scales)
-        load_scale_rows(ts_raw, tab_scales)
-
-        for a in range(K_PASSES):
-            nc.vector.tensor_copy(
-                w1p[0][:, a, :].bitcast(U16).rearrange("p (t m) -> p t m", t=PACK),
-                w1_first[a][:].bitcast(U16).rearrange("p (m t) -> p t m", t=PACK),
-            )
-            load_table(a)
-
-        w1s[0] = staged([P, H], U8, "w1s0", AT_W1S)
-        nc.vector.tensor_copy(
-            w1s[0][:].rearrange("p (b t m) -> p t b m", t=PACK, m=P),
-            w1s_raw[:].rearrange("p (b m t) -> p t b m", t=PACK, m=P),
-        )
-        shift_rows(w1s[1], w1s[0])
-        ts[0] = staged([P, S], U8, "ts0", AT_TS)
-        nc.vector.tensor_copy(ts[0][:], ts_raw[:].indirect(live[:]))
-        shift_rows(ts[1], ts[0])
-
-        per_row_cols = 2 * H_PASSES * PADDED
-        consts = staged([P, per_row_cols + SLOTS], F32, "consts", AT_CONSTS)
-        per_row = consts[:, 0:per_row_cols].rearrange("p (v b t) -> p v b t", v=2, t=PADDED)
-        bias = per_row[:, 0, :, 0:PACK]
-        gains = per_row[:, 1, :, 0:PACK]
-        strength = consts[:, per_row_cols : per_row_cols + SLOTS]
-        nc.sync.dma_start(bias, b1.rearrange("(b p t) -> p b t", p=P, t=PACK))
-        w1_rest = staged([P, K_PASSES, (H - PASS) // 2], I32, "w1_rest", AT_W1_REST)
-        nc.sync.dma_start(w1_rest[:], w1_i32[:, :, PASS // 2 : H // 2])
-        nc.sync.dma_start(strength, wgt)
-        nc.sync.dma_start(gains, gain.rearrange("(b p t) -> p b t", p=P, t=PACK))
-        slope = tile([P, H_PASSES, PACK], F32, "slope")
-        level = tile([P, H_PASSES, PACK], F32, "level")
 
         for a in range(K_PASSES):
             for j in range(2):
@@ -183,51 +191,59 @@ def tile_list_draft_tree_sketch_kernel(tc, tab_words, tab_scales, offs, w1_words
         for j in range(2):
             for r in range(FIRST_WAVE):
                 add_bias(r, j)
+        load_ws(1)
+        order_w1(1, w1_rest[:, :, 0 : PASS // 2])
+        order_w1(2, w1_rest[:, :, PASS // 2 : PASS])
+        load_ws(2)
+        inv_half = staged([P, H_PASSES, PACK], F32, "inv_half", AT_INV)
+        nc.vector.reciprocal(inv_half[:], half_gain[:])
+        nc.vector.tensor_scalar(inv_capped[:], inv_half[:], 0.5, LARGEST, ALU.mult, ALU.min)
+        nc.vector.tensor_scalar_max(inv_gain[:], inv_capped[:], -LARGEST)
         for r in range(FIRST_WAVE, AHEAD):
             project(r)
-        order_w1(1, w1_rest[:, :, 0 : PASS // 2])
 
-        def load_ws(b):
-            ws_raw[b] = staged([P, PACK, N], F32, "ws_raw%d" % b, AT_WS[b])
-            nc.sync.dma_start(ws_raw[b][:], ws[PASS * b : PASS * (b + 1), :].rearrange("(p t) n -> p t n", t=PACK))
-
-        load_ws(0)
-        load_ws(1)
-
-        def weave_ws(b, i):
+        def weave_ws(b, i, copy):
             cols = slice(WS_PIECE * i, WS_PIECE * (i + 1))
-            nc.scalar.copy(
-                ws_bf[b][:, cols, :].rearrange("p (c i) t -> p c t i", i=RUN),
+            if b == 0:
+                ws_bf[b, i] = staged([P, WS_PIECE, PACK], BF16, "ws_bf0_%d" % i, AT_WEIGHTS + 4 * SLOTS * (WOVEN_ON + i))
+            else:
+                ws_bf[b, i] = tile([P, WS_PIECE, PACK], BF16, "ws_bf%d_%d" % (b, i))
+            copy(
+                ws_bf[b, i][:].rearrange("p (c i) t -> p c t i", i=RUN),
                 ws_raw[b][:, :, cols].rearrange("p t (c i) -> p c t i", i=RUN),
             )
 
-        def quantize_ws(b, lo, hi):
-            nc.vector.quantize_mx(ws_q[b][:, lo:hi].bitcast(FP8X4), ws_s[b][:, lo:hi], ws_bf[b][:, lo:hi, :].rearrange("p n t -> p (n t)"))
+        def quantize_ws(b, i):
+            cols = slice(WS_PIECE * i, WS_PIECE * (i + 1))
+            nc.vector.quantize_mx(ws_q[b][:, cols].bitcast(FP8X4), ws_s[b][:, cols], ws_bf[b, i][:].rearrange("p n t -> p (n t)"))
 
         units = [(0, 0, SLOTS), (1, 0, SLOTS), (2, 0, HALF), (2, HALF, HALF)]
-        x = [tile([P, PACK, w], F32, "x%d" % u) for u, (b, c, w) in enumerate(units)]
-        f = [tile([P, PACK, w], F32, "f%d" % u) for u, (b, c, w) in enumerate(units)]
+        unit_at = [0, 2 * UNIT_BYTES, 0, UNIT_BYTES]
+        ux = {}
+        th = {}
         z = [tile([P, w, PACK], BF16, "z%d" % u) for u, (b, c, w) in enumerate(units)]
         z_q = [tile([P, w], U32, "z_q%d" % u) for u, (b, c, w) in enumerate(units)]
         z_s = [tile([P, w], U8, "z_s%d" % u) for u, (b, c, w) in enumerate(units)]
 
         def pick(u, t):
             b, c, w = units[u]
+            if t == 0:
+                ux[u] = staged([P, PACK, w], F32, "ux%d" % u, AT_UNITS + unit_at[u])
+                th[u] = staged([P, PACK, w], F32, "th%d" % u, AT_UNITS + unit_at[u] + PACK * w * 4)
             looked_up = h[PACK * b + t][:].indirect(picks[:, c // LIST : (c + w) // LIST])
-            nc.vector.tensor_tensor(x[u][:, t, :], looked_up, strength[:, c : c + w], ALU.mult)
+            nc.vector.tensor_tensor(ux[u][:, t, :], looked_up, weights[PACK * b + t][:, c : c + w], ALU.mult)
 
         def gate(u, t):
-            nc.scalar.activation(f[u][:, t, :], x[u][:, t, :], ACT.Tanh, scale=0.5)
-
-        def factor(u, t):
             b = units[u][0]
-            nc.vector.tensor_scalar(f[u][:, t, :], f[u][:, t, :], slope[:, b, t : t + 1], level[:, b, t : t + 1], ALU.mult, ALU.add)
+            nc.scalar.activation(th[u][:, t, :], ux[u][:, t, :], ACT.Tanh, scale=inv_gain[:, b, t : t + 1])
 
         def weave_z(u, lo, hi):
-            nc.vector.tensor_tensor(
-                z[u][:, lo:hi, :].rearrange("p (c i) t -> p c t i", i=RUN),
-                x[u][:, :, lo:hi].rearrange("p t (c i) -> p c t i", i=RUN),
-                f[u][:, :, lo:hi].rearrange("p t (c i) -> p c t i", i=RUN),
+            nc.vector.scalar_tensor_tensor(
+                z[u][:, lo:hi, :],
+                th[u][:, :, lo:hi].rearrange("p t m -> p m t"),
+                3.0,
+                ux[u][:, :, lo:hi].rearrange("p t m -> p m t"),
+                ALU.add,
                 ALU.mult,
             )
 
@@ -257,49 +273,46 @@ def tile_list_draft_tree_sketch_kernel(tc, tab_words, tab_scales, offs, w1_words
 
         def store(part, copy):
             c, w, per_bank = parts[part]
-            rows = per_bank * P
-            for g in range(N // rows):
-                res = tile([P, per_bank, w], F32, "res%d_%d" % (part, g))
+            out_rows = per_bank * P
+            for g in range(N // out_rows):
+                at = AT_RES + 4 * (c * (N // P) + g * per_bank * w)
+                res = staged([P, per_bank, w], F32, "res%d_%d" % (part, g), at)
                 copy(res[:], scores[part, g][:])
-                nc.sync.dma_start(out[rows * g : rows * (g + 1), c : c + w].rearrange("(e p) m -> p e m", p=P), res[:])
+                nc.sync.dma_start(out[out_rows * g : out_rows * (g + 1), c : c + w].rearrange("(e p) m -> p e m", p=P), res[:])
 
         steps = [(u, t) for u in range(len(units)) for t in range(PACK)]
         last_projected = SLICES - 1 - AHEAD
         pieces = N // WS_PIECE
-        weave_steps = list(range(AHEAD, last_projected, 2))
-        weave_steps.extend(range(last_projected, last_projected + H_PASSES * pieces - len(weave_steps)))
+        vector_steps = list(range(WOVEN_ON, WOVEN_ON + pieces))
+        scalar_steps = [5, 7, 9, 10, 11, 12]
         score_steps = [last_projected, 3 * PACK - 1]
         for s, (u, t) in enumerate(steps):
             pick(u, t)
             if s <= last_projected:
                 project(s + AHEAD)
-            gate(u, t)
-            if s == 0:
-                nc.scalar.mul(slope[:], gains, 0.5)
-                nc.scalar.mul(level[:], gains, 1.5)
-            if s == 1:
-                order_w1(2, w1_rest[:, :, PASS // 2 : PASS])
-                load_ws(2)
-            if s in weave_steps:
-                weave_ws(*divmod(weave_steps.index(s), pieces))
-            if s >= BEHIND:
-                factor(*steps[s - BEHIND])
-            if u > 0 and t == BEHIND:
+            if s > 0:
+                gate(*steps[s - 1])
+            if s in vector_steps:
+                weave_ws(0, vector_steps.index(s), nc.vector.tensor_copy)
+            if s in scalar_steps:
+                b, i = divmod(scalar_steps.index(s), pieces)
+                weave_ws(b + 1, i, nc.scalar.copy)
+            if u > 0 and t == 1:
                 weave_z(u - 1, 0, units[u - 1][2])
-            if u > 0 and t == BEHIND + 1:
+            if u > 0 and t == 2:
                 quantize_z(u - 1, 0, units[u - 1][2])
-            if s - 1 in weave_steps[1::pieces]:
-                quantize_ws(weave_steps.index(s - 1) // pieces, 0, 2 * WS_PIECE)
-            if s - 1 in weave_steps[2::pieces]:
-                quantize_ws(weave_steps.index(s - 1) // pieces, 2 * WS_PIECE, N)
+            if s - 1 in vector_steps:
+                quantize_ws(0, vector_steps.index(s - 1))
+            if s - 1 in scalar_steps:
+                b, i = divmod(scalar_steps.index(s - 1), pieces)
+                quantize_ws(b + 1, i)
             if s in score_steps:
                 for part in range(len(parts)):
                     score(part, score_steps.index(s))
 
         last_pass, last_unit = H_PASSES - 1, len(units) - 1
+        gate(*steps[-1])
         score(0, last_pass)
-        for u, t in steps[-BEHIND:]:
-            factor(u, t)
         store(0, nc.scalar.copy)
         for lo in (0, QUARTER):
             weave_z(last_unit, lo, lo + QUARTER)

@@ -42,18 +42,19 @@ WS_BYTES = PACK * N * 4
 TAB_BYTES = 4 * T
 AT_WS = (0, WS_BYTES, 2 * WS_BYTES)
 AT_ROWS = AT_WS[0]
-AT_TS_RAW = AT_ROWS + S + H
-AT_W1S_RAW = AT_TS_RAW + T
-AT_TS_PICKED = AT_W1S_RAW + H
+AT_TS_RAW = AT_ROWS + S + PASS
+AT_TS_PICKED = AT_TS_RAW + T
 W1P_BYTES = 2 * K_PASSES * PASS
 AT_TAB = (AT_WS[1], 3 * WS_BYTES - W1P_BYTES)
 AT_W1P = AT_TAB[1] + W1P_BYTES
-AT_INV = AT_W1P + 2 * W1P_BYTES
+AT_ROWS_REST = AT_W1P + 2 * W1P_BYTES
+AT_INV = AT_ROWS_REST + H - PASS
 AT_W1_FIRST = AT_TAB[1] + TAB_BYTES
 AT_W1_REST = AT_W1_FIRST
 AT_WEIGHTS = AT_W1_REST + 2 * K_PASSES * (H - PASS)
 AT_UNITS = AT_WEIGHTS + SLICES * SLOTS * 4
-UNIT_BYTES = PACK * SLOTS * 4
+STAGGER = 1
+UNIT_BYTES = PACK * SLOTS * 4 + 128
 AT_RES = AT_UNITS + 2 * UNIT_BYTES
 WOVEN_ON = 2
 
@@ -74,10 +75,11 @@ def tile_list_draft_tree_sketch_kernel(tc, tab_words, tab_scales, offs, w1_words
         live = tile([P, S // LIST], U16, "live")
         picks = tile([P, SLOTS // LIST], U16, "picks")
         ts_raw = staged([P, T], U8, "ts_raw", AT_TS_RAW)
-        w1s_raw = staged([P, H], U8, "w1s_raw", AT_W1S_RAW)
+        w1s_raw = tile([P, H], U8, "w1s_raw")
         ts_picked = staged([P, S], U8, "ts_picked", AT_TS_PICKED)
-        rows = staged([P, S + H], U8, "rows", AT_ROWS)
-        scales = tile([P, K_PASSES, S + H], U8, "scales")
+        rows = staged([P, S + PASS], U8, "rows", AT_ROWS)
+        scales = tile([P, K_PASSES, S + PASS], U8, "scales")
+        scales_rest = tile([P, K_PASSES, H - PASS], U8, "scales_rest")
         w1p = {0: tile([P, K_PASSES, PASS * 2], U8, "w1p0")}
         tab = [staged([P, T], I32, "tab%d" % a, AT_TAB[a]) for a in range(K_PASSES)]
         v = [[tile([P, BANK], U32, "v%d_%d" % (a, j)) for j in range(2)] for a in range(K_PASSES)]
@@ -99,6 +101,7 @@ def tile_list_draft_tree_sketch_kernel(tc, tab_words, tab_scales, offs, w1_words
         nc.vector.memset(ts_raw[0:ROWS_AT, :].bitcast(I32), 0)
         nc.vector.memset(w1s_raw[0:ROWS_AT, :].bitcast(I32), 0)
         nc.vector.memset(scales[:].rearrange("p a c -> p (a c)").bitcast(I32), 0)
+        nc.vector.memset(scales_rest[:].rearrange("p a c -> p (a c)").bitcast(I32), 0)
 
         w1_i32 = w1_words.bitcast(I32).rearrange("a p c -> p a c")
 
@@ -118,17 +121,21 @@ def tile_list_draft_tree_sketch_kernel(tc, tab_words, tab_scales, offs, w1_words
         nc.sync.dma_start(bias, b1.rearrange("(b p t) -> p b t", p=P, t=PACK))
 
         nc.vector.tensor_copy(ts_picked[:], ts_raw[:].indirect(live[:]))
-        nc.vector.tensor_copy(
-            rows[:, S : S + H].rearrange("p (b t m) -> p t b m", t=PACK, m=P),
-            w1s_raw[:].rearrange("p (b m t) -> p t b m", t=PACK, m=P),
-        )
+
+        def order_scales(dst, src):
+            nc.vector.tensor_copy(dst.rearrange("p (b t m) -> p t b m", t=PACK, m=P), src.rearrange("p (b m t) -> p t b m", t=PACK, m=P))
+
+        def deal_rows(dst, src):
+            per_quadrant = K_PASSES * SCALE_ROWS
+            for q in range(P // QUADRANT):
+                nc.sync.dma_start(
+                    dst[QUADRANT * q : QUADRANT * q + SCALE_ROWS, :, :].rearrange("p a c -> p (a c)").bitcast(I32),
+                    src[ROWS_AT + per_quadrant * q : ROWS_AT + per_quadrant * (q + 1), :].bitcast(I32),
+                )
+
+        order_scales(rows[:, S : S + PASS], w1s_raw[:, 0:PASS])
         nc.vector.tensor_copy(rows[ROWS_AT:P, 0:S].bitcast(I32), ts_picked[ROWS_AT:P, :].bitcast(I32))
-        per_quadrant = K_PASSES * SCALE_ROWS
-        for q in range(P // QUADRANT):
-            nc.sync.dma_start(
-                scales[QUADRANT * q : QUADRANT * q + SCALE_ROWS, :, :].rearrange("p a c -> p (a c)").bitcast(I32),
-                rows[ROWS_AT + per_quadrant * q : ROWS_AT + per_quadrant * (q + 1), :].bitcast(I32),
-            )
+        deal_rows(scales, rows)
 
         def order_w1(b, src):
             if b > 0:
@@ -166,7 +173,7 @@ def tile_list_draft_tree_sketch_kernel(tc, tab_words, tab_scales, offs, w1_words
             nc.tensor.matmul_mx(
                 acc[r, j][:],
                 lhsT=w1p[b][:, a, 2 * P * t : 2 * P * (t + 1)].bitcast(FP4X4),
-                lhsT_scale=scales[:, a, S + P * r : S + P * (r + 1)],
+                lhsT_scale=scales[:, a, S + P * r : S + P * (r + 1)] if b == 0 else scales_rest[:, a, P * (r - PACK) : P * (r - PACK + 1)],
                 rhs=v[a][j][:].bitcast(FP8X4),
                 rhs_scale=scales[:, a, BANK * j : BANK * (j + 1)],
                 start=(a == 0),
@@ -186,12 +193,22 @@ def tile_list_draft_tree_sketch_kernel(tc, tab_words, tab_scales, offs, w1_words
         for a in range(K_PASSES):
             for j in range(2):
                 gather_words(a, j)
-                for r in range(FIRST_WAVE):
-                    project_pass(r, j, a)
         for j in range(2):
-            for r in range(FIRST_WAVE):
-                add_bias(r, j)
+            project_pass(0, j, 0)
+        project_pass(0, 0, 1)
+        add_bias(0, 0)
+        project_pass(1, 0, 0)
+        project_pass(0, 1, 1)
+        add_bias(0, 1)
+        project_pass(1, 0, 1)
+        add_bias(1, 0)
+        for a in range(K_PASSES):
+            project_pass(1, 1, a)
+        add_bias(1, 1)
         load_ws(1)
+        rows_rest = staged([P, H - PASS], U8, "rows_rest", AT_ROWS_REST)
+        order_scales(rows_rest[:], w1s_raw[:, PASS:H])
+        deal_rows(scales_rest, rows_rest)
         order_w1(1, w1_rest[:, :, 0 : PASS // 2])
         order_w1(2, w1_rest[:, :, PASS // 2 : PASS])
         load_ws(2)
@@ -228,14 +245,14 @@ def tile_list_draft_tree_sketch_kernel(tc, tab_words, tab_scales, offs, w1_words
         def pick(u, t):
             b, c, w = units[u]
             if t == 0:
-                ux[u] = staged([P, PACK, w], F32, "ux%d" % u, AT_UNITS + unit_at[u])
-                th[u] = staged([P, PACK, w], F32, "th%d" % u, AT_UNITS + unit_at[u] + PACK * w * 4)
+                ux[u] = staged([P, PACK, w + STAGGER], F32, "ux%d" % u, AT_UNITS + unit_at[u])
+                th[u] = staged([P, PACK, w + STAGGER], F32, "th%d" % u, AT_UNITS + unit_at[u] + PACK * w * 4 + 64)
             looked_up = h[PACK * b + t][:].indirect(picks[:, c // LIST : (c + w) // LIST])
-            nc.vector.tensor_tensor(ux[u][:, t, :], looked_up, weights[PACK * b + t][:, c : c + w], ALU.mult)
+            nc.vector.tensor_tensor(ux[u][:, t, 0:w], looked_up, weights[PACK * b + t][:, c : c + w], ALU.mult)
 
         def gate(u, t):
-            b = units[u][0]
-            nc.scalar.activation(th[u][:, t, :], ux[u][:, t, :], ACT.Tanh, scale=inv_gain[:, b, t : t + 1])
+            b, c, w = units[u]
+            nc.scalar.activation(th[u][:, t, 0:w], ux[u][:, t, 0:w], ACT.Tanh, scale=inv_gain[:, b, t : t + 1])
 
         def weave_z(u, lo, hi):
             nc.vector.scalar_tensor_tensor(
@@ -283,8 +300,7 @@ def tile_list_draft_tree_sketch_kernel(tc, tab_words, tab_scales, offs, w1_words
         steps = [(u, t) for u in range(len(units)) for t in range(PACK)]
         last_projected = SLICES - 1 - AHEAD
         pieces = N // WS_PIECE
-        vector_steps = list(range(WOVEN_ON, WOVEN_ON + pieces))
-        scalar_steps = [5, 7, 9, 10, 11, 12]
+        weave_steps = [WOVEN_ON, WOVEN_ON + 1, WOVEN_ON + 2, 5, 7, 9, 10, 11, 12]
         score_steps = [last_projected, 3 * PACK - 1]
         for s, (u, t) in enumerate(steps):
             pick(u, t)
@@ -292,20 +308,15 @@ def tile_list_draft_tree_sketch_kernel(tc, tab_words, tab_scales, offs, w1_words
                 project(s + AHEAD)
             if s > 0:
                 gate(*steps[s - 1])
-            if s in vector_steps:
-                weave_ws(0, vector_steps.index(s), nc.vector.tensor_copy)
-            if s in scalar_steps:
-                b, i = divmod(scalar_steps.index(s), pieces)
-                weave_ws(b + 1, i, nc.scalar.copy)
+            if s in weave_steps:
+                b, i = divmod(weave_steps.index(s), pieces)
+                weave_ws(b, i, nc.vector.tensor_copy if b == 0 else nc.scalar.copy)
             if u > 0 and t == 1:
                 weave_z(u - 1, 0, units[u - 1][2])
             if u > 0 and t == 2:
                 quantize_z(u - 1, 0, units[u - 1][2])
-            if s - 1 in vector_steps:
-                quantize_ws(0, vector_steps.index(s - 1))
-            if s - 1 in scalar_steps:
-                b, i = divmod(scalar_steps.index(s - 1), pieces)
-                quantize_ws(b + 1, i)
+            if s - 1 in weave_steps:
+                quantize_ws(*divmod(weave_steps.index(s - 1), pieces))
             if s in score_steps:
                 for part in range(len(parts)):
                     score(part, score_steps.index(s))

@@ -27,36 +27,37 @@ BANK = 512
 BANKS = 8
 H_BANKS = 4
 HALF = SLOTS // 2
-QUARTER = SLOTS // 4
+LATE = SLOTS // 4
+EARLY = SLOTS - LATE
 RUN = 2
 QUADRANT = 32
 SCALE_ROWS = 4
 ROWS_AT = P - K_PASSES * 16
 PADDED = 8
-WS_PIECE = 256
-FIRST_WAVE = 2
+WS_PIECE = 384
 AHEAD = 3
 LARGEST = 3.0e38
 
 WS_BYTES = PACK * N * 4
 TAB_BYTES = 4 * T
+W1P_BYTES = 2 * K_PASSES * PASS
 AT_WS = (0, WS_BYTES, 2 * WS_BYTES)
 AT_ROWS = AT_WS[0]
+AT_HALF_FIRST = AT_ROWS
 AT_TS_RAW = AT_ROWS + S + PASS
 AT_TS_PICKED = AT_TS_RAW + T
-W1P_BYTES = 2 * K_PASSES * PASS
-AT_TAB = (AT_WS[1], 3 * WS_BYTES - W1P_BYTES)
-AT_W1P = AT_TAB[1] + W1P_BYTES
+AT_W1_FIRST = AT_WS[2] - W1P_BYTES
+AT_W1_REST = AT_W1_FIRST
+AT_TAB = (3 * WS_BYTES, 3 * WS_BYTES + TAB_BYTES)
+AT_W1P = AT_TAB[1]
 AT_ROWS_REST = AT_W1P + 2 * W1P_BYTES
 AT_INV = AT_ROWS_REST + H - PASS
-AT_W1_FIRST = AT_TAB[1] + TAB_BYTES
-AT_W1_REST = AT_W1_FIRST
-AT_WEIGHTS = AT_W1_REST + 2 * K_PASSES * (H - PASS)
+AT_WEIGHTS = AT_TAB[1] + TAB_BYTES
 AT_UNITS = AT_WEIGHTS + SLICES * SLOTS * 4
 STAGGER = 1
 UNIT_BYTES = PACK * SLOTS * 4 + 128
 AT_RES = AT_UNITS + 2 * UNIT_BYTES
-WOVEN_ON = 2
+WOVEN_ON = 1
 
 
 def tile_list_draft_tree_sketch_kernel(tc, tab_words, tab_scales, offs, w1_words, w1_scales, b1, offs2, wgt, gain, ws, out):
@@ -77,7 +78,6 @@ def tile_list_draft_tree_sketch_kernel(tc, tab_words, tab_scales, offs, w1_words
         ts_raw = staged([P, T], U8, "ts_raw", AT_TS_RAW)
         w1s_raw = tile([P, H], U8, "w1s_raw")
         ts_picked = staged([P, S], U8, "ts_picked", AT_TS_PICKED)
-        rows = staged([P, S + PASS], U8, "rows", AT_ROWS)
         scales = tile([P, K_PASSES, S + PASS], U8, "scales")
         scales_rest = tile([P, K_PASSES, H - PASS], U8, "scales_rest")
         w1p = {0: tile([P, K_PASSES, PASS * 2], U8, "w1p0")}
@@ -93,8 +93,8 @@ def tile_list_draft_tree_sketch_kernel(tc, tab_words, tab_scales, offs, w1_words
         gains = gains_pad[:, :, 0:PACK]
         bias = bias_pad[:, :, 0:PACK]
         strength = tile([P, SLOTS], F32, "strength")
-        half_gain = tile([P, H_PASSES, PACK], F32, "half_gain")
-        inv_capped = tile([P, H_PASSES, PACK], F32, "inv_capped")
+        half_first = staged([P, PACK], F32, "half_first", AT_HALF_FIRST)
+        half_rest = tile([P, H_PASSES - 1, PACK], F32, "half_rest")
         inv_gain = tile([P, H_PASSES, PACK], F32, "inv_gain")
         weights = [staged([P, SLOTS], F32, "weights%d" % r, AT_WEIGHTS + 4 * SLOTS * r) for r in range(SLICES)]
 
@@ -112,30 +112,26 @@ def tile_list_draft_tree_sketch_kernel(tc, tab_words, tab_scales, offs, w1_words
         nc.sync.dma_start(live[:], offs)
         load_scale_rows(ts_raw, tab_scales)
         load_scale_rows(w1s_raw, w1_scales)
-        nc.sync.dma_start(gains, gain.rearrange("(b p t) -> p b t", p=P, t=PACK))
+        nc.scalar.dma_start(gains, gain.rearrange("(b p t) -> p b t", p=P, t=PACK))
         nc.sync.dma_start(strength[:], wgt)
         nc.sync.dma_start(w1_first[:], w1_i32[:, :, 0 : PASS // 2])
         for a in range(K_PASSES):
             nc.sync.dma_start(tab[a][:], tab_words[a].rearrange("p t i -> p (t i)").bitcast(I32))
         nc.sync.dma_start(picks[:], offs2)
-        nc.sync.dma_start(bias, b1.rearrange("(b p t) -> p b t", p=P, t=PACK))
+        nc.scalar.dma_start(bias, b1.rearrange("(b p t) -> p b t", p=P, t=PACK))
 
         nc.vector.tensor_copy(ts_picked[:], ts_raw[:].indirect(live[:]))
 
         def order_scales(dst, src):
             nc.vector.tensor_copy(dst.rearrange("p (b t m) -> p t b m", t=PACK, m=P), src.rearrange("p (b m t) -> p t b m", t=PACK, m=P))
 
-        def deal_rows(dst, src):
+        def deal_rows(dst, src, queue):
             per_quadrant = K_PASSES * SCALE_ROWS
             for q in range(P // QUADRANT):
-                nc.sync.dma_start(
+                queue.dma_start(
                     dst[QUADRANT * q : QUADRANT * q + SCALE_ROWS, :, :].rearrange("p a c -> p (a c)").bitcast(I32),
                     src[ROWS_AT + per_quadrant * q : ROWS_AT + per_quadrant * (q + 1), :].bitcast(I32),
                 )
-
-        order_scales(rows[:, S : S + PASS], w1s_raw[:, 0:PASS])
-        nc.vector.tensor_copy(rows[ROWS_AT:P, 0:S].bitcast(I32), ts_picked[ROWS_AT:P, :].bitcast(I32))
-        deal_rows(scales, rows)
 
         def order_w1(b, src):
             if b > 0:
@@ -149,10 +145,21 @@ def tile_list_draft_tree_sketch_kernel(tc, tab_words, tab_scales, offs, w1_words
         w1_rest = staged([P, K_PASSES, (H - PASS) // 2], I32, "w1_rest", AT_W1_REST)
         nc.sync.dma_start(w1_rest[:], w1_i32[:, :, PASS // 2 : H // 2])
 
-        nc.scalar.mul(half_gain[:], gains, 0.5)
-        for r in range(SLICES):
+        def weigh(r):
             b, t = divmod(r, PACK)
-            nc.scalar.activation(weights[r][:], strength[:], ACT.Identity, scale=half_gain[:, b, t : t + 1])
+            half = half_first[:, t : t + 1] if b == 0 else half_rest[:, b - 1, t : t + 1]
+            nc.scalar.activation(weights[r][:], strength[:], ACT.Identity, scale=half)
+
+        nc.scalar.mul(half_first[:], gains[:, 0, :], 0.5)
+        nc.scalar.mul(half_rest[:], gains[:, 1:H_PASSES, :], 0.5)
+        for r in range(PACK):
+            weigh(r)
+        rows = staged([P, S + PASS], U8, "rows", AT_ROWS)
+        order_scales(rows[:, S : S + PASS], w1s_raw[:, 0:PASS])
+        nc.vector.tensor_copy(rows[ROWS_AT:P, 0:S].bitcast(I32), ts_picked[ROWS_AT:P, :].bitcast(I32))
+        deal_rows(scales, rows, nc.scalar)
+        for r in range(PACK, SLICES):
+            weigh(r)
 
         def load_ws(b):
             ws_raw[b] = staged([P, PACK, N], F32, "ws_raw%d" % b, AT_WS[b])
@@ -193,36 +200,23 @@ def tile_list_draft_tree_sketch_kernel(tc, tab_words, tab_scales, offs, w1_words
         for a in range(K_PASSES):
             for j in range(2):
                 gather_words(a, j)
-        for j in range(2):
-            project_pass(0, j, 0)
-        project_pass(0, 0, 1)
-        add_bias(0, 0)
-        project_pass(1, 0, 0)
-        project_pass(0, 1, 1)
-        add_bias(0, 1)
-        project_pass(1, 0, 1)
-        add_bias(1, 0)
-        for a in range(K_PASSES):
-            project_pass(1, 1, a)
-        add_bias(1, 1)
-        load_ws(1)
         rows_rest = staged([P, H - PASS], U8, "rows_rest", AT_ROWS_REST)
         order_scales(rows_rest[:], w1s_raw[:, PASS:H])
-        deal_rows(scales_rest, rows_rest)
+        deal_rows(scales_rest, rows_rest, nc.sync)
         order_w1(1, w1_rest[:, :, 0 : PASS // 2])
         order_w1(2, w1_rest[:, :, PASS // 2 : PASS])
+        load_ws(1)
         load_ws(2)
-        inv_half = staged([P, H_PASSES, PACK], F32, "inv_half", AT_INV)
-        nc.vector.reciprocal(inv_half[:], half_gain[:])
-        nc.vector.tensor_scalar(inv_capped[:], inv_half[:], 0.5, LARGEST, ALU.mult, ALU.min)
-        nc.vector.tensor_scalar_max(inv_gain[:], inv_capped[:], -LARGEST)
-        for r in range(FIRST_WAVE, AHEAD):
+        inv_raw = staged([P, H_PASSES, PACK], F32, "inv_raw", AT_INV)
+        nc.vector.reciprocal(inv_raw[:], gains)
+        nc.vector.tensor_scalar(inv_gain[:], inv_raw[:], LARGEST, -LARGEST, ALU.min, ALU.max)
+        for r in range(AHEAD):
             project(r)
 
         def weave_ws(b, i, copy):
             cols = slice(WS_PIECE * i, WS_PIECE * (i + 1))
             if b == 0:
-                ws_bf[b, i] = staged([P, WS_PIECE, PACK], BF16, "ws_bf0_%d" % i, AT_WEIGHTS + 4 * SLOTS * (WOVEN_ON + i))
+                ws_bf[b, i] = staged([P, WS_PIECE, PACK], BF16, "ws_bf0_%d" % i, AT_WEIGHTS + 4 * SLOTS * WOVEN_ON + 2 * PACK * WS_PIECE * i)
             else:
                 ws_bf[b, i] = tile([P, WS_PIECE, PACK], BF16, "ws_bf%d_%d" % (b, i))
             copy(
@@ -234,8 +228,8 @@ def tile_list_draft_tree_sketch_kernel(tc, tab_words, tab_scales, offs, w1_words
             cols = slice(WS_PIECE * i, WS_PIECE * (i + 1))
             nc.vector.quantize_mx(ws_q[b][:, cols].bitcast(FP8X4), ws_s[b][:, cols], ws_bf[b, i][:].rearrange("p n t -> p (n t)"))
 
-        units = [(0, 0, SLOTS), (1, 0, SLOTS), (2, 0, HALF), (2, HALF, HALF)]
-        unit_at = [0, 2 * UNIT_BYTES, 0, UNIT_BYTES]
+        units = [(0, 0, SLOTS), (1, 0, SLOTS), (2, 0, EARLY), (2, EARLY, LATE)]
+        unit_at = [0, 2 * UNIT_BYTES, 0, 0]
         ux = {}
         th = {}
         z = [tile([P, w, PACK], BF16, "z%d" % u) for u, (b, c, w) in enumerate(units)]
@@ -267,47 +261,53 @@ def tile_list_draft_tree_sketch_kernel(tc, tab_words, tab_scales, offs, w1_words
         def quantize_z(u, lo, hi):
             nc.vector.quantize_mx(z_q[u][:, lo:hi].bitcast(FP8X4), z_s[u][:, lo:hi], z[u][:, lo:hi, :].rearrange("p m t -> p (m t)"))
 
-        parts = [(0, HALF, 2), (HALF, QUARTER, 3), (HALF + QUARTER, QUARTER, 3)]
+        parts = [(0, EARLY, 1), (EARLY, LATE, 3)]
+        widths = [(HALF, LATE), (LATE,)]
         scores = {}
 
-        def score(part, b):
+        def score(part, b, tiles):
             c, w, per_bank = parts[part]
-            u = b if b < H_PASSES - 1 else b + c // HALF
-            lo = c - units[u][1]
-            for n in range(N // P):
+            u = b if b < H_PASSES - 1 else b + part
+            for n in tiles:
                 g, e = divmod(n, per_bank)
                 if b == 0 and e == 0:
                     scores[part, g] = psum.tile([P, per_bank, w], F32, name="score", tag="bank%d" % ((H_BANKS + len(scores)) % BANKS))
-                nc.tensor.matmul_mx(
-                    scores[part, g][:, e, :],
-                    lhsT=ws_q[b][:, P * n : P * (n + 1)].bitcast(FP8X4),
-                    lhsT_scale=ws_s[b][:, P * n : P * (n + 1)],
-                    rhs=z_q[u][:, lo : lo + w].bitcast(FP8X4),
-                    rhs_scale=z_s[u][:, lo : lo + w],
-                    start=(b == 0 and e == 0),
-                    stop=(b == H_PASSES - 1 and e == per_bank - 1),
-                )
+                done = 0
+                for width in widths[part]:
+                    lo = c - units[u][1] + done
+                    nc.tensor.matmul_mx(
+                        scores[part, g][:, e, done : done + width],
+                        lhsT=ws_q[b][:, P * n : P * (n + 1)].bitcast(FP8X4),
+                        lhsT_scale=ws_s[b][:, P * n : P * (n + 1)],
+                        rhs=z_q[u][:, lo : lo + width].bitcast(FP8X4),
+                        rhs_scale=z_s[u][:, lo : lo + width],
+                        start=(b == 0 and e == 0 and done == 0),
+                        stop=(b == H_PASSES - 1 and e == per_bank - 1 and done + width == w),
+                    )
+                    done += width
 
-        def store(part, copy):
+        def store(part, g, copy):
             c, w, per_bank = parts[part]
             out_rows = per_bank * P
-            for g in range(N // out_rows):
-                at = AT_RES + 4 * (c * (N // P) + g * per_bank * w)
-                res = staged([P, per_bank, w], F32, "res%d_%d" % (part, g), at)
-                copy(res[:], scores[part, g][:])
-                nc.sync.dma_start(out[out_rows * g : out_rows * (g + 1), c : c + w].rearrange("(e p) m -> p e m", p=P), res[:])
+            at = AT_RES + 4 * (c * (N // P) + g * per_bank * w)
+            res = staged([P, per_bank, w], F32, "res%d_%d" % (part, g), at)
+            copy(res[:], scores[part, g][:])
+            nc.sync.dma_start(out[out_rows * g : out_rows * (g + 1), c : c + w].rearrange("(e p) m -> p e m", p=P), res[:])
 
         steps = [(u, t) for u in range(len(units)) for t in range(PACK)]
         last_projected = SLICES - 1 - AHEAD
         pieces = N // WS_PIECE
-        weave_steps = [WOVEN_ON, WOVEN_ON + 1, WOVEN_ON + 2, 5, 7, 9, 10, 11, 12]
+        weave_steps = [WOVEN_ON + 1, WOVEN_ON + 2, 6, 9, 10, 11]
         score_steps = [last_projected, 3 * PACK - 1]
-        for s, (u, t) in enumerate(steps):
+        last_pass, last_unit = H_PASSES - 1, len(units) - 1
+        for s, (u, t) in enumerate(steps[:-PACK]):
             pick(u, t)
             if s <= last_projected:
                 project(s + AHEAD)
             if s > 0:
                 gate(*steps[s - 1])
+            if s == len(steps) - PACK - 1:
+                gate(u, t)
             if s in weave_steps:
                 b, i = divmod(weave_steps.index(s), pieces)
                 weave_ws(b, i, nc.vector.tensor_copy if b == 0 else nc.scalar.copy)
@@ -319,16 +319,28 @@ def tile_list_draft_tree_sketch_kernel(tc, tab_words, tab_scales, offs, w1_words
                 quantize_ws(*divmod(weave_steps.index(s - 1), pieces))
             if s in score_steps:
                 for part in range(len(parts)):
-                    score(part, score_steps.index(s))
+                    score(part, score_steps.index(s), range(N // P))
 
-        last_pass, last_unit = H_PASSES - 1, len(units) - 1
-        gate(*steps[-1])
-        score(0, last_pass)
-        store(0, nc.scalar.copy)
-        for lo in (0, QUARTER):
-            weave_z(last_unit, lo, lo + QUARTER)
-        for lo in (0, QUARTER):
-            quantize_z(last_unit, lo, lo + QUARTER)
-        for part, copy in ((1, nc.scalar.copy), (2, nc.vector.tensor_copy)):
-            score(part, last_pass)
-            store(part, copy)
+        tiles = N // P
+        weave_z(last_unit - 1, 0, EARLY)
+        pick(last_unit, 0)
+        quantize_z(last_unit - 1, 0, EARLY)
+        score(0, last_pass, range(tiles // 2))
+        gate(last_unit, 0)
+        pick(last_unit, 1)
+        gate(last_unit, 1)
+        quantize_ws(last_pass, pieces - 1)
+        score(0, last_pass, range(tiles // 2, tiles))
+        for t in range(2, PACK):
+            pick(last_unit, t)
+            gate(last_unit, t)
+        for g in range(tiles // 2):
+            store(0, g, nc.scalar.copy)
+        weave_z(last_unit, 0, LATE)
+        store(0, tiles // 2, nc.vector.tensor_copy)
+        quantize_z(last_unit, 0, LATE)
+        score(1, last_pass, range(tiles))
+        store(0, tiles - 2, nc.vector.tensor_copy)
+        store(0, tiles - 1, nc.scalar.copy)
+        store(1, 0, nc.vector.tensor_copy)
+        store(1, 1, nc.scalar.copy)

@@ -29,7 +29,7 @@ H_BANKS = 4
 HALF = SLOTS // 2
 LATE = SLOTS // 4
 EARLY = SLOTS - LATE
-RUN = 2
+RUN = 4
 QUADRANT = 32
 SCALE_ROWS = 4
 ROWS_AT = P - K_PASSES * 16

@@ -35,29 +35,35 @@ SCALE_ROWS = 4
 ROWS_AT = P - K_PASSES * 16
 PADDED = 8
 WS_PIECE = 384
+HELD = 1
 AHEAD = 3
 LARGEST = 3.0e38
 
 WS_BYTES = PACK * N * 4
 TAB_BYTES = 4 * T
 W1P_BYTES = 2 * K_PASSES * PASS
-AT_WS = (0, WS_BYTES, 2 * WS_BYTES)
-AT_ROWS = AT_WS[0]
+ON_GPSIMD = 2
+EDGE = 512
+AT_TAB = (0, TAB_BYTES)
+AT_W1P = AT_TAB[1]
+AT_INV = AT_W1P + 2 * W1P_BYTES
+AT_WS0 = AT_INV + 64
+AT_WS2 = AT_WS0 + WS_BYTES
+AT_ROWS = AT_WS2
 AT_HALF_FIRST = AT_ROWS
 AT_TS_RAW = AT_ROWS + S + PASS
-AT_TS_PICKED = AT_TS_RAW + T
-AT_W1_FIRST = AT_WS[2] - W1P_BYTES
-AT_W1_REST = AT_W1_FIRST
-AT_TAB = (3 * WS_BYTES, 3 * WS_BYTES + TAB_BYTES)
-AT_W1P = AT_TAB[1]
-AT_ROWS_REST = AT_W1P + 2 * W1P_BYTES
-AT_INV = AT_ROWS_REST + H - PASS
-AT_WEIGHTS = AT_TAB[1] + TAB_BYTES
-AT_UNITS = AT_WEIGHTS + SLICES * SLOTS * 4
+AT_WEIGHTS = AT_WS2 + WS_BYTES - EDGE
+AT_ROWS_REST = AT_WEIGHTS + SLICES * SLOTS * 4
+AT_W1_FIRST = AT_ROWS_REST - EDGE
+AT_W1_REST = AT_ROWS_REST + H - PASS
+AT_WS = (AT_WS0, AT_W1_REST, AT_WS2)
+AT_W1P_FIRST = AT_WS[1] + WS_BYTES
+AT_TS_PICKED = AT_W1P_FIRST
+AT_UNITS = AT_W1P_FIRST + W1P_BYTES
 STAGGER = 1
 UNIT_BYTES = PACK * SLOTS * 4 + 128
 AT_RES = AT_UNITS + 2 * UNIT_BYTES
-WOVEN_ON = 1
+WOVEN_ON = 2
 
 
 def tile_list_draft_tree_sketch_kernel(tc, tab_words, tab_scales, offs, w1_words, w1_scales, b1, offs2, wgt, gain, ws, out):
@@ -80,7 +86,7 @@ def tile_list_draft_tree_sketch_kernel(tc, tab_words, tab_scales, offs, w1_words
         ts_picked = staged([P, S], U8, "ts_picked", AT_TS_PICKED)
         scales = tile([P, K_PASSES, S + PASS], U8, "scales")
         scales_rest = tile([P, K_PASSES, H - PASS], U8, "scales_rest")
-        w1p = {0: tile([P, K_PASSES, PASS * 2], U8, "w1p0")}
+        w1p = {}
         tab = [staged([P, T], I32, "tab%d" % a, AT_TAB[a]) for a in range(K_PASSES)]
         v = [[tile([P, BANK], U32, "v%d_%d" % (a, j)) for j in range(2)] for a in range(K_PASSES)]
         ws_raw = {}
@@ -93,10 +99,11 @@ def tile_list_draft_tree_sketch_kernel(tc, tab_words, tab_scales, offs, w1_words
         gains = gains_pad[:, :, 0:PACK]
         bias = bias_pad[:, :, 0:PACK]
         strength = tile([P, SLOTS], F32, "strength")
-        half_first = staged([P, PACK], F32, "half_first", AT_HALF_FIRST)
-        half_rest = tile([P, H_PASSES - 1, PACK], F32, "half_rest")
+        half_first = staged([P, HELD], F32, "half_first", AT_HALF_FIRST)
+        half_gain = tile([P, H_PASSES, PACK], F32, "half_gain")
         inv_gain = tile([P, H_PASSES, PACK], F32, "inv_gain")
-        weights = [staged([P, SLOTS], F32, "weights%d" % r, AT_WEIGHTS + 4 * SLOTS * r) for r in range(SLICES)]
+        on_scalar = SLICES - ON_GPSIMD
+        weights = [staged([P, SLOTS], F32, "weights%d" % r, AT_WEIGHTS + 4 * SLOTS * r)[:] for r in range(on_scalar)]
 
         nc.vector.memset(ts_raw[0:ROWS_AT, :].bitcast(I32), 0)
         nc.vector.memset(w1s_raw[0:ROWS_AT, :].bitcast(I32), 0)
@@ -122,8 +129,8 @@ def tile_list_draft_tree_sketch_kernel(tc, tab_words, tab_scales, offs, w1_words
 
         nc.vector.tensor_copy(ts_picked[:], ts_raw[:].indirect(live[:]))
 
-        def order_scales(dst, src):
-            nc.vector.tensor_copy(dst.rearrange("p (b t m) -> p t b m", t=PACK, m=P), src.rearrange("p (b m t) -> p t b m", t=PACK, m=P))
+        def order_scales(engine, dst, src):
+            engine.tensor_copy(dst.rearrange("p (b t m) -> p t b m", t=PACK, m=P), src.rearrange("p (b m t) -> p t b m", t=PACK, m=P))
 
         def deal_rows(dst, src, queue):
             per_quadrant = K_PASSES * SCALE_ROWS
@@ -134,81 +141,85 @@ def tile_list_draft_tree_sketch_kernel(tc, tab_words, tab_scales, offs, w1_words
                 )
 
         def order_w1(b, src):
-            if b > 0:
-                w1p[b] = staged([P, K_PASSES, PASS * 2], U8, "w1p%d" % b, AT_W1P + W1P_BYTES * (b - 1))
+            w1p[b] = staged([P, K_PASSES, PASS * 2], U8, "w1p%d" % b, AT_W1P + W1P_BYTES * (b - 1) if b > 0 else AT_W1P_FIRST)
             nc.vector.tensor_copy(
                 w1p[b][:].bitcast(U16).rearrange("p a (t m) -> p a t m", t=PACK),
                 src.bitcast(U16).rearrange("p a (m t) -> p a t m", t=PACK),
             )
 
+        def weigh(r):
+            b, t = divmod(r, PACK)
+            half = half_first[:, r : r + 1] if r < HELD else half_gain[:, b, t : t + 1]
+            nc.scalar.activation(weights[r], strength[:], ACT.Identity, scale=half)
+
+        nc.scalar.mul(half_first[:], gains[:, 0, 0:HELD], 0.5)
+        nc.scalar.mul(half_gain[:], gains, 0.5)
+        for r in range(HELD):
+            weigh(r)
+        rows = staged([P, S + PASS], U8, "rows", AT_ROWS)
+        order_scales(nc.vector, rows[:, S : S + PASS], w1s_raw[:, 0:PASS])
+        nc.vector.tensor_copy(rows[ROWS_AT:P, 0:S].bitcast(I32), ts_picked[ROWS_AT:P, :].bitcast(I32))
+        deal_rows(scales, rows, nc.scalar)
+        for r in range(HELD, on_scalar):
+            weigh(r)
+
         order_w1(0, w1_first[:])
         w1_rest = staged([P, K_PASSES, (H - PASS) // 2], I32, "w1_rest", AT_W1_REST)
         nc.sync.dma_start(w1_rest[:], w1_i32[:, :, PASS // 2 : H // 2])
-
-        def weigh(r):
+        rows_rest = staged([P, H - PASS], U8, "rows_rest", AT_ROWS_REST)
+        order_scales(nc.gpsimd, rows_rest[:], w1s_raw[:, PASS:H])
+        deal_rows(scales_rest, rows_rest, nc.sync)
+        weights_last = staged([P, ON_GPSIMD, SLOTS], F32, "weights_last", AT_WEIGHTS + 4 * SLOTS * on_scalar)
+        for r in range(on_scalar, SLICES):
             b, t = divmod(r, PACK)
-            half = half_first[:, t : t + 1] if b == 0 else half_rest[:, b - 1, t : t + 1]
-            nc.scalar.activation(weights[r][:], strength[:], ACT.Identity, scale=half)
-
-        nc.scalar.mul(half_first[:], gains[:, 0, :], 0.5)
-        nc.scalar.mul(half_rest[:], gains[:, 1:H_PASSES, :], 0.5)
-        for r in range(PACK):
-            weigh(r)
-        rows = staged([P, S + PASS], U8, "rows", AT_ROWS)
-        order_scales(rows[:, S : S + PASS], w1s_raw[:, 0:PASS])
-        nc.vector.tensor_copy(rows[ROWS_AT:P, 0:S].bitcast(I32), ts_picked[ROWS_AT:P, :].bitcast(I32))
-        deal_rows(scales, rows, nc.scalar)
-        for r in range(PACK, SLICES):
-            weigh(r)
+            nc.gpsimd.tensor_scalar(weights_last[:, r - on_scalar, :], strength[:], half_gain[:, b, t : t + 1], 0.0, ALU.mult, ALU.add)
+            weights.append(weights_last[:, r - on_scalar, :])
 
         def load_ws(b):
             ws_raw[b] = staged([P, PACK, N], F32, "ws_raw%d" % b, AT_WS[b])
             nc.sync.dma_start(ws_raw[b][:], ws[PASS * b : PASS * (b + 1), :].rearrange("(p t) n -> p t n", t=PACK))
 
-        load_ws(0)
+        def gather_words(a, j, lo, hi):
+            entries = live[:, (BANK * j + lo) // LIST : (BANK * j + hi) // LIST]
+            nc.vector.tensor_copy(v[a][j][:, lo:hi], tab[a][:].bitcast(U32).indirect(entries))
 
-        def gather_words(a, j):
-            columns = BANK // LIST
-            nc.vector.tensor_copy(v[a][j][:], tab[a][:].bitcast(U32).indirect(live[:, columns * j : columns * (j + 1)]))
-
-        acc = {}
-
-        def project_pass(r, j, a):
+        def project_part(r, j, lo, hi, bank):
             b, t = divmod(r, PACK)
-            if a == 0:
-                acc[r, j] = psum.tile([P, BANK], F32, name="acc", tag="bank%d" % (len(acc) % H_BANKS))
-            nc.tensor.matmul_mx(
-                acc[r, j][:],
-                lhsT=w1p[b][:, a, 2 * P * t : 2 * P * (t + 1)].bitcast(FP4X4),
-                lhsT_scale=scales[:, a, S + P * r : S + P * (r + 1)] if b == 0 else scales_rest[:, a, P * (r - PACK) : P * (r - PACK + 1)],
-                rhs=v[a][j][:].bitcast(FP8X4),
-                rhs_scale=scales[:, a, BANK * j : BANK * (j + 1)],
-                start=(a == 0),
-                stop=(a == K_PASSES - 1),
-            )
-
-        def add_bias(r, j):
-            b, t = divmod(r, PACK)
-            nc.scalar.activation(h[r][:, BANK * j : BANK * (j + 1)], acc[r, j][:], ACT.Identity, bias=bias[:, b, t : t + 1])
+            acc = psum.tile([P, hi - lo], F32, name="acc", tag="bank%d" % bank)
+            cols = slice(BANK * j + lo, BANK * j + hi)
+            passes = list(range(K_PASSES)) if r == 0 else list(reversed(range(K_PASSES)))
+            for a in passes:
+                nc.tensor.matmul_mx(
+                    acc[:],
+                    lhsT=w1p[b][:, a, 2 * P * t : 2 * P * (t + 1)].bitcast(FP4X4),
+                    lhsT_scale=scales[:, a, S + P * r : S + P * (r + 1)] if b == 0 else scales_rest[:, a, P * (r - PACK) : P * (r - PACK + 1)],
+                    rhs=v[a][j][:, lo:hi].bitcast(FP8X4),
+                    rhs_scale=scales[:, a, cols],
+                    start=(a == passes[0]),
+                    stop=(a == passes[-1]),
+                )
+            nc.scalar.activation(h[r][:, cols], acc[:], ACT.Identity, bias=bias[:, b, t : t + 1])
 
         def project(r):
-            for j in range(2):
-                for a in range(K_PASSES):
-                    project_pass(r, j, a)
-                add_bias(r, j)
+            if r == 0:
+                project_part(r, 0, 0, BANK, 0)
+                project_part(r, 1, 0, BANK // 2, 1)
+                project_part(r, 1, BANK // 2, BANK, H_BANKS)
+            else:
+                for j in range(2):
+                    project_part(r, j, 0, BANK, (r + 1) % 2 + 2 * j)
 
-        for a in range(K_PASSES):
-            for j in range(2):
-                gather_words(a, j)
-        rows_rest = staged([P, H - PASS], U8, "rows_rest", AT_ROWS_REST)
-        order_scales(rows_rest[:], w1s_raw[:, PASS:H])
-        deal_rows(scales_rest, rows_rest, nc.sync)
+        for j in range(2):
+            gather_words(0, j, 0, BANK)
+        gather_words(1, 0, 0, BANK)
+        gather_words(1, 1, 0, BANK // 2)
+        gather_words(1, 1, BANK // 2, BANK)
+        inv_raw = staged([P, H_PASSES, PACK], F32, "inv_raw", AT_INV)
+        nc.vector.reciprocal(inv_raw[:], gains)
+        load_ws(0)
         order_w1(1, w1_rest[:, :, 0 : PASS // 2])
         order_w1(2, w1_rest[:, :, PASS // 2 : PASS])
         load_ws(1)
-        load_ws(2)
-        inv_raw = staged([P, H_PASSES, PACK], F32, "inv_raw", AT_INV)
-        nc.vector.reciprocal(inv_raw[:], gains)
         nc.vector.tensor_scalar(inv_gain[:], inv_raw[:], LARGEST, -LARGEST, ALU.min, ALU.max)
         for r in range(AHEAD):
             project(r)
@@ -302,6 +313,8 @@ def tile_list_draft_tree_sketch_kernel(tc, tab_words, tab_scales, offs, w1_words
         last_pass, last_unit = H_PASSES - 1, len(units) - 1
         for s, (u, t) in enumerate(steps[:-PACK]):
             pick(u, t)
+            if s == 0:
+                load_ws(2)
             if s <= last_projected:
                 project(s + AHEAD)
             if s > 0:
@@ -312,9 +325,10 @@ def tile_list_draft_tree_sketch_kernel(tc, tab_words, tab_scales, offs, w1_words
                 b, i = divmod(weave_steps.index(s), pieces)
                 weave_ws(b, i, nc.vector.tensor_copy if b == 0 else nc.scalar.copy)
             if u > 0 and t == 1:
-                weave_z(u - 1, 0, units[u - 1][2])
-            if u > 0 and t == 2:
-                quantize_z(u - 1, 0, units[u - 1][2])
+                for lo in (0, HALF):
+                    weave_z(u - 1, lo, lo + HALF)
+                for lo in (0, HALF):
+                    quantize_z(u - 1, lo, lo + HALF)
             if s - 1 in weave_steps:
                 quantize_ws(*divmod(weave_steps.index(s - 1), pieces))
             if s in score_steps:

@@ -36,6 +36,7 @@ ROWS_AT = P - K_PASSES * 16
 PADDED = 8
 WS_PIECE = 384
 HELD = 1
+WARM_UPS = 3
 AHEAD = 3
 LARGEST = 3.0e38
 
@@ -209,8 +210,19 @@ def tile_list_draft_tree_sketch_kernel(tc, tab_words, tab_scales, offs, w1_words
                 for j in range(2):
                     project_part(r, j, 0, BANK, (r + 1) % 2 + 2 * j)
 
-        for j in range(2):
-            gather_words(0, j, 0, BANK)
+        gather_words(0, 0, 0, BANK)
+        warm = psum.tile([P, BANK], F32, name="warm", tag="bank%d" % (BANKS - 1))
+        for n in range(WARM_UPS):
+            nc.tensor.matmul_mx(
+                warm[:],
+                lhsT=w1p[0][:, 0, 0 : 2 * P].bitcast(FP4X4),
+                lhsT_scale=w1s_raw[:, 0:P],
+                rhs=v[0][0][:].bitcast(FP8X4),
+                rhs_scale=ts_raw[:, 0:BANK],
+                start=True,
+                stop=True,
+            )
+        gather_words(0, 1, 0, BANK)
         gather_words(1, 0, 0, BANK)
         gather_words(1, 1, 0, BANK // 2)
         gather_words(1, 1, BANK // 2, BANK)

@@ -35,32 +35,33 @@ SCALE_ROWS = 4
 ROWS_AT = P - K_PASSES * 16
 PADDED = 8
 WS_PIECE = 384
-HELD = 1
-WARM_UPS = 3
+WARM_UPS = 2
 AHEAD = 3
 LARGEST = 3.0e38
 
 WS_BYTES = PACK * N * 4
 TAB_BYTES = 4 * T
 W1P_BYTES = 2 * K_PASSES * PASS
-ON_GPSIMD = 2
+WEIGHT_BYTES = 4 * SLOTS
+ON_SCALAR = 8
+GPSIMD_FIRST = 2
 EDGE = 512
-AT_TAB = (0, TAB_BYTES)
-AT_W1P = AT_TAB[1]
-AT_INV = AT_W1P + 2 * W1P_BYTES
-AT_WS0 = AT_INV + 64
-AT_WS2 = AT_WS0 + WS_BYTES
-AT_ROWS = AT_WS2
-AT_HALF_FIRST = AT_ROWS
-AT_TS_RAW = AT_ROWS + S + PASS
-AT_WEIGHTS = AT_WS2 + WS_BYTES - EDGE
-AT_ROWS_REST = AT_WEIGHTS + SLICES * SLOTS * 4
-AT_W1_FIRST = AT_ROWS_REST - EDGE
-AT_W1_REST = AT_ROWS_REST + H - PASS
-AT_WS = (AT_WS0, AT_W1_REST, AT_WS2)
-AT_W1P_FIRST = AT_WS[1] + WS_BYTES
-AT_TS_PICKED = AT_W1P_FIRST
-AT_UNITS = AT_W1P_FIRST + W1P_BYTES
+AT_TAB = (TAB_BYTES, 0)
+AT_INV = 2 * TAB_BYTES - 64
+AT_WS1 = 0
+AT_ROWS_REST = 2 * TAB_BYTES
+AT_WS2 = AT_ROWS_REST
+AT_TS_RAW = AT_WS2 + WS_BYTES
+AT_W1_FIRST = AT_TS_RAW + T
+AT_W1_REST = AT_W1_FIRST + W1P_BYTES
+AT_HALF_LAST = AT_W1_REST + 2 * W1P_BYTES
+AT_TS_PICKED = AT_HALF_LAST - EDGE
+AT_SCALES_REST = AT_HALF_LAST + 64
+AT_WEIGHTS = AT_SCALES_REST + K_PASSES * (H - PASS)
+AT_ROWS = AT_WEIGHTS + SLICES * WEIGHT_BYTES
+AT_WS0 = AT_ROWS
+AT_WS = (AT_WS0, AT_WS1, AT_WS2)
+AT_UNITS = AT_WS0 + WS_BYTES
 STAGGER = 1
 UNIT_BYTES = PACK * SLOTS * 4 + 128
 AT_RES = AT_UNITS + 2 * UNIT_BYTES
@@ -85,8 +86,10 @@ def tile_list_draft_tree_sketch_kernel(tc, tab_words, tab_scales, offs, w1_words
         ts_raw = staged([P, T], U8, "ts_raw", AT_TS_RAW)
         w1s_raw = tile([P, H], U8, "w1s_raw")
         ts_picked = staged([P, S], U8, "ts_picked", AT_TS_PICKED)
+        rows = staged([P, S + PASS], U8, "rows", AT_ROWS)
         scales = tile([P, K_PASSES, S + PASS], U8, "scales")
-        scales_rest = tile([P, K_PASSES, H - PASS], U8, "scales_rest")
+        rows_rest = staged([P, H - PASS], U8, "rows_rest", AT_ROWS_REST)
+        half_last = staged([P, SLICES - ON_SCALAR - GPSIMD_FIRST], F32, "half_last", AT_HALF_LAST)
         w1p = {}
         tab = [staged([P, T], I32, "tab%d" % a, AT_TAB[a]) for a in range(K_PASSES)]
         v = [[tile([P, BANK], U32, "v%d_%d" % (a, j)) for j in range(2)] for a in range(K_PASSES)]
@@ -100,16 +103,14 @@ def tile_list_draft_tree_sketch_kernel(tc, tab_words, tab_scales, offs, w1_words
         gains = gains_pad[:, :, 0:PACK]
         bias = bias_pad[:, :, 0:PACK]
         strength = tile([P, SLOTS], F32, "strength")
-        half_first = staged([P, HELD], F32, "half_first", AT_HALF_FIRST)
         half_gain = tile([P, H_PASSES, PACK], F32, "half_gain")
         inv_gain = tile([P, H_PASSES, PACK], F32, "inv_gain")
-        on_scalar = SLICES - ON_GPSIMD
-        weights = [staged([P, SLOTS], F32, "weights%d" % r, AT_WEIGHTS + 4 * SLOTS * r)[:] for r in range(on_scalar)]
+        unheld = ON_SCALAR + GPSIMD_FIRST
+        weights = [staged([P, SLOTS], F32, "weights%d" % r, AT_WEIGHTS + WEIGHT_BYTES * r)[:] for r in range(SLICES)]
 
-        nc.vector.memset(ts_raw[0:ROWS_AT, :].bitcast(I32), 0)
         nc.vector.memset(w1s_raw[0:ROWS_AT, :].bitcast(I32), 0)
+        nc.vector.memset(ts_raw[0:ROWS_AT, :].bitcast(I32), 0)
         nc.vector.memset(scales[:].rearrange("p a c -> p (a c)").bitcast(I32), 0)
-        nc.vector.memset(scales_rest[:].rearrange("p a c -> p (a c)").bitcast(I32), 0)
 
         w1_i32 = w1_words.bitcast(I32).rearrange("a p c -> p a c")
 
@@ -117,21 +118,19 @@ def tile_list_draft_tree_sketch_kernel(tc, tab_words, tab_scales, offs, w1_words
             nc.sync.dma_start(dst[ROWS_AT:P, :].bitcast(I32), src.bitcast(I32).rearrange("a j c -> j a c"))
 
         w1_first = staged([P, K_PASSES, PASS // 2], I32, "w1_first", AT_W1_FIRST)
+        load_scale_rows(w1s_raw, w1_scales)
         nc.sync.dma_start(live[:], offs)
         load_scale_rows(ts_raw, tab_scales)
-        load_scale_rows(w1s_raw, w1_scales)
         nc.scalar.dma_start(gains, gain.rearrange("(b p t) -> p b t", p=P, t=PACK))
         nc.sync.dma_start(strength[:], wgt)
-        nc.sync.dma_start(w1_first[:], w1_i32[:, :, 0 : PASS // 2])
         for a in range(K_PASSES):
             nc.sync.dma_start(tab[a][:], tab_words[a].rearrange("p t i -> p (t i)").bitcast(I32))
+        nc.sync.dma_start(w1_first[:], w1_i32[:, :, 0 : PASS // 2])
         nc.sync.dma_start(picks[:], offs2)
         nc.scalar.dma_start(bias, b1.rearrange("(b p t) -> p b t", p=P, t=PACK))
 
-        nc.vector.tensor_copy(ts_picked[:], ts_raw[:].indirect(live[:]))
-
-        def order_scales(engine, dst, src):
-            engine.tensor_copy(dst.rearrange("p (b t m) -> p t b m", t=PACK, m=P), src.rearrange("p (b m t) -> p t b m", t=PACK, m=P))
+        def order_scales(dst, src):
+            nc.vector.tensor_copy(dst.rearrange("p (b t m) -> p t b m", t=PACK, m=P), src.rearrange("p (b m t) -> p t b m", t=PACK, m=P))
 
         def deal_rows(dst, src, queue):
             per_quadrant = K_PASSES * SCALE_ROWS
@@ -141,40 +140,38 @@ def tile_list_draft_tree_sketch_kernel(tc, tab_words, tab_scales, offs, w1_words
                     src[ROWS_AT + per_quadrant * q : ROWS_AT + per_quadrant * (q + 1), :].bitcast(I32),
                 )
 
-        def order_w1(b, src):
-            w1p[b] = staged([P, K_PASSES, PASS * 2], U8, "w1p%d" % b, AT_W1P + W1P_BYTES * (b - 1) if b > 0 else AT_W1P_FIRST)
-            nc.vector.tensor_copy(
-                w1p[b][:].bitcast(U16).rearrange("p a (t m) -> p a t m", t=PACK),
-                src.bitcast(U16).rearrange("p a (m t) -> p a t m", t=PACK),
+        def order_w1(b, src, copy, walk):
+            w1p[b] = tile([P, K_PASSES, PASS * 2], U8, "w1p%d" % b)
+            copy(
+                w1p[b][:].bitcast(U16).rearrange("p a (t m) -> " + walk, t=PACK),
+                src.bitcast(U16).rearrange("p a (m t) -> " + walk, t=PACK),
             )
 
         def weigh(r):
             b, t = divmod(r, PACK)
-            half = half_first[:, r : r + 1] if r < HELD else half_gain[:, b, t : t + 1]
-            nc.scalar.activation(weights[r], strength[:], ACT.Identity, scale=half)
+            if r < ON_SCALAR:
+                nc.scalar.activation(weights[r], strength[:], ACT.Identity, scale=half_gain[:, b, t : t + 1])
+            else:
+                half = half_gain[:, b, t : t + 1] if r < unheld else half_last[:, r - unheld : r - unheld + 1]
+                nc.gpsimd.tensor_scalar(weights[r], strength[:], half, 0.0, ALU.mult, ALU.add)
 
-        nc.scalar.mul(half_first[:], gains[:, 0, 0:HELD], 0.5)
-        nc.scalar.mul(half_gain[:], gains, 0.5)
-        for r in range(HELD):
-            weigh(r)
-        rows = staged([P, S + PASS], U8, "rows", AT_ROWS)
-        order_scales(nc.vector, rows[:, S : S + PASS], w1s_raw[:, 0:PASS])
+        order_scales(rows[:, S : S + PASS], w1s_raw[:, 0:PASS])
+        order_scales(rows_rest[:], w1s_raw[:, PASS:H])
+        nc.vector.tensor_copy(ts_picked[:], ts_raw[:].indirect(live[:]))
         nc.vector.tensor_copy(rows[ROWS_AT:P, 0:S].bitcast(I32), ts_picked[ROWS_AT:P, :].bitcast(I32))
-        deal_rows(scales, rows, nc.scalar)
-        for r in range(HELD, on_scalar):
-            weigh(r)
-
-        order_w1(0, w1_first[:])
+        nc.scalar.mul(half_gain[:], gains, 0.5)
+        deal_rows(scales, rows, nc.sync)
         w1_rest = staged([P, K_PASSES, (H - PASS) // 2], I32, "w1_rest", AT_W1_REST)
         nc.sync.dma_start(w1_rest[:], w1_i32[:, :, PASS // 2 : H // 2])
-        rows_rest = staged([P, H - PASS], U8, "rows_rest", AT_ROWS_REST)
-        order_scales(nc.gpsimd, rows_rest[:], w1s_raw[:, PASS:H])
+        for r in range(unheld):
+            weigh(r)
+        order_w1(0, w1_first[:], nc.scalar.copy, "p a m t")
+        scales_rest = staged([P, K_PASSES, H - PASS], U8, "scales_rest", AT_SCALES_REST)
+        nc.gpsimd.memset(scales_rest[:].rearrange("p a c -> p (a c)").bitcast(I32), 0)
         deal_rows(scales_rest, rows_rest, nc.sync)
-        weights_last = staged([P, ON_GPSIMD, SLOTS], F32, "weights_last", AT_WEIGHTS + 4 * SLOTS * on_scalar)
-        for r in range(on_scalar, SLICES):
-            b, t = divmod(r, PACK)
-            nc.gpsimd.tensor_scalar(weights_last[:, r - on_scalar, :], strength[:], half_gain[:, b, t : t + 1], 0.0, ALU.mult, ALU.add)
-            weights.append(weights_last[:, r - on_scalar, :])
+        nc.gpsimd.tensor_scalar(half_last[:], gains[:, H_PASSES - 1, unheld - SLICES + PACK : PACK], 0.5, 0.0, ALU.mult, ALU.add)
+        for r in range(unheld, SLICES):
+            weigh(r)
 
         def load_ws(b):
             ws_raw[b] = staged([P, PACK, N], F32, "ws_raw%d" % b, AT_WS[b])
@@ -188,7 +185,7 @@ def tile_list_draft_tree_sketch_kernel(tc, tab_words, tab_scales, offs, w1_words
             b, t = divmod(r, PACK)
             acc = psum.tile([P, hi - lo], F32, name="acc", tag="bank%d" % bank)
             cols = slice(BANK * j + lo, BANK * j + hi)
-            passes = list(range(K_PASSES)) if r == 0 else list(reversed(range(K_PASSES)))
+            passes = list(range(K_PASSES)) if r == 0 or (r == 1 and j == 0) else list(reversed(range(K_PASSES)))
             for a in passes:
                 nc.tensor.matmul_mx(
                     acc[:],
@@ -202,38 +199,39 @@ def tile_list_draft_tree_sketch_kernel(tc, tab_words, tab_scales, offs, w1_words
             nc.scalar.activation(h[r][:, cols], acc[:], ACT.Identity, bias=bias[:, b, t : t + 1])
 
         def project(r):
-            if r == 0:
-                project_part(r, 0, 0, BANK, 0)
-                project_part(r, 1, 0, BANK // 2, 1)
-                project_part(r, 1, BANK // 2, BANK, H_BANKS)
-            else:
-                for j in range(2):
-                    project_part(r, j, 0, BANK, (r + 1) % 2 + 2 * j)
+            for j in range(2):
+                project_part(r, j, 0, BANK, r % 2 + 2 * j)
 
         gather_words(0, 0, 0, BANK)
         warm = psum.tile([P, BANK], F32, name="warm", tag="bank%d" % (BANKS - 1))
         for n in range(WARM_UPS):
             nc.tensor.matmul_mx(
                 warm[:],
-                lhsT=w1p[0][:, 0, 0 : 2 * P].bitcast(FP4X4),
+                lhsT=w1_first[:, 0, 0 : P // 2].bitcast(U8).bitcast(FP4X4),
                 lhsT_scale=w1s_raw[:, 0:P],
                 rhs=v[0][0][:].bitcast(FP8X4),
-                rhs_scale=ts_raw[:, 0:BANK],
+                rhs_scale=w1s_raw[:, 0:BANK],
                 start=True,
                 stop=True,
             )
         gather_words(0, 1, 0, BANK)
+        inv_raw = staged([P, H_PASSES, PACK], F32, "inv_raw", AT_INV)
+        nc.vector.reciprocal(inv_raw[:], gains)
         gather_words(1, 0, 0, BANK)
         gather_words(1, 1, 0, BANK // 2)
         gather_words(1, 1, BANK // 2, BANK)
-        inv_raw = staged([P, H_PASSES, PACK], F32, "inv_raw", AT_INV)
-        nc.vector.reciprocal(inv_raw[:], gains)
         load_ws(0)
-        order_w1(1, w1_rest[:, :, 0 : PASS // 2])
-        order_w1(2, w1_rest[:, :, PASS // 2 : PASS])
         load_ws(1)
         nc.vector.tensor_scalar(inv_gain[:], inv_raw[:], LARGEST, -LARGEST, ALU.min, ALU.max)
-        for r in range(AHEAD):
+        order_w1(1, w1_rest[:, :, 0 : PASS // 2], nc.vector.tensor_copy, "p a t m")
+        order_w1(2, w1_rest[:, :, PASS // 2 : PASS], nc.vector.tensor_copy, "p a t m")
+        load_ws(2)
+        project_part(0, 0, 0, BANK, 0)
+        project_part(1, 0, 0, BANK, 1)
+        project_part(0, 1, 0, BANK // 2, 2)
+        project_part(0, 1, BANK // 2, BANK, H_BANKS)
+        project_part(1, 1, 0, BANK, 3)
+        for r in range(2, AHEAD):
             project(r)
 
         def weave_ws(b, i, copy):
@@ -325,8 +323,6 @@ def tile_list_draft_tree_sketch_kernel(tc, tab_words, tab_scales, offs, w1_words
         last_pass, last_unit = H_PASSES - 1, len(units) - 1
         for s, (u, t) in enumerate(steps[:-PACK]):
             pick(u, t)
-            if s == 0:
-                load_ws(2)
             if s <= last_projected:
                 project(s + AHEAD)
             if s > 0:

@@ -25,7 +25,7 @@ SLICES = H_PASSES * PACK
 LIST = 16
 BANK = 512
 BANKS = 8
-H_BANKS = 4
+H_BANKS = 7
 HALF = SLOTS // 2
 LATE = SLOTS // 4
 EARLY = SLOTS - LATE
@@ -35,7 +35,7 @@ SCALE_ROWS = 4
 ROWS_AT = P - K_PASSES * 16
 PADDED = 8
 WS_PIECE = 384
-WARM_UPS = 2
+WARM_UPS = 4
 AHEAD = 3
 LARGEST = 3.0e38
 
@@ -43,11 +43,10 @@ WS_BYTES = PACK * N * 4
 TAB_BYTES = 4 * T
 W1P_BYTES = 2 * K_PASSES * PASS
 WEIGHT_BYTES = 4 * SLOTS
-ON_SCALAR = 8
-GPSIMD_FIRST = 2
+ON_SCALAR = 7
 EDGE = 512
-AT_TAB = (TAB_BYTES, 0)
-AT_INV = 2 * TAB_BYTES - 64
+AT_TAB = (0, TAB_BYTES)
+AT_INV = WS_BYTES + 64
 AT_WS1 = 0
 AT_ROWS_REST = 2 * TAB_BYTES
 AT_WS2 = AT_ROWS_REST
@@ -89,7 +88,7 @@ def tile_list_draft_tree_sketch_kernel(tc, tab_words, tab_scales, offs, w1_words
         rows = staged([P, S + PASS], U8, "rows", AT_ROWS)
         scales = tile([P, K_PASSES, S + PASS], U8, "scales")
         rows_rest = staged([P, H - PASS], U8, "rows_rest", AT_ROWS_REST)
-        half_last = staged([P, SLICES - ON_SCALAR - GPSIMD_FIRST], F32, "half_last", AT_HALF_LAST)
+        half_last = staged([P, SLICES - ON_SCALAR], F32, "half_last", AT_HALF_LAST)
         w1p = {}
         tab = [staged([P, T], I32, "tab%d" % a, AT_TAB[a]) for a in range(K_PASSES)]
         v = [[tile([P, BANK], U32, "v%d_%d" % (a, j)) for j in range(2)] for a in range(K_PASSES)]
@@ -103,13 +102,12 @@ def tile_list_draft_tree_sketch_kernel(tc, tab_words, tab_scales, offs, w1_words
         gains = gains_pad[:, :, 0:PACK]
         bias = bias_pad[:, :, 0:PACK]
         strength = tile([P, SLOTS], F32, "strength")
-        half_gain = tile([P, H_PASSES, PACK], F32, "half_gain")
+        half_gain = tile([P, H_PASSES - 1, PACK], F32, "half_gain")
         inv_gain = tile([P, H_PASSES, PACK], F32, "inv_gain")
-        unheld = ON_SCALAR + GPSIMD_FIRST
         weights = [staged([P, SLOTS], F32, "weights%d" % r, AT_WEIGHTS + WEIGHT_BYTES * r)[:] for r in range(SLICES)]
 
-        nc.vector.memset(w1s_raw[0:ROWS_AT, :].bitcast(I32), 0)
         nc.vector.memset(ts_raw[0:ROWS_AT, :].bitcast(I32), 0)
+        nc.vector.memset(w1s_raw[0:ROWS_AT, :].bitcast(I32), 0)
         nc.vector.memset(scales[:].rearrange("p a c -> p (a c)").bitcast(I32), 0)
 
         w1_i32 = w1_words.bitcast(I32).rearrange("a p c -> p a c")
@@ -118,9 +116,9 @@ def tile_list_draft_tree_sketch_kernel(tc, tab_words, tab_scales, offs, w1_words
             nc.sync.dma_start(dst[ROWS_AT:P, :].bitcast(I32), src.bitcast(I32).rearrange("a j c -> j a c"))
 
         w1_first = staged([P, K_PASSES, PASS // 2], I32, "w1_first", AT_W1_FIRST)
-        load_scale_rows(w1s_raw, w1_scales)
         nc.sync.dma_start(live[:], offs)
         load_scale_rows(ts_raw, tab_scales)
+        load_scale_rows(w1s_raw, w1_scales)
         nc.scalar.dma_start(gains, gain.rearrange("(b p t) -> p b t", p=P, t=PACK))
         nc.sync.dma_start(strength[:], wgt)
         for a in range(K_PASSES):
@@ -129,8 +127,8 @@ def tile_list_draft_tree_sketch_kernel(tc, tab_words, tab_scales, offs, w1_words
         nc.sync.dma_start(picks[:], offs2)
         nc.scalar.dma_start(bias, b1.rearrange("(b p t) -> p b t", p=P, t=PACK))
 
-        def order_scales(dst, src):
-            nc.vector.tensor_copy(dst.rearrange("p (b t m) -> p t b m", t=PACK, m=P), src.rearrange("p (b m t) -> p t b m", t=PACK, m=P))
+        def order_scales(engine, dst, src):
+            engine.tensor_copy(dst.rearrange("p (b t m) -> p t b m", t=PACK, m=P), src.rearrange("p (b m t) -> p t b m", t=PACK, m=P))
 
         def deal_rows(dst, src, queue):
             per_quadrant = K_PASSES * SCALE_ROWS
@@ -140,11 +138,12 @@ def tile_list_draft_tree_sketch_kernel(tc, tab_words, tab_scales, offs, w1_words
                     src[ROWS_AT + per_quadrant * q : ROWS_AT + per_quadrant * (q + 1), :].bitcast(I32),
                 )
 
-        def order_w1(b, src, copy, walk):
-            w1p[b] = tile([P, K_PASSES, PASS * 2], U8, "w1p%d" % b)
+        def order_w1(b, src, copy, walk, lo, hi):
+            if lo == 0:
+                w1p[b] = tile([P, K_PASSES, PASS * 2], U8, "w1p%d" % b)
             copy(
-                w1p[b][:].bitcast(U16).rearrange("p a (t m) -> " + walk, t=PACK),
-                src.bitcast(U16).rearrange("p a (m t) -> " + walk, t=PACK),
+                w1p[b][:].bitcast(U16).rearrange("p a (t m) -> p a t m", t=PACK)[:, :, lo:hi, :].rearrange("p a t m -> " + walk),
+                src.bitcast(U16).rearrange("p a (m t) -> p a t m", t=PACK)[:, :, lo:hi, :].rearrange("p a t m -> " + walk),
             )
 
         def weigh(r):
@@ -152,25 +151,27 @@ def tile_list_draft_tree_sketch_kernel(tc, tab_words, tab_scales, offs, w1_words
             if r < ON_SCALAR:
                 nc.scalar.activation(weights[r], strength[:], ACT.Identity, scale=half_gain[:, b, t : t + 1])
             else:
-                half = half_gain[:, b, t : t + 1] if r < unheld else half_last[:, r - unheld : r - unheld + 1]
-                nc.gpsimd.tensor_scalar(weights[r], strength[:], half, 0.0, ALU.mult, ALU.add)
+                nc.gpsimd.tensor_scalar(weights[r], strength[:], half_last[:, r - ON_SCALAR : r - ON_SCALAR + 1], 0.0, ALU.mult, ALU.add)
 
-        order_scales(rows[:, S : S + PASS], w1s_raw[:, 0:PASS])
-        order_scales(rows_rest[:], w1s_raw[:, PASS:H])
         nc.vector.tensor_copy(ts_picked[:], ts_raw[:].indirect(live[:]))
+        order_scales(nc.gpsimd, rows_rest[:], w1s_raw[:, PASS:H])
+        order_scales(nc.vector, rows[:, S : S + PASS], w1s_raw[:, 0:PASS])
         nc.vector.tensor_copy(rows[ROWS_AT:P, 0:S].bitcast(I32), ts_picked[ROWS_AT:P, :].bitcast(I32))
-        nc.scalar.mul(half_gain[:], gains, 0.5)
+        nc.scalar.mul(half_gain[:], gains[:, 0 : H_PASSES - 1, :], 0.5)
         deal_rows(scales, rows, nc.sync)
         w1_rest = staged([P, K_PASSES, (H - PASS) // 2], I32, "w1_rest", AT_W1_REST)
         nc.sync.dma_start(w1_rest[:], w1_i32[:, :, PASS // 2 : H // 2])
-        for r in range(unheld):
+        for t in range(0, PACK, 2):
+            order_w1(0, w1_first[:], nc.scalar.copy, "p a m t", t, t + 2)
+        for r in range(ON_SCALAR):
             weigh(r)
-        order_w1(0, w1_first[:], nc.scalar.copy, "p a m t")
         scales_rest = staged([P, K_PASSES, H - PASS], U8, "scales_rest", AT_SCALES_REST)
         nc.gpsimd.memset(scales_rest[:].rearrange("p a c -> p (a c)").bitcast(I32), 0)
         deal_rows(scales_rest, rows_rest, nc.sync)
-        nc.gpsimd.tensor_scalar(half_last[:], gains[:, H_PASSES - 1, unheld - SLICES + PACK : PACK], 0.5, 0.0, ALU.mult, ALU.add)
-        for r in range(unheld, SLICES):
+        for b in range(1, H_PASSES):
+            lo = max(ON_SCALAR, PACK * b)
+            nc.gpsimd.tensor_scalar(half_last[:, lo - ON_SCALAR : PACK * (b + 1) - ON_SCALAR], gains[:, b, lo - PACK * b : PACK], 0.5, 0.0, ALU.mult, ALU.add)
+        for r in range(ON_SCALAR, SLICES):
             weigh(r)
 
         def load_ws(b):
@@ -181,11 +182,15 @@ def tile_list_draft_tree_sketch_kernel(tc, tab_words, tab_scales, offs, w1_words
             entries = live[:, (BANK * j + lo) // LIST : (BANK * j + hi) // LIST]
             nc.vector.tensor_copy(v[a][j][:, lo:hi], tab[a][:].bitcast(U32).indirect(entries))
 
-        def project_part(r, j, lo, hi, bank):
+        sums = []
+
+        def project_part(r, j, lo, hi):
             b, t = divmod(r, PACK)
+            bank = len(sums) % H_BANKS
+            sums.append(bank)
             acc = psum.tile([P, hi - lo], F32, name="acc", tag="bank%d" % bank)
             cols = slice(BANK * j + lo, BANK * j + hi)
-            passes = list(range(K_PASSES)) if r == 0 or (r == 1 and j == 0) else list(reversed(range(K_PASSES)))
+            passes = list(range(K_PASSES)) if r == 0 else list(reversed(range(K_PASSES)))
             for a in passes:
                 nc.tensor.matmul_mx(
                     acc[:],
@@ -200,14 +205,14 @@ def tile_list_draft_tree_sketch_kernel(tc, tab_words, tab_scales, offs, w1_words
 
         def project(r):
             for j in range(2):
-                project_part(r, j, 0, BANK, r % 2 + 2 * j)
+                project_part(r, j, 0, BANK)
 
         gather_words(0, 0, 0, BANK)
         warm = psum.tile([P, BANK], F32, name="warm", tag="bank%d" % (BANKS - 1))
         for n in range(WARM_UPS):
             nc.tensor.matmul_mx(
                 warm[:],
-                lhsT=w1_first[:, 0, 0 : P // 2].bitcast(U8).bitcast(FP4X4),
+                lhsT=w1s_raw[:, 0 : 2 * P].bitcast(FP4X4),
                 lhsT_scale=w1s_raw[:, 0:P],
                 rhs=v[0][0][:].bitcast(FP8X4),
                 rhs_scale=w1s_raw[:, 0:BANK],
@@ -215,23 +220,21 @@ def tile_list_draft_tree_sketch_kernel(tc, tab_words, tab_scales, offs, w1_words
                 stop=True,
             )
         gather_words(0, 1, 0, BANK)
-        inv_raw = staged([P, H_PASSES, PACK], F32, "inv_raw", AT_INV)
-        nc.vector.reciprocal(inv_raw[:], gains)
         gather_words(1, 0, 0, BANK)
         gather_words(1, 1, 0, BANK // 2)
         gather_words(1, 1, BANK // 2, BANK)
+        inv_raw = staged([P, H_PASSES, PACK], F32, "inv_raw", AT_INV)
+        nc.vector.reciprocal(inv_raw[:], gains)
         load_ws(0)
         load_ws(1)
+        order_w1(1, w1_rest[:, :, 0 : PASS // 2], nc.vector.tensor_copy, "p a t m", 0, PACK)
         nc.vector.tensor_scalar(inv_gain[:], inv_raw[:], LARGEST, -LARGEST, ALU.min, ALU.max)
-        order_w1(1, w1_rest[:, :, 0 : PASS // 2], nc.vector.tensor_copy, "p a t m")
-        order_w1(2, w1_rest[:, :, PASS // 2 : PASS], nc.vector.tensor_copy, "p a t m")
+        order_w1(2, w1_rest[:, :, PASS // 2 : PASS], nc.vector.tensor_copy, "p a t m", 0, PACK)
         load_ws(2)
-        project_part(0, 0, 0, BANK, 0)
-        project_part(1, 0, 0, BANK, 1)
-        project_part(0, 1, 0, BANK // 2, 2)
-        project_part(0, 1, BANK // 2, BANK, H_BANKS)
-        project_part(1, 1, 0, BANK, 3)
-        for r in range(2, AHEAD):
+        project_part(0, 0, 0, BANK)
+        project_part(0, 1, 0, BANK // 2)
+        project_part(0, 1, BANK // 2, BANK)
+        for r in range(1, AHEAD):
             project(r)
 
         def weave_ws(b, i, copy):
@@ -292,7 +295,7 @@ def tile_list_draft_tree_sketch_kernel(tc, tab_words, tab_scales, offs, w1_words
             for n in tiles:
                 g, e = divmod(n, per_bank)
                 if b == 0 and e == 0:
-                    scores[part, g] = psum.tile([P, per_bank, w], F32, name="score", tag="bank%d" % ((H_BANKS + len(scores)) % BANKS))
+                    scores[part, g] = psum.tile([P, per_bank, w], F32, name="score", tag="bank%d" % (H_BANKS if not scores else (len(sums) + len(scores) - 1) % H_BANKS))
                 done = 0
                 for width in widths[part]:
                     lo = c - units[u][1] + done
@@ -318,7 +321,7 @@ def tile_list_draft_tree_sketch_kernel(tc, tab_words, tab_scales, offs, w1_words
         steps = [(u, t) for u in range(len(units)) for t in range(PACK)]
         last_projected = SLICES - 1 - AHEAD
         pieces = N // WS_PIECE
-        weave_steps = [WOVEN_ON + 1, WOVEN_ON + 2, 6, 9, 10, 11]
+        weave_steps = [WOVEN_ON + 1, WOVEN_ON + 2, 6, 9]
         score_steps = [last_projected, 3 * PACK - 1]
         last_pass, last_unit = H_PASSES - 1, len(units) - 1
         for s, (u, t) in enumerate(steps[:-PACK]):
@@ -344,25 +347,23 @@ def tile_list_draft_tree_sketch_kernel(tc, tab_words, tab_scales, offs, w1_words
                     score(part, score_steps.index(s), range(N // P))
 
         tiles = N // P
+        for i in range(pieces):
+            weave_ws(last_pass, i, nc.scalar.copy)
         weave_z(last_unit - 1, 0, EARLY)
-        pick(last_unit, 0)
         quantize_z(last_unit - 1, 0, EARLY)
+        quantize_ws(last_pass, 0)
         score(0, last_pass, range(tiles // 2))
-        gate(last_unit, 0)
-        pick(last_unit, 1)
-        gate(last_unit, 1)
-        quantize_ws(last_pass, pieces - 1)
-        score(0, last_pass, range(tiles // 2, tiles))
-        for t in range(2, PACK):
+        for t in range(PACK):
             pick(last_unit, t)
             gate(last_unit, t)
-        for g in range(tiles // 2):
-            store(0, g, nc.scalar.copy)
+            if t == 0:
+                store(0, 0, nc.scalar.copy)
+        quantize_ws(last_pass, 1)
+        score(0, last_pass, range(tiles // 2, tiles))
         weave_z(last_unit, 0, LATE)
-        store(0, tiles // 2, nc.vector.tensor_copy)
         quantize_z(last_unit, 0, LATE)
         score(1, last_pass, range(tiles))
-        store(0, tiles - 2, nc.vector.tensor_copy)
-        store(0, tiles - 1, nc.scalar.copy)
+        for g in range(1, tiles):
+            store(0, g, nc.vector.tensor_copy if g == tiles - 2 else nc.scalar.copy)
         store(1, 0, nc.vector.tensor_copy)
         store(1, 1, nc.scalar.copy)

@@ -43,7 +43,7 @@ WS_BYTES = PACK * N * 4
 TAB_BYTES = 4 * T
 W1P_BYTES = 2 * K_PASSES * PASS
 WEIGHT_BYTES = 4 * SLOTS
-ON_SCALAR = 7
+ON_SCALAR = 9
 EDGE = 512
 AT_TAB = (0, TAB_BYTES)
 AT_INV = WS_BYTES + 64
@@ -102,7 +102,7 @@ def tile_list_draft_tree_sketch_kernel(tc, tab_words, tab_scales, offs, w1_words
         gains = gains_pad[:, :, 0:PACK]
         bias = bias_pad[:, :, 0:PACK]
         strength = tile([P, SLOTS], F32, "strength")
-        half_gain = tile([P, H_PASSES - 1, PACK], F32, "half_gain")
+        half_gain = tile([P, H_PASSES, PACK], F32, "half_gain")
         inv_gain = tile([P, H_PASSES, PACK], F32, "inv_gain")
         weights = [staged([P, SLOTS], F32, "weights%d" % r, AT_WEIGHTS + WEIGHT_BYTES * r)[:] for r in range(SLICES)]
 
@@ -157,7 +157,7 @@ def tile_list_draft_tree_sketch_kernel(tc, tab_words, tab_scales, offs, w1_words
         order_scales(nc.gpsimd, rows_rest[:], w1s_raw[:, PASS:H])
         order_scales(nc.vector, rows[:, S : S + PASS], w1s_raw[:, 0:PASS])
         nc.vector.tensor_copy(rows[ROWS_AT:P, 0:S].bitcast(I32), ts_picked[ROWS_AT:P, :].bitcast(I32))
-        nc.scalar.mul(half_gain[:], gains[:, 0 : H_PASSES - 1, :], 0.5)
+        nc.scalar.mul(half_gain[:], gains, 0.5)
         deal_rows(scales, rows, nc.sync)
         w1_rest = staged([P, K_PASSES, (H - PASS) // 2], I32, "w1_rest", AT_W1_REST)
         nc.sync.dma_start(w1_rest[:], w1_i32[:, :, PASS // 2 : H // 2])
@@ -168,9 +168,7 @@ def tile_list_draft_tree_sketch_kernel(tc, tab_words, tab_scales, offs, w1_words
         scales_rest = staged([P, K_PASSES, H - PASS], U8, "scales_rest", AT_SCALES_REST)
         nc.gpsimd.memset(scales_rest[:].rearrange("p a c -> p (a c)").bitcast(I32), 0)
         deal_rows(scales_rest, rows_rest, nc.sync)
-        for b in range(1, H_PASSES):
-            lo = max(ON_SCALAR, PACK * b)
-            nc.gpsimd.tensor_scalar(half_last[:, lo - ON_SCALAR : PACK * (b + 1) - ON_SCALAR], gains[:, b, lo - PACK * b : PACK], 0.5, 0.0, ALU.mult, ALU.add)
+        nc.gpsimd.tensor_scalar(half_last[:], gains[:, H_PASSES - 1, ON_SCALAR - SLICES + PACK : PACK], 0.5, 0.0, ALU.mult, ALU.add)
         for r in range(ON_SCALAR, SLICES):
             weigh(r)
 

@@ -34,7 +34,7 @@ QUADRANT = 32
 SCALE_ROWS = 4
 ROWS_AT = P - K_PASSES * 16
 PADDED = 8
-WS_PIECE = 384
+WS_PIECES = ((512, 256), (384, 384), (384, 384))
 WARM_UPS = 4
 AHEAD = 3
 LARGEST = 3.0e38
@@ -43,7 +43,7 @@ WS_BYTES = PACK * N * 4
 TAB_BYTES = 4 * T
 W1P_BYTES = 2 * K_PASSES * PASS
 WEIGHT_BYTES = 4 * SLOTS
-ON_SCALAR = 9
+ON_SCALAR = 8
 EDGE = 512
 AT_TAB = (0, TAB_BYTES)
 AT_INV = WS_BYTES + 64
@@ -64,7 +64,9 @@ AT_UNITS = AT_WS0 + WS_BYTES
 STAGGER = 1
 UNIT_BYTES = PACK * SLOTS * 4 + 128
 AT_RES = AT_UNITS + 2 * UNIT_BYTES
-WOVEN_ON = 2
+AT_H = AT_UNITS + 4 * UNIT_BYTES
+H_BYTES = 4 * S
+WOVEN_ON = 3
 
 
 def tile_list_draft_tree_sketch_kernel(tc, tab_words, tab_scales, offs, w1_words, w1_scales, b1, offs2, wgt, gain, ws, out):
@@ -95,14 +97,14 @@ def tile_list_draft_tree_sketch_kernel(tc, tab_words, tab_scales, offs, w1_words
         ws_raw = {}
         ws_bf = {}
         ws_q = [tile([P, N], U32, "ws_q%d" % b) for b in range(H_PASSES)]
-        ws_s = [tile([P, N], U8, "ws_s%d" % b) for b in range(H_PASSES)]
-        h = [tile([P, S], F32, "h%d" % r) for r in range(SLICES)]
+        ws_s = {}
+        h = [staged([P, S], F32, "h%d" % r, AT_H + H_BYTES * r) for r in range(SLICES)]
         gains_pad = tile([P, H_PASSES, PADDED], F32, "gains")
         bias_pad = tile([P, H_PASSES, PADDED], F32, "bias")
         gains = gains_pad[:, :, 0:PACK]
         bias = bias_pad[:, :, 0:PACK]
         strength = tile([P, SLOTS], F32, "strength")
-        half_gain = tile([P, H_PASSES, PACK], F32, "half_gain")
+        half_gain = tile([P, H_PASSES - 1, PACK], F32, "half_gain")
         inv_gain = tile([P, H_PASSES, PACK], F32, "inv_gain")
         weights = [staged([P, SLOTS], F32, "weights%d" % r, AT_WEIGHTS + WEIGHT_BYTES * r)[:] for r in range(SLICES)]
 
@@ -157,7 +159,7 @@ def tile_list_draft_tree_sketch_kernel(tc, tab_words, tab_scales, offs, w1_words
         order_scales(nc.gpsimd, rows_rest[:], w1s_raw[:, PASS:H])
         order_scales(nc.vector, rows[:, S : S + PASS], w1s_raw[:, 0:PASS])
         nc.vector.tensor_copy(rows[ROWS_AT:P, 0:S].bitcast(I32), ts_picked[ROWS_AT:P, :].bitcast(I32))
-        nc.scalar.mul(half_gain[:], gains, 0.5)
+        nc.scalar.mul(half_gain[:], gains[:, 0 : H_PASSES - 1, :], 0.5)
         deal_rows(scales, rows, nc.sync)
         w1_rest = staged([P, K_PASSES, (H - PASS) // 2], I32, "w1_rest", AT_W1_REST)
         nc.sync.dma_start(w1_rest[:], w1_i32[:, :, PASS // 2 : H // 2])
@@ -236,18 +238,23 @@ def tile_list_draft_tree_sketch_kernel(tc, tab_words, tab_scales, offs, w1_words
             project(r)
 
         def weave_ws(b, i, copy):
-            cols = slice(WS_PIECE * i, WS_PIECE * (i + 1))
-            if b == 0:
-                ws_bf[b, i] = staged([P, WS_PIECE, PACK], BF16, "ws_bf0_%d" % i, AT_WEIGHTS + 4 * SLOTS * WOVEN_ON + 2 * PACK * WS_PIECE * i)
+            width = WS_PIECES[b][i]
+            cols = slice(WS_PIECES[b][0] * i, WS_PIECES[b][0] * i + width)
+            if (b, i) == (0, 0):
+                ws_bf[b, i] = staged([P, width, PACK], BF16, "ws_bf0_0", AT_H + H_BYTES * WOVEN_ON)
             else:
-                ws_bf[b, i] = tile([P, WS_PIECE, PACK], BF16, "ws_bf%d_%d" % (b, i))
+                ws_bf[b, i] = tile([P, width, PACK], BF16, "ws_bf%d_%d" % (b, i))
             copy(
                 ws_bf[b, i][:].rearrange("p (c i) t -> p c t i", i=RUN),
                 ws_raw[b][:, :, cols].rearrange("p t (c i) -> p c t i", i=RUN),
             )
 
         def quantize_ws(b, i):
-            cols = slice(WS_PIECE * i, WS_PIECE * (i + 1))
+            cols = slice(WS_PIECES[b][0] * i, WS_PIECES[b][0] * i + WS_PIECES[b][i])
+            if (b, i) == (0, 0):
+                ws_s[b] = staged([P, N], U8, "ws_s0", AT_WEIGHTS + WEIGHT_BYTES * (WOVEN_ON + 1))
+            elif i == 0:
+                ws_s[b] = tile([P, N], U8, "ws_s%d" % b)
             nc.vector.quantize_mx(ws_q[b][:, cols].bitcast(FP8X4), ws_s[b][:, cols], ws_bf[b, i][:].rearrange("p n t -> p (n t)"))
 
         units = [(0, 0, SLOTS), (1, 0, SLOTS), (2, 0, EARLY), (2, EARLY, LATE)]
@@ -318,8 +325,8 @@ def tile_list_draft_tree_sketch_kernel(tc, tab_words, tab_scales, offs, w1_words
 
         steps = [(u, t) for u in range(len(units)) for t in range(PACK)]
         last_projected = SLICES - 1 - AHEAD
-        pieces = N // WS_PIECE
-        weave_steps = [WOVEN_ON + 1, WOVEN_ON + 2, 6, 9]
+        pieces = len(WS_PIECES[0])
+        weave_steps = [WOVEN_ON, 5, 6, 9]
         score_steps = [last_projected, 3 * PACK - 1]
         last_pass, last_unit = H_PASSES - 1, len(units) - 1
         for s, (u, t) in enumerate(steps[:-PACK]):
@@ -332,7 +339,7 @@ def tile_list_draft_tree_sketch_kernel(tc, tab_words, tab_scales, offs, w1_words
                 gate(u, t)
             if s in weave_steps:
                 b, i = divmod(weave_steps.index(s), pieces)
-                weave_ws(b, i, nc.vector.tensor_copy if b == 0 else nc.scalar.copy)
+                weave_ws(b, i, nc.vector.tensor_copy if (b, i) == (0, 0) else nc.scalar.copy)
             if u > 0 and t == 1:
                 for lo in (0, HALF):
                     weave_z(u - 1, lo, lo + HALF)
@@ -348,11 +355,12 @@ def tile_list_draft_tree_sketch_kernel(tc, tab_words, tab_scales, offs, w1_words
         for i in range(pieces):
             weave_ws(last_pass, i, nc.scalar.copy)
         weave_z(last_unit - 1, 0, EARLY)
-        quantize_z(last_unit - 1, 0, EARLY)
-        quantize_ws(last_pass, 0)
-        score(0, last_pass, range(tiles // 2))
         for t in range(PACK):
             pick(last_unit, t)
+            if t == 0:
+                quantize_z(last_unit - 1, 0, EARLY)
+                quantize_ws(last_pass, 0)
+                score(0, last_pass, range(tiles // 2))
             gate(last_unit, t)
             if t == 0:
                 store(0, 0, nc.scalar.copy)

@@ -34,7 +34,7 @@ QUADRANT = 32
 SCALE_ROWS = 4
 ROWS_AT = P - K_PASSES * 16
 PADDED = 8
-WS_PIECES = ((512, 256), (384, 384), (384, 384))
+WS_PIECE = 384
 WARM_UPS = 4
 AHEAD = 3
 LARGEST = 3.0e38
@@ -48,15 +48,15 @@ EDGE = 512
 AT_TAB = (0, TAB_BYTES)
 AT_INV = WS_BYTES + 64
 AT_WS1 = 0
-AT_ROWS_REST = 2 * TAB_BYTES
-AT_WS2 = AT_ROWS_REST
-AT_TS_RAW = AT_WS2 + WS_BYTES
+AT_TS_RAW = 2 * TAB_BYTES
 AT_W1_FIRST = AT_TS_RAW + T
 AT_W1_REST = AT_W1_FIRST + W1P_BYTES
-AT_HALF_LAST = AT_W1_REST + 2 * W1P_BYTES
-AT_TS_PICKED = AT_HALF_LAST - EDGE
-AT_SCALES_REST = AT_HALF_LAST + 64
-AT_WEIGHTS = AT_SCALES_REST + K_PASSES * (H - PASS)
+AT_ROWS_REST = AT_W1_REST + 2 * W1P_BYTES
+AT_TS_PICKED = AT_ROWS_REST - EDGE
+AT_HALF_LAST = AT_ROWS_REST + H - PASS
+AT_HALF_ONE = AT_HALF_LAST - 64
+AT_WS2 = AT_ROWS_REST
+AT_WEIGHTS = AT_WS2 + WS_BYTES
 AT_ROWS = AT_WEIGHTS + SLICES * WEIGHT_BYTES
 AT_WS0 = AT_ROWS
 AT_WS = (AT_WS0, AT_WS1, AT_WS2)
@@ -89,8 +89,10 @@ def tile_list_draft_tree_sketch_kernel(tc, tab_words, tab_scales, offs, w1_words
         ts_picked = staged([P, S], U8, "ts_picked", AT_TS_PICKED)
         rows = staged([P, S + PASS], U8, "rows", AT_ROWS)
         scales = tile([P, K_PASSES, S + PASS], U8, "scales")
+        scales_rest = tile([P, K_PASSES, H - PASS], U8, "scales_rest")
+        half_one = staged([P, 32], F32, "half_one", AT_HALF_ONE)
         rows_rest = staged([P, H - PASS], U8, "rows_rest", AT_ROWS_REST)
-        half_last = staged([P, SLICES - ON_SCALAR], F32, "half_last", AT_HALF_LAST)
+        half_last = staged([P, SLICES - ON_SCALAR - 1], F32, "half_last", AT_HALF_LAST)
         w1p = {}
         tab = [staged([P, T], I32, "tab%d" % a, AT_TAB[a]) for a in range(K_PASSES)]
         v = [[tile([P, BANK], U32, "v%d_%d" % (a, j)) for j in range(2)] for a in range(K_PASSES)]
@@ -111,6 +113,7 @@ def tile_list_draft_tree_sketch_kernel(tc, tab_words, tab_scales, offs, w1_words
         nc.vector.memset(ts_raw[0:ROWS_AT, :].bitcast(I32), 0)
         nc.vector.memset(w1s_raw[0:ROWS_AT, :].bitcast(I32), 0)
         nc.vector.memset(scales[:].rearrange("p a c -> p (a c)").bitcast(I32), 0)
+        nc.vector.memset(scales_rest[:].rearrange("p a c -> p (a c)").bitcast(I32), 0)
 
         w1_i32 = w1_words.bitcast(I32).rearrange("a p c -> p a c")
 
@@ -129,8 +132,8 @@ def tile_list_draft_tree_sketch_kernel(tc, tab_words, tab_scales, offs, w1_words
         nc.sync.dma_start(picks[:], offs2)
         nc.scalar.dma_start(bias, b1.rearrange("(b p t) -> p b t", p=P, t=PACK))
 
-        def order_scales(engine, dst, src):
-            engine.tensor_copy(dst.rearrange("p (b t m) -> p t b m", t=PACK, m=P), src.rearrange("p (b m t) -> p t b m", t=PACK, m=P))
+        def order_scales(dst, src):
+            nc.gpsimd.tensor_copy(dst.rearrange("p (b t m) -> p t b m", t=PACK, m=P), src.rearrange("p (b m t) -> p t b m", t=PACK, m=P))
 
         def deal_rows(dst, src, queue):
             per_quadrant = K_PASSES * SCALE_ROWS
@@ -152,14 +155,17 @@ def tile_list_draft_tree_sketch_kernel(tc, tab_words, tab_scales, offs, w1_words
             b, t = divmod(r, PACK)
             if r < ON_SCALAR:
                 nc.scalar.activation(weights[r], strength[:], ACT.Identity, scale=half_gain[:, b, t : t + 1])
+            elif r == ON_SCALAR:
+                nc.vector.tensor_scalar(weights[r], strength[:], half_one[:, 0:1], None, ALU.mult)
             else:
-                nc.gpsimd.tensor_scalar(weights[r], strength[:], half_last[:, r - ON_SCALAR : r - ON_SCALAR + 1], 0.0, ALU.mult, ALU.add)
+                nc.gpsimd.tensor_scalar(weights[r], strength[:], half_last[:, r - ON_SCALAR - 1 : r - ON_SCALAR], 0.0, ALU.mult, ALU.add)
 
         nc.vector.tensor_copy(ts_picked[:], ts_raw[:].indirect(live[:]))
-        order_scales(nc.gpsimd, rows_rest[:], w1s_raw[:, PASS:H])
-        order_scales(nc.vector, rows[:, S : S + PASS], w1s_raw[:, 0:PASS])
+        order_scales(rows[:, S : S + PASS], w1s_raw[:, 0:PASS])
         nc.vector.tensor_copy(rows[ROWS_AT:P, 0:S].bitcast(I32), ts_picked[ROWS_AT:P, :].bitcast(I32))
         nc.scalar.mul(half_gain[:], gains[:, 0 : H_PASSES - 1, :], 0.5)
+        nc.scalar.mul(half_one[:, 0:1], gains[:, H_PASSES - 1, 0:1], 0.5)
+        weigh(ON_SCALAR)
         deal_rows(scales, rows, nc.sync)
         w1_rest = staged([P, K_PASSES, (H - PASS) // 2], I32, "w1_rest", AT_W1_REST)
         nc.sync.dma_start(w1_rest[:], w1_i32[:, :, PASS // 2 : H // 2])
@@ -167,11 +173,10 @@ def tile_list_draft_tree_sketch_kernel(tc, tab_words, tab_scales, offs, w1_words
             order_w1(0, w1_first[:], nc.scalar.copy, "p a m t", t, t + 2)
         for r in range(ON_SCALAR):
             weigh(r)
-        scales_rest = staged([P, K_PASSES, H - PASS], U8, "scales_rest", AT_SCALES_REST)
-        nc.gpsimd.memset(scales_rest[:].rearrange("p a c -> p (a c)").bitcast(I32), 0)
+        order_scales(rows_rest[:], w1s_raw[:, PASS:H])
         deal_rows(scales_rest, rows_rest, nc.sync)
-        nc.gpsimd.tensor_scalar(half_last[:], gains[:, H_PASSES - 1, ON_SCALAR - SLICES + PACK : PACK], 0.5, 0.0, ALU.mult, ALU.add)
-        for r in range(ON_SCALAR, SLICES):
+        nc.gpsimd.tensor_scalar(half_last[:], gains[:, H_PASSES - 1, 1:PACK], 0.5, 0.0, ALU.mult, ALU.add)
+        for r in range(ON_SCALAR + 1, SLICES):
             weigh(r)
 
         def load_ws(b):
@@ -238,19 +243,18 @@ def tile_list_draft_tree_sketch_kernel(tc, tab_words, tab_scales, offs, w1_words
             project(r)
 
         def weave_ws(b, i, copy):
-            width = WS_PIECES[b][i]
-            cols = slice(WS_PIECES[b][0] * i, WS_PIECES[b][0] * i + width)
-            if (b, i) == (0, 0):
-                ws_bf[b, i] = staged([P, width, PACK], BF16, "ws_bf0_0", AT_H + H_BYTES * WOVEN_ON)
+            cols = slice(WS_PIECE * i, WS_PIECE * (i + 1))
+            if b == 0:
+                ws_bf[b, i] = staged([P, WS_PIECE, PACK], BF16, "ws_bf0_%d" % i, AT_H + H_BYTES * (WOVEN_ON + i))
             else:
-                ws_bf[b, i] = tile([P, width, PACK], BF16, "ws_bf%d_%d" % (b, i))
+                ws_bf[b, i] = tile([P, WS_PIECE, PACK], BF16, "ws_bf%d_%d" % (b, i))
             copy(
                 ws_bf[b, i][:].rearrange("p (c i) t -> p c t i", i=RUN),
                 ws_raw[b][:, :, cols].rearrange("p t (c i) -> p c t i", i=RUN),
             )
 
         def quantize_ws(b, i):
-            cols = slice(WS_PIECES[b][0] * i, WS_PIECES[b][0] * i + WS_PIECES[b][i])
+            cols = slice(WS_PIECE * i, WS_PIECE * (i + 1))
             if (b, i) == (0, 0):
                 ws_s[b] = staged([P, N], U8, "ws_s0", AT_WEIGHTS + WEIGHT_BYTES * (WOVEN_ON + 1))
             elif i == 0:
@@ -325,8 +329,8 @@ def tile_list_draft_tree_sketch_kernel(tc, tab_words, tab_scales, offs, w1_words
 
         steps = [(u, t) for u in range(len(units)) for t in range(PACK)]
         last_projected = SLICES - 1 - AHEAD
-        pieces = len(WS_PIECES[0])
-        weave_steps = [WOVEN_ON, 5, 6, 9]
+        pieces = N // WS_PIECE
+        weave_steps = [WOVEN_ON, WOVEN_ON + 1, 6, 9]
         score_steps = [last_projected, 3 * PACK - 1]
         last_pass, last_unit = H_PASSES - 1, len(units) - 1
         for s, (u, t) in enumerate(steps[:-PACK]):
@@ -339,7 +343,7 @@ def tile_list_draft_tree_sketch_kernel(tc, tab_words, tab_scales, offs, w1_words
                 gate(u, t)
             if s in weave_steps:
                 b, i = divmod(weave_steps.index(s), pieces)
-                weave_ws(b, i, nc.vector.tensor_copy if (b, i) == (0, 0) else nc.scalar.copy)
+                weave_ws(b, i, nc.vector.tensor_copy if b == 0 else nc.scalar.copy)
             if u > 0 and t == 1:
                 for lo in (0, HALF):
                     weave_z(u - 1, lo, lo + HALF)

@@ -43,7 +43,7 @@ WS_BYTES = PACK * N * 4
 TAB_BYTES = 4 * T
 W1P_BYTES = 2 * K_PASSES * PASS
 WEIGHT_BYTES = 4 * SLOTS
-ON_SCALAR = 8
+ON_SCALAR = 9
 EDGE = 512
 AT_TAB = (0, TAB_BYTES)
 AT_INV = WS_BYTES + 64
@@ -51,10 +51,9 @@ AT_WS1 = 0
 AT_TS_RAW = 2 * TAB_BYTES
 AT_W1_FIRST = AT_TS_RAW + T
 AT_W1_REST = AT_W1_FIRST + W1P_BYTES
-AT_ROWS_REST = AT_W1_REST + 2 * W1P_BYTES
-AT_TS_PICKED = AT_ROWS_REST - EDGE
-AT_HALF_LAST = AT_ROWS_REST + H - PASS
-AT_HALF_ONE = AT_HALF_LAST - 64
+AT_HALF_LAST = AT_W1_REST + 2 * W1P_BYTES
+AT_TS_PICKED = AT_HALF_LAST - EDGE
+AT_ROWS_REST = AT_HALF_LAST + 64
 AT_WS2 = AT_ROWS_REST
 AT_WEIGHTS = AT_WS2 + WS_BYTES
 AT_ROWS = AT_WEIGHTS + SLICES * WEIGHT_BYTES
@@ -90,9 +89,8 @@ def tile_list_draft_tree_sketch_kernel(tc, tab_words, tab_scales, offs, w1_words
         rows = staged([P, S + PASS], U8, "rows", AT_ROWS)
         scales = tile([P, K_PASSES, S + PASS], U8, "scales")
         scales_rest = tile([P, K_PASSES, H - PASS], U8, "scales_rest")
-        half_one = staged([P, 32], F32, "half_one", AT_HALF_ONE)
         rows_rest = staged([P, H - PASS], U8, "rows_rest", AT_ROWS_REST)
-        half_last = staged([P, SLICES - ON_SCALAR - 1], F32, "half_last", AT_HALF_LAST)
+        half_last = staged([P, SLICES - ON_SCALAR], F32, "half_last", AT_HALF_LAST)
         w1p = {}
         tab = [staged([P, T], I32, "tab%d" % a, AT_TAB[a]) for a in range(K_PASSES)]
         v = [[tile([P, BANK], U32, "v%d_%d" % (a, j)) for j in range(2)] for a in range(K_PASSES)]
@@ -106,7 +104,7 @@ def tile_list_draft_tree_sketch_kernel(tc, tab_words, tab_scales, offs, w1_words
         gains = gains_pad[:, :, 0:PACK]
         bias = bias_pad[:, :, 0:PACK]
         strength = tile([P, SLOTS], F32, "strength")
-        half_gain = tile([P, H_PASSES - 1, PACK], F32, "half_gain")
+        half_gain = tile([P, H_PASSES, PACK], F32, "half_gain")
         inv_gain = tile([P, H_PASSES, PACK], F32, "inv_gain")
         weights = [staged([P, SLOTS], F32, "weights%d" % r, AT_WEIGHTS + WEIGHT_BYTES * r)[:] for r in range(SLICES)]
 
@@ -124,13 +122,13 @@ def tile_list_draft_tree_sketch_kernel(tc, tab_words, tab_scales, offs, w1_words
         nc.sync.dma_start(live[:], offs)
         load_scale_rows(ts_raw, tab_scales)
         load_scale_rows(w1s_raw, w1_scales)
-        nc.scalar.dma_start(gains, gain.rearrange("(b p t) -> p b t", p=P, t=PACK))
+        nc.sync.dma_start(gains, gain.rearrange("(b p t) -> p b t", p=P, t=PACK))
         nc.sync.dma_start(strength[:], wgt)
         for a in range(K_PASSES):
             nc.sync.dma_start(tab[a][:], tab_words[a].rearrange("p t i -> p (t i)").bitcast(I32))
         nc.sync.dma_start(w1_first[:], w1_i32[:, :, 0 : PASS // 2])
+        nc.sync.dma_start(bias, b1.rearrange("(b p t) -> p b t", p=P, t=PACK))
         nc.sync.dma_start(picks[:], offs2)
-        nc.scalar.dma_start(bias, b1.rearrange("(b p t) -> p b t", p=P, t=PACK))
 
         def order_scales(dst, src):
             nc.gpsimd.tensor_copy(dst.rearrange("p (b t m) -> p t b m", t=PACK, m=P), src.rearrange("p (b m t) -> p t b m", t=PACK, m=P))
@@ -143,40 +141,36 @@ def tile_list_draft_tree_sketch_kernel(tc, tab_words, tab_scales, offs, w1_words
                     src[ROWS_AT + per_quadrant * q : ROWS_AT + per_quadrant * (q + 1), :].bitcast(I32),
                 )
 
-        def order_w1(b, src, copy, walk, lo, hi):
+        def order_w1(b, src, copy, lo, hi):
             if lo == 0:
                 w1p[b] = tile([P, K_PASSES, PASS * 2], U8, "w1p%d" % b)
             copy(
-                w1p[b][:].bitcast(U16).rearrange("p a (t m) -> p a t m", t=PACK)[:, :, lo:hi, :].rearrange("p a t m -> " + walk),
-                src.bitcast(U16).rearrange("p a (m t) -> p a t m", t=PACK)[:, :, lo:hi, :].rearrange("p a t m -> " + walk),
+                w1p[b][:].bitcast(U16).rearrange("p a (t m) -> p a t m", t=PACK)[:, :, lo:hi, :],
+                src.bitcast(U16).rearrange("p a (m t) -> p a t m", t=PACK)[:, :, lo:hi, :],
             )
 
         def weigh(r):
             b, t = divmod(r, PACK)
             if r < ON_SCALAR:
                 nc.scalar.activation(weights[r], strength[:], ACT.Identity, scale=half_gain[:, b, t : t + 1])
-            elif r == ON_SCALAR:
-                nc.vector.tensor_scalar(weights[r], strength[:], half_one[:, 0:1], None, ALU.mult)
             else:
-                nc.gpsimd.tensor_scalar(weights[r], strength[:], half_last[:, r - ON_SCALAR - 1 : r - ON_SCALAR], 0.0, ALU.mult, ALU.add)
+                nc.gpsimd.tensor_scalar(weights[r], strength[:], half_last[:, r - ON_SCALAR : r - ON_SCALAR + 1], 0.0, ALU.mult, ALU.add)
 
         nc.vector.tensor_copy(ts_picked[:], ts_raw[:].indirect(live[:]))
         order_scales(rows[:, S : S + PASS], w1s_raw[:, 0:PASS])
         nc.vector.tensor_copy(rows[ROWS_AT:P, 0:S].bitcast(I32), ts_picked[ROWS_AT:P, :].bitcast(I32))
-        nc.scalar.mul(half_gain[:], gains[:, 0 : H_PASSES - 1, :], 0.5)
-        nc.scalar.mul(half_one[:, 0:1], gains[:, H_PASSES - 1, 0:1], 0.5)
-        weigh(ON_SCALAR)
+        nc.scalar.mul(half_gain[:], gains, 0.5)
         deal_rows(scales, rows, nc.sync)
         w1_rest = staged([P, K_PASSES, (H - PASS) // 2], I32, "w1_rest", AT_W1_REST)
         nc.sync.dma_start(w1_rest[:], w1_i32[:, :, PASS // 2 : H // 2])
         for t in range(0, PACK, 2):
-            order_w1(0, w1_first[:], nc.scalar.copy, "p a m t", t, t + 2)
+            order_w1(0, w1_first[:], nc.scalar.copy, t, t + 2)
         for r in range(ON_SCALAR):
             weigh(r)
         order_scales(rows_rest[:], w1s_raw[:, PASS:H])
         deal_rows(scales_rest, rows_rest, nc.sync)
-        nc.gpsimd.tensor_scalar(half_last[:], gains[:, H_PASSES - 1, 1:PACK], 0.5, 0.0, ALU.mult, ALU.add)
-        for r in range(ON_SCALAR + 1, SLICES):
+        nc.gpsimd.tensor_scalar(half_last[:], gains[:, H_PASSES - 1, ON_SCALAR - SLICES + PACK : PACK], 0.5, 0.0, ALU.mult, ALU.add)
+        for r in range(ON_SCALAR, SLICES):
             weigh(r)
 
         def load_ws(b):
@@ -232,9 +226,9 @@ def tile_list_draft_tree_sketch_kernel(tc, tab_words, tab_scales, offs, w1_words
         nc.vector.reciprocal(inv_raw[:], gains)
         load_ws(0)
         load_ws(1)
-        order_w1(1, w1_rest[:, :, 0 : PASS // 2], nc.vector.tensor_copy, "p a t m", 0, PACK)
+        order_w1(1, w1_rest[:, :, 0 : PASS // 2], nc.vector.tensor_copy, 0, PACK)
         nc.vector.tensor_scalar(inv_gain[:], inv_raw[:], LARGEST, -LARGEST, ALU.min, ALU.max)
-        order_w1(2, w1_rest[:, :, PASS // 2 : PASS], nc.vector.tensor_copy, "p a t m", 0, PACK)
+        order_w1(2, w1_rest[:, :, PASS // 2 : PASS], nc.vector.tensor_copy, 0, PACK)
         load_ws(2)
         project_part(0, 0, 0, BANK)
         project_part(0, 1, 0, BANK // 2)

@@ -43,7 +43,7 @@ WS_BYTES = PACK * N * 4
 TAB_BYTES = 4 * T
 W1P_BYTES = 2 * K_PASSES * PASS
 WEIGHT_BYTES = 4 * SLOTS
-ON_SCALAR = 9
+ON_SCALAR = 8
 EDGE = 512
 AT_TAB = (0, TAB_BYTES)
 AT_INV = WS_BYTES + 64
@@ -51,9 +51,10 @@ AT_WS1 = 0
 AT_TS_RAW = 2 * TAB_BYTES
 AT_W1_FIRST = AT_TS_RAW + T
 AT_W1_REST = AT_W1_FIRST + W1P_BYTES
-AT_HALF_LAST = AT_W1_REST + 2 * W1P_BYTES
-AT_TS_PICKED = AT_HALF_LAST - EDGE
-AT_ROWS_REST = AT_HALF_LAST + 64
+AT_ROWS_REST = AT_W1_REST + 2 * W1P_BYTES
+AT_TS_PICKED = AT_ROWS_REST - EDGE
+AT_HALF_LAST = AT_ROWS_REST + H - PASS
+AT_HALF_ONE = AT_HALF_LAST - 64
 AT_WS2 = AT_ROWS_REST
 AT_WEIGHTS = AT_WS2 + WS_BYTES
 AT_ROWS = AT_WEIGHTS + SLICES * WEIGHT_BYTES
@@ -89,8 +90,9 @@ def tile_list_draft_tree_sketch_kernel(tc, tab_words, tab_scales, offs, w1_words
         rows = staged([P, S + PASS], U8, "rows", AT_ROWS)
         scales = tile([P, K_PASSES, S + PASS], U8, "scales")
         scales_rest = tile([P, K_PASSES, H - PASS], U8, "scales_rest")
+        half_one = staged([P, 32], F32, "half_one", AT_HALF_ONE)
         rows_rest = staged([P, H - PASS], U8, "rows_rest", AT_ROWS_REST)
-        half_last = staged([P, SLICES - ON_SCALAR], F32, "half_last", AT_HALF_LAST)
+        half_last = staged([P, SLICES - ON_SCALAR - 1], F32, "half_last", AT_HALF_LAST)
         w1p = {}
         tab = [staged([P, T], I32, "tab%d" % a, AT_TAB[a]) for a in range(K_PASSES)]
         v = [[tile([P, BANK], U32, "v%d_%d" % (a, j)) for j in range(2)] for a in range(K_PASSES)]
@@ -104,7 +106,7 @@ def tile_list_draft_tree_sketch_kernel(tc, tab_words, tab_scales, offs, w1_words
         gains = gains_pad[:, :, 0:PACK]
         bias = bias_pad[:, :, 0:PACK]
         strength = tile([P, SLOTS], F32, "strength")
-        half_gain = tile([P, H_PASSES, PACK], F32, "half_gain")
+        half_gain = tile([P, H_PASSES - 1, PACK], F32, "half_gain")
         inv_gain = tile([P, H_PASSES, PACK], F32, "inv_gain")
         weights = [staged([P, SLOTS], F32, "weights%d" % r, AT_WEIGHTS + WEIGHT_BYTES * r)[:] for r in range(SLICES)]
 
@@ -141,11 +143,13 @@ def tile_list_draft_tree_sketch_kernel(tc, tab_words, tab_scales, offs, w1_words
                     src[ROWS_AT + per_quadrant * q : ROWS_AT + per_quadrant * (q + 1), :].bitcast(I32),
                 )
 
-        def order_w1(b, src, copy, lo, hi):
-            if lo == 0:
-                w1p[b] = tile([P, K_PASSES, PASS * 2], U8, "w1p%d" % b)
+        def order_w1(b, src, copy, lo, hi, at=None):
+            shape, name = [P, K_PASSES, 2 * P * (hi - lo)], "w1p%d_%d" % (b, lo)
+            ordered = tile(shape, U8, name) if at is None else staged(shape, U8, name, at)
+            for t in range(lo, hi):
+                w1p[PACK * b + t] = ordered[:, :, 2 * P * (t - lo) : 2 * P * (t - lo + 1)]
             copy(
-                w1p[b][:].bitcast(U16).rearrange("p a (t m) -> p a t m", t=PACK)[:, :, lo:hi, :],
+                ordered[:].bitcast(U16).rearrange("p a (t m) -> p a t m", m=P),
                 src.bitcast(U16).rearrange("p a (m t) -> p a t m", t=PACK)[:, :, lo:hi, :],
             )
 
@@ -154,12 +158,15 @@ def tile_list_draft_tree_sketch_kernel(tc, tab_words, tab_scales, offs, w1_words
             if r < ON_SCALAR:
                 nc.scalar.activation(weights[r], strength[:], ACT.Identity, scale=half_gain[:, b, t : t + 1])
             else:
-                nc.gpsimd.tensor_scalar(weights[r], strength[:], half_last[:, r - ON_SCALAR : r - ON_SCALAR + 1], 0.0, ALU.mult, ALU.add)
+                half = half_one[:, 0:1] if r == ON_SCALAR else half_last[:, r - ON_SCALAR - 1 : r - ON_SCALAR]
+                nc.gpsimd.tensor_scalar(weights[r], strength[:], half, 0.0, ALU.mult, ALU.add)
 
         nc.vector.tensor_copy(ts_picked[:], ts_raw[:].indirect(live[:]))
         order_scales(rows[:, S : S + PASS], w1s_raw[:, 0:PASS])
         nc.vector.tensor_copy(rows[ROWS_AT:P, 0:S].bitcast(I32), ts_picked[ROWS_AT:P, :].bitcast(I32))
-        nc.scalar.mul(half_gain[:], gains, 0.5)
+        nc.scalar.mul(half_one[:, 0:1], gains[:, H_PASSES - 1, 0:1], 0.5)
+        nc.scalar.mul(half_gain[:], gains[:, 0 : H_PASSES - 1, :], 0.5)
+        weigh(ON_SCALAR)
         deal_rows(scales, rows, nc.sync)
         w1_rest = staged([P, K_PASSES, (H - PASS) // 2], I32, "w1_rest", AT_W1_REST)
         nc.sync.dma_start(w1_rest[:], w1_i32[:, :, PASS // 2 : H // 2])
@@ -169,8 +176,8 @@ def tile_list_draft_tree_sketch_kernel(tc, tab_words, tab_scales, offs, w1_words
             weigh(r)
         order_scales(rows_rest[:], w1s_raw[:, PASS:H])
         deal_rows(scales_rest, rows_rest, nc.sync)
-        nc.gpsimd.tensor_scalar(half_last[:], gains[:, H_PASSES - 1, ON_SCALAR - SLICES + PACK : PACK], 0.5, 0.0, ALU.mult, ALU.add)
-        for r in range(ON_SCALAR, SLICES):
+        nc.gpsimd.tensor_scalar(half_last[:], gains[:, H_PASSES - 1, 1:PACK], 0.5, 0.0, ALU.mult, ALU.add)
+        for r in range(ON_SCALAR + 1, SLICES):
             weigh(r)
 
         def load_ws(b):
@@ -193,7 +200,7 @@ def tile_list_draft_tree_sketch_kernel(tc, tab_words, tab_scales, offs, w1_words
             for a in passes:
                 nc.tensor.matmul_mx(
                     acc[:],
-                    lhsT=w1p[b][:, a, 2 * P * t : 2 * P * (t + 1)].bitcast(FP4X4),
+                    lhsT=w1p[r][:, a, :].bitcast(FP4X4),
                     lhsT_scale=scales[:, a, S + P * r : S + P * (r + 1)] if b == 0 else scales_rest[:, a, P * (r - PACK) : P * (r - PACK + 1)],
                     rhs=v[a][j][:, lo:hi].bitcast(FP8X4),
                     rhs_scale=scales[:, a, cols],
@@ -228,7 +235,7 @@ def tile_list_draft_tree_sketch_kernel(tc, tab_words, tab_scales, offs, w1_words
         load_ws(1)
         order_w1(1, w1_rest[:, :, 0 : PASS // 2], nc.vector.tensor_copy, 0, PACK)
         nc.vector.tensor_scalar(inv_gain[:], inv_raw[:], LARGEST, -LARGEST, ALU.min, ALU.max)
-        order_w1(2, w1_rest[:, :, PASS // 2 : PASS], nc.vector.tensor_copy, 0, PACK)
+        order_w1(2, w1_rest[:, :, PASS // 2 : PASS], nc.vector.tensor_copy, 0, PACK // 2)
         load_ws(2)
         project_part(0, 0, 0, BANK)
         project_part(0, 1, 0, BANK // 2)
@@ -259,7 +266,8 @@ def tile_list_draft_tree_sketch_kernel(tc, tab_words, tab_scales, offs, w1_words
         unit_at = [0, 2 * UNIT_BYTES, 0, 0]
         ux = {}
         th = {}
-        z = [tile([P, w, PACK], BF16, "z%d" % u) for u, (b, c, w) in enumerate(units)]
+        z = [tile([P, w, PACK], BF16, "z%d" % u) for u, (b, c, w) in enumerate(units[:-1])]
+        z.append(staged([P, LATE, PACK], BF16, "z_last", AT_RES + 4 * EARLY * (N // P - 1)))
         z_q = [tile([P, w], U32, "z_q%d" % u) for u, (b, c, w) in enumerate(units)]
         z_s = [tile([P, w], U8, "z_s%d" % u) for u, (b, c, w) in enumerate(units)]
 
@@ -329,6 +337,8 @@ def tile_list_draft_tree_sketch_kernel(tc, tab_words, tab_scales, offs, w1_words
         last_pass, last_unit = H_PASSES - 1, len(units) - 1
         for s, (u, t) in enumerate(steps[:-PACK]):
             pick(u, t)
+            if s == AHEAD:
+                order_w1(2, w1_rest[:, :, PASS // 2 : PASS], nc.scalar.copy, PACK // 2, PACK, AT_INV + 64)
             if s <= last_projected:
                 project(s + AHEAD)
             if s > 0:
@@ -368,6 +378,6 @@ def tile_list_draft_tree_sketch_kernel(tc, tab_words, tab_scales, offs, w1_words
         quantize_z(last_unit, 0, LATE)
         score(1, last_pass, range(tiles))
         for g in range(1, tiles):
-            store(0, g, nc.vector.tensor_copy if g == tiles - 2 else nc.scalar.copy)
+            store(0, g, nc.vector.tensor_copy if g == tiles - 1 else nc.scalar.copy)
         store(1, 0, nc.vector.tensor_copy)
         store(1, 1, nc.scalar.copy)

@@ -33,6 +33,7 @@ RUN = 4
 QUADRANT = 32
 SCALE_ROWS = 4
 ROWS_AT = P - K_PASSES * 16
+W1_ROWS_AT = QUADRANT
 PADDED = 8
 WS_PIECE = 384
 WARM_UPS = 4
@@ -111,19 +112,20 @@ def tile_list_draft_tree_sketch_kernel(tc, tab_words, tab_scales, offs, w1_words
         weights = [staged([P, SLOTS], F32, "weights%d" % r, AT_WEIGHTS + WEIGHT_BYTES * r)[:] for r in range(SLICES)]
 
         nc.vector.memset(ts_raw[0:ROWS_AT, :].bitcast(I32), 0)
-        nc.vector.memset(w1s_raw[0:ROWS_AT, :].bitcast(I32), 0)
+        nc.gpsimd.memset(w1s_raw[0:W1_ROWS_AT, :].bitcast(I32), 0)
+        nc.vector.memset(w1s_raw[2 * QUADRANT : P, :].bitcast(I32), 0)
         nc.vector.memset(scales[:].rearrange("p a c -> p (a c)").bitcast(I32), 0)
         nc.vector.memset(scales_rest[:].rearrange("p a c -> p (a c)").bitcast(I32), 0)
 
         w1_i32 = w1_words.bitcast(I32).rearrange("a p c -> p a c")
 
-        def load_scale_rows(dst, src):
-            nc.sync.dma_start(dst[ROWS_AT:P, :].bitcast(I32), src.bitcast(I32).rearrange("a j c -> j a c"))
+        def load_scale_rows(dst, src, at):
+            nc.sync.dma_start(dst[at : at + QUADRANT, :].bitcast(I32), src.bitcast(I32).rearrange("a j c -> j a c"))
 
         w1_first = staged([P, K_PASSES, PASS // 2], I32, "w1_first", AT_W1_FIRST)
         nc.sync.dma_start(live[:], offs)
-        load_scale_rows(ts_raw, tab_scales)
-        load_scale_rows(w1s_raw, w1_scales)
+        load_scale_rows(ts_raw, tab_scales, ROWS_AT)
+        load_scale_rows(w1s_raw, w1_scales, W1_ROWS_AT)
         nc.sync.dma_start(gains, gain.rearrange("(b p t) -> p b t", p=P, t=PACK))
         nc.sync.dma_start(strength[:], wgt)
         for a in range(K_PASSES):
@@ -137,10 +139,10 @@ def tile_list_draft_tree_sketch_kernel(tc, tab_words, tab_scales, offs, w1_words
 
         def deal_rows(dst, src, queue):
             per_quadrant = K_PASSES * SCALE_ROWS
-            for q in range(P // QUADRANT):
+            for q in (0, 2, 1, 3):
                 queue.dma_start(
                     dst[QUADRANT * q : QUADRANT * q + SCALE_ROWS, :, :].rearrange("p a c -> p (a c)").bitcast(I32),
-                    src[ROWS_AT + per_quadrant * q : ROWS_AT + per_quadrant * (q + 1), :].bitcast(I32),
+                    src[W1_ROWS_AT + per_quadrant * q : W1_ROWS_AT + per_quadrant * (q + 1), :].bitcast(I32),
                 )
 
         def order_w1(b, src, copy, lo, hi, at=None):
@@ -163,7 +165,7 @@ def tile_list_draft_tree_sketch_kernel(tc, tab_words, tab_scales, offs, w1_words
 
         nc.vector.tensor_copy(ts_picked[:], ts_raw[:].indirect(live[:]))
         order_scales(rows[:, S : S + PASS], w1s_raw[:, 0:PASS])
-        nc.vector.tensor_copy(rows[ROWS_AT:P, 0:S].bitcast(I32), ts_picked[ROWS_AT:P, :].bitcast(I32))
+        nc.vector.tensor_copy(rows[W1_ROWS_AT : W1_ROWS_AT + QUADRANT, 0:S].bitcast(I32), ts_picked[ROWS_AT:P, :].bitcast(I32))
         nc.scalar.mul(half_one[:, 0:1], gains[:, H_PASSES - 1, 0:1], 0.5)
         nc.scalar.mul(half_gain[:], gains[:, 0 : H_PASSES - 1, :], 0.5)
         weigh(ON_SCALAR)

@@ -67,6 +67,7 @@ UNIT_BYTES = PACK * SLOTS * 4 + 128
 AT_RES = AT_UNITS + 2 * UNIT_BYTES
 AT_H = AT_UNITS + 4 * UNIT_BYTES
 H_BYTES = 4 * S
+AT_Z_EARLY = AT_H + SLICES * H_BYTES
 WOVEN_ON = 3
 
 
@@ -245,30 +246,45 @@ def tile_list_draft_tree_sketch_kernel(tc, tab_words, tab_scales, offs, w1_words
         for r in range(1, AHEAD):
             project(r)
 
+        def piece(b, i):
+            return slice(WS_PIECE * i, WS_PIECE * (i + 1) if b == 1 or i == 0 else N - P)
+
+        def weave(dst, src, copy):
+            copy(dst.rearrange("p (c i) t -> p c t i", i=RUN), src.rearrange("p t (c i) -> p c t i", i=RUN))
+
         def weave_ws(b, i, copy):
-            cols = slice(WS_PIECE * i, WS_PIECE * (i + 1))
+            cols = piece(b, i)
             if b == 0:
-                ws_bf[b, i] = staged([P, WS_PIECE, PACK], BF16, "ws_bf0_%d" % i, AT_H + H_BYTES * (WOVEN_ON + i))
+                ws_bf[b, i] = staged([P, cols.stop - cols.start, PACK], BF16, "ws_bf0_%d" % i, AT_H + H_BYTES * (WOVEN_ON + i))
             else:
-                ws_bf[b, i] = tile([P, WS_PIECE, PACK], BF16, "ws_bf%d_%d" % (b, i))
-            copy(
-                ws_bf[b, i][:].rearrange("p (c i) t -> p c t i", i=RUN),
-                ws_raw[b][:, :, cols].rearrange("p t (c i) -> p c t i", i=RUN),
-            )
+                ws_bf[b, i] = tile([P, cols.stop - cols.start, PACK], BF16, "ws_bf%d_%d" % (b, i))
+            weave(ws_bf[b, i][:], ws_raw[b][:, :, cols], copy)
 
         def quantize_ws(b, i):
-            cols = slice(WS_PIECE * i, WS_PIECE * (i + 1))
+            cols = piece(b, i)
             if (b, i) == (0, 0):
                 ws_s[b] = staged([P, N], U8, "ws_s0", AT_WEIGHTS + WEIGHT_BYTES * (WOVEN_ON + 1))
             elif i == 0:
                 ws_s[b] = tile([P, N], U8, "ws_s%d" % b)
             nc.vector.quantize_mx(ws_q[b][:, cols].bitcast(FP8X4), ws_s[b][:, cols], ws_bf[b, i][:].rearrange("p n t -> p (n t)"))
 
+        last_bf = staged([P, 2, P, PACK], BF16, "last_bf", AT_Z_EARLY)
+        last_q = tile([P, 2 * P], U32, "last_q")
+        last_s = tile([P, 2 * P], U8, "last_s")
+
+        def stationary(b, n):
+            if n == N // P - 1 and b != 1:
+                cols = slice(P * (b // 2), P * (b // 2 + 1))
+                return last_q[:, cols], last_s[:, cols]
+            cols = slice(P * n, P * (n + 1))
+            return ws_q[b][:, cols], ws_s[b][:, cols]
+
         units = [(0, 0, SLOTS), (1, 0, SLOTS), (2, 0, EARLY), (2, EARLY, LATE)]
         unit_at = [0, 2 * UNIT_BYTES, 0, 0]
         ux = {}
         th = {}
-        z = [tile([P, w, PACK], BF16, "z%d" % u) for u, (b, c, w) in enumerate(units[:-1])]
+        z = [tile([P, w, PACK], BF16, "z%d" % u) for u, (b, c, w) in enumerate(units[:-2])]
+        z.append(staged([P, EARLY, PACK], BF16, "z_early", AT_Z_EARLY))
         z.append(staged([P, LATE, PACK], BF16, "z_last", AT_RES + 4 * EARLY * (N // P - 1)))
         z_q = [tile([P, w], U32, "z_q%d" % u) for u, (b, c, w) in enumerate(units)]
         z_s = [tile([P, w], U8, "z_s%d" % u) for u, (b, c, w) in enumerate(units)]
@@ -307,18 +323,19 @@ def tile_list_draft_tree_sketch_kernel(tc, tab_words, tab_scales, offs, w1_words
             u = b if b < H_PASSES - 1 else b + part
             for n in tiles:
                 g, e = divmod(n, per_bank)
-                if b == 0 and e == 0:
+                opens = (part, g) not in scores
+                if opens:
                     scores[part, g] = psum.tile([P, per_bank, w], F32, name="score", tag="bank%d" % (H_BANKS if not scores else (len(sums) + len(scores) - 1) % H_BANKS))
                 done = 0
                 for width in widths[part]:
                     lo = c - units[u][1] + done
                     nc.tensor.matmul_mx(
                         scores[part, g][:, e, done : done + width],
-                        lhsT=ws_q[b][:, P * n : P * (n + 1)].bitcast(FP8X4),
-                        lhsT_scale=ws_s[b][:, P * n : P * (n + 1)],
+                        lhsT=stationary(b, n)[0].bitcast(FP8X4),
+                        lhsT_scale=stationary(b, n)[1],
                         rhs=z_q[u][:, lo : lo + width].bitcast(FP8X4),
                         rhs_scale=z_s[u][:, lo : lo + width],
-                        start=(b == 0 and e == 0 and done == 0),
+                        start=(opens and done == 0),
                         stop=(b == H_PASSES - 1 and e == per_bank - 1 and done + width == w),
                     )
                     done += width
@@ -359,12 +376,13 @@ def tile_list_draft_tree_sketch_kernel(tc, tab_words, tab_scales, offs, w1_words
                 quantize_ws(*divmod(weave_steps.index(s - 1), pieces))
             if s in score_steps:
                 for part in range(len(parts)):
-                    score(part, score_steps.index(s), range(N // P))
+                    score(part, score_steps.index(s), range(N // P - (s == score_steps[0])))
 
         tiles = N // P
         for i in range(pieces):
             weave_ws(last_pass, i, nc.scalar.copy)
         weave_z(last_unit - 1, 0, EARLY)
+        weave(last_bf[:, 0], ws_raw[0][:, :, N - P : N], nc.scalar.copy)
         for t in range(PACK):
             pick(last_unit, t)
             if t == 0:
@@ -374,7 +392,11 @@ def tile_list_draft_tree_sketch_kernel(tc, tab_words, tab_scales, offs, w1_words
             gate(last_unit, t)
             if t == 0:
                 store(0, 0, nc.scalar.copy)
+        weave(last_bf[:, 1], ws_raw[last_pass][:, :, N - P : N], nc.vector.tensor_copy)
         quantize_ws(last_pass, 1)
+        nc.vector.quantize_mx(last_q[:].bitcast(FP8X4), last_s[:], last_bf[:].rearrange("p b n t -> p (b n t)"))
+        for part in range(len(parts)):
+            score(part, 0, [tiles - 1])
         score(0, last_pass, range(tiles // 2, tiles))
         weave_z(last_unit, 0, LATE)
         quantize_z(last_unit, 0, LATE)

@@ -36,7 +36,7 @@ ROWS_AT = P - K_PASSES * 16
 W1_ROWS_AT = QUADRANT
 PADDED = 8
 WS_PIECE = 384
-WARM_UPS = 4
+WARM_UPS = (256, 256, 512, 512, 512, 512)
 AHEAD = 3
 LARGEST = 3.0e38
 
@@ -52,7 +52,8 @@ AT_WS1 = 0
 AT_TS_RAW = 2 * TAB_BYTES
 AT_W1_FIRST = AT_TS_RAW + T
 AT_W1_REST = AT_W1_FIRST + W1P_BYTES
-AT_ROWS_REST = AT_W1_REST + 2 * W1P_BYTES
+AT_BIAS = AT_W1_REST + 2 * W1P_BYTES
+AT_ROWS_REST = AT_BIAS + 128
 AT_TS_PICKED = AT_ROWS_REST - EDGE
 AT_HALF_LAST = AT_ROWS_REST + H - PASS
 AT_HALF_ONE = AT_HALF_LAST - 64
@@ -104,19 +105,19 @@ def tile_list_draft_tree_sketch_kernel(tc, tab_words, tab_scales, offs, w1_words
         ws_s = {}
         h = [staged([P, S], F32, "h%d" % r, AT_H + H_BYTES * r) for r in range(SLICES)]
         gains_pad = tile([P, H_PASSES, PADDED], F32, "gains")
-        bias_pad = tile([P, H_PASSES, PADDED], F32, "bias")
+        bias_pad = staged([P, H_PASSES, PADDED], F32, "bias", AT_BIAS)
         gains = gains_pad[:, :, 0:PACK]
         bias = bias_pad[:, :, 0:PACK]
         strength = tile([P, SLOTS], F32, "strength")
         half_gain = tile([P, H_PASSES - 1, PACK], F32, "half_gain")
-        inv_gain = tile([P, H_PASSES, PACK], F32, "inv_gain")
+        inv_gain = staged([P, H_PASSES, PACK], F32, "inv_gain", AT_INV)
         weights = [staged([P, SLOTS], F32, "weights%d" % r, AT_WEIGHTS + WEIGHT_BYTES * r)[:] for r in range(SLICES)]
 
         nc.vector.memset(ts_raw[0:ROWS_AT, :].bitcast(I32), 0)
         nc.gpsimd.memset(w1s_raw[0:W1_ROWS_AT, :].bitcast(I32), 0)
         nc.vector.memset(w1s_raw[2 * QUADRANT : P, :].bitcast(I32), 0)
         nc.vector.memset(scales[:].rearrange("p a c -> p (a c)").bitcast(I32), 0)
-        nc.vector.memset(scales_rest[:].rearrange("p a c -> p (a c)").bitcast(I32), 0)
+        nc.gpsimd.memset(scales_rest[:].rearrange("p a c -> p (a c)").bitcast(I32), 0)
 
         w1_i32 = w1_words.bitcast(I32).rearrange("a p c -> p a c")
 
@@ -132,7 +133,6 @@ def tile_list_draft_tree_sketch_kernel(tc, tab_words, tab_scales, offs, w1_words
         for a in range(K_PASSES):
             nc.sync.dma_start(tab[a][:], tab_words[a].rearrange("p t i -> p (t i)").bitcast(I32))
         nc.sync.dma_start(w1_first[:], w1_i32[:, :, 0 : PASS // 2])
-        nc.sync.dma_start(bias, b1.rearrange("(b p t) -> p b t", p=P, t=PACK))
         nc.sync.dma_start(picks[:], offs2)
 
         def order_scales(dst, src):
@@ -167,10 +167,13 @@ def tile_list_draft_tree_sketch_kernel(tc, tab_words, tab_scales, offs, w1_words
         nc.vector.tensor_copy(ts_picked[:], ts_raw[:].indirect(live[:]))
         order_scales(rows[:, S : S + PASS], w1s_raw[:, 0:PASS])
         nc.vector.tensor_copy(rows[W1_ROWS_AT : W1_ROWS_AT + QUADRANT, 0:S].bitcast(I32), ts_picked[ROWS_AT:P, :].bitcast(I32))
+        inv_raw = tile([P, H_PASSES, PACK], F32, "inv_raw")
+        nc.vector.reciprocal(inv_raw[:], gains)
         nc.scalar.mul(half_one[:, 0:1], gains[:, H_PASSES - 1, 0:1], 0.5)
         nc.scalar.mul(half_gain[:], gains[:, 0 : H_PASSES - 1, :], 0.5)
         weigh(ON_SCALAR)
         deal_rows(scales, rows, nc.sync)
+        nc.sync.dma_start(bias, b1.rearrange("(b p t) -> p b t", p=P, t=PACK))
         w1_rest = staged([P, K_PASSES, (H - PASS) // 2], I32, "w1_rest", AT_W1_REST)
         nc.sync.dma_start(w1_rest[:], w1_i32[:, :, PASS // 2 : H // 2])
         for t in range(0, PACK, 2):
@@ -200,50 +203,53 @@ def tile_list_draft_tree_sketch_kernel(tc, tab_words, tab_scales, offs, w1_words
             acc = psum.tile([P, hi - lo], F32, name="acc", tag="bank%d" % bank)
             cols = slice(BANK * j + lo, BANK * j + hi)
             passes = list(range(K_PASSES)) if r == 0 else list(reversed(range(K_PASSES)))
+            cuts = [lo, lo + BANK // 2, hi] if hi - lo == BANK - P else [lo, hi]
             for a in passes:
-                nc.tensor.matmul_mx(
-                    acc[:],
-                    lhsT=w1p[r][:, a, :].bitcast(FP4X4),
-                    lhsT_scale=scales[:, a, S + P * r : S + P * (r + 1)] if b == 0 else scales_rest[:, a, P * (r - PACK) : P * (r - PACK + 1)],
-                    rhs=v[a][j][:, lo:hi].bitcast(FP8X4),
-                    rhs_scale=scales[:, a, cols],
-                    start=(a == passes[0]),
-                    stop=(a == passes[-1]),
-                )
+                for x, y in zip(cuts, cuts[1:]):
+                    nc.tensor.matmul_mx(
+                        acc[:, x - lo : y - lo],
+                        lhsT=w1p[r][:, a, :].bitcast(FP4X4),
+                        lhsT_scale=scales[:, a, S + P * r : S + P * (r + 1)] if b == 0 else scales_rest[:, a, P * (r - PACK) : P * (r - PACK + 1)],
+                        rhs=v[a][j][:, x:y].bitcast(FP8X4),
+                        rhs_scale=scales[:, a, BANK * j + x : BANK * j + y],
+                        start=(a == passes[0] and x == lo),
+                        stop=(a == passes[-1] and y == hi),
+                    )
             nc.scalar.activation(h[r][:, cols], acc[:], ACT.Identity, bias=bias[:, b, t : t + 1])
 
         def project(r):
             for j in range(2):
                 project_part(r, j, 0, BANK)
 
-        gather_words(0, 0, 0, BANK)
+        gather_words(0, 0, 0, BANK // 2)
+        gather_words(0, 0, BANK // 2, BANK)
         warm = psum.tile([P, BANK], F32, name="warm", tag="bank%d" % (BANKS - 1))
-        for n in range(WARM_UPS):
+        for n in WARM_UPS:
             nc.tensor.matmul_mx(
-                warm[:],
+                warm[:, 0:n],
                 lhsT=w1s_raw[:, 0 : 2 * P].bitcast(FP4X4),
                 lhsT_scale=w1s_raw[:, 0:P],
-                rhs=v[0][0][:].bitcast(FP8X4),
-                rhs_scale=w1s_raw[:, 0:BANK],
+                rhs=v[0][0][:, 0:n].bitcast(FP8X4),
+                rhs_scale=w1s_raw[:, 0:n],
                 start=True,
                 stop=True,
             )
         gather_words(0, 1, 0, BANK)
         gather_words(1, 0, 0, BANK)
-        gather_words(1, 1, 0, BANK // 2)
-        gather_words(1, 1, BANK // 2, BANK)
-        inv_raw = staged([P, H_PASSES, PACK], F32, "inv_raw", AT_INV)
-        nc.vector.reciprocal(inv_raw[:], gains)
+        gather_words(1, 1, 0, BANK - P)
+        gather_words(1, 1, BANK - P, BANK)
         load_ws(0)
         load_ws(1)
         order_w1(1, w1_rest[:, :, 0 : PASS // 2], nc.vector.tensor_copy, 0, PACK)
         nc.vector.tensor_scalar(inv_gain[:], inv_raw[:], LARGEST, -LARGEST, ALU.min, ALU.max)
-        order_w1(2, w1_rest[:, :, PASS // 2 : PASS], nc.vector.tensor_copy, 0, PACK // 2)
+        order_w1(2, w1_rest[:, :, PASS // 2 : PASS], nc.vector.tensor_copy, 0, PACK)
         load_ws(2)
         project_part(0, 0, 0, BANK)
-        project_part(0, 1, 0, BANK // 2)
-        project_part(0, 1, BANK // 2, BANK)
-        for r in range(1, AHEAD):
+        project_part(1, 0, 0, BANK)
+        project_part(0, 1, 0, BANK - P)
+        project_part(0, 1, BANK - P, BANK)
+        project_part(1, 1, 0, BANK)
+        for r in range(2, AHEAD):
             project(r)
 
         def piece(b, i):
@@ -258,7 +264,10 @@ def tile_list_draft_tree_sketch_kernel(tc, tab_words, tab_scales, offs, w1_words
                 ws_bf[b, i] = staged([P, cols.stop - cols.start, PACK], BF16, "ws_bf0_%d" % i, AT_H + H_BYTES * (WOVEN_ON + i))
             else:
                 ws_bf[b, i] = tile([P, cols.stop - cols.start, PACK], BF16, "ws_bf%d_%d" % (b, i))
-            weave(ws_bf[b, i][:], ws_raw[b][:, :, cols], copy)
+            if (b, i) == (0, 1):
+                weave(ws_bf[b, i][:, 0:P, :], ws_raw[b][:, :, cols.start : cols.start + P], copy)
+            else:
+                weave(ws_bf[b, i][:], ws_raw[b][:, :, cols], copy)
 
         def quantize_ws(b, i):
             cols = piece(b, i)
@@ -356,8 +365,6 @@ def tile_list_draft_tree_sketch_kernel(tc, tab_words, tab_scales, offs, w1_words
         last_pass, last_unit = H_PASSES - 1, len(units) - 1
         for s, (u, t) in enumerate(steps[:-PACK]):
             pick(u, t)
-            if s == AHEAD:
-                order_w1(2, w1_rest[:, :, PASS // 2 : PASS], nc.scalar.copy, PACK // 2, PACK, AT_INV + 64)
             if s <= last_projected:
                 project(s + AHEAD)
             if s > 0:
@@ -372,7 +379,11 @@ def tile_list_draft_tree_sketch_kernel(tc, tab_words, tab_scales, offs, w1_words
                     weave_z(u - 1, lo, lo + HALF)
                 for lo in (0, HALF):
                     quantize_z(u - 1, lo, lo + HALF)
-            if s - 1 in weave_steps:
+            if s == last_projected - 1:
+                weave(ws_bf[0, 1][:, P : 2 * P, :], ws_raw[0][:, :, WS_PIECE + P : N - P], nc.scalar.copy)
+            if s == last_projected:
+                quantize_ws(0, 1)
+            if s - 1 in weave_steps and s - 1 != WOVEN_ON + 1:
                 quantize_ws(*divmod(weave_steps.index(s - 1), pieces))
             if s in score_steps:
                 for part in range(len(parts)):

@@ -44,7 +44,7 @@ WS_BYTES = PACK * N * 4
 TAB_BYTES = 4 * T
 W1P_BYTES = 2 * K_PASSES * PASS
 WEIGHT_BYTES = 4 * SLOTS
-ON_SCALAR = 8
+ON_SCALAR = 9
 EDGE = 512
 AT_TAB = (0, TAB_BYTES)
 AT_INV = WS_BYTES + 64
@@ -109,7 +109,7 @@ def tile_list_draft_tree_sketch_kernel(tc, tab_words, tab_scales, offs, w1_words
         gains = gains_pad[:, :, 0:PACK]
         bias = bias_pad[:, :, 0:PACK]
         strength = tile([P, SLOTS], F32, "strength")
-        half_gain = tile([P, H_PASSES - 1, PACK], F32, "half_gain")
+        half_gain = tile([P, H_PASSES, PACK], F32, "half_gain")
         inv_gain = staged([P, H_PASSES, PACK], F32, "inv_gain", AT_INV)
         weights = [staged([P, SLOTS], F32, "weights%d" % r, AT_WEIGHTS + WEIGHT_BYTES * r)[:] for r in range(SLICES)]
 
@@ -169,8 +169,8 @@ def tile_list_draft_tree_sketch_kernel(tc, tab_words, tab_scales, offs, w1_words
         nc.vector.tensor_copy(rows[W1_ROWS_AT : W1_ROWS_AT + QUADRANT, 0:S].bitcast(I32), ts_picked[ROWS_AT:P, :].bitcast(I32))
         inv_raw = tile([P, H_PASSES, PACK], F32, "inv_raw")
         nc.vector.reciprocal(inv_raw[:], gains)
-        nc.scalar.mul(half_one[:, 0:1], gains[:, H_PASSES - 1, 0:1], 0.5)
-        nc.scalar.mul(half_gain[:], gains[:, 0 : H_PASSES - 1, :], 0.5)
+        nc.scalar.mul(half_one[:, 0:1], gains[:, H_PASSES - 1, 1:2], 0.5)
+        nc.scalar.mul(half_gain[:], gains, 0.5)
         weigh(ON_SCALAR)
         deal_rows(scales, rows, nc.sync)
         nc.sync.dma_start(bias, b1.rearrange("(b p t) -> p b t", p=P, t=PACK))
@@ -182,7 +182,7 @@ def tile_list_draft_tree_sketch_kernel(tc, tab_words, tab_scales, offs, w1_words
             weigh(r)
         order_scales(rows_rest[:], w1s_raw[:, PASS:H])
         deal_rows(scales_rest, rows_rest, nc.sync)
-        nc.gpsimd.tensor_scalar(half_last[:], gains[:, H_PASSES - 1, 1:PACK], 0.5, 0.0, ALU.mult, ALU.add)
+        nc.gpsimd.tensor_scalar(half_last[:], gains[:, H_PASSES - 1, 2:PACK], 0.5, 0.0, ALU.mult, ALU.add)
         for r in range(ON_SCALAR + 1, SLICES):
             weigh(r)
 

@@ -57,6 +57,7 @@ AT_ROWS_REST = AT_BIAS + 128
 AT_TS_PICKED = AT_ROWS_REST - EDGE
 AT_HALF_LAST = AT_ROWS_REST + H - PASS
 AT_HALF_ONE = AT_HALF_LAST - 64
+AT_HALF_OWN = AT_HALF_ONE - 128
 AT_WS2 = AT_ROWS_REST
 AT_WEIGHTS = AT_WS2 + WS_BYTES
 AT_ROWS = AT_WEIGHTS + SLICES * WEIGHT_BYTES
@@ -95,6 +96,7 @@ def tile_list_draft_tree_sketch_kernel(tc, tab_words, tab_scales, offs, w1_words
         scales_rest = tile([P, K_PASSES, H - PASS], U8, "scales_rest")
         half_one = staged([P, 32], F32, "half_one", AT_HALF_ONE)
         rows_rest = staged([P, H - PASS], U8, "rows_rest", AT_ROWS_REST)
+        half_own = staged([P, 32], F32, "half_own", AT_HALF_OWN)
         half_last = staged([P, SLICES - ON_SCALAR - 1], F32, "half_last", AT_HALF_LAST)
         w1p = {}
         tab = [staged([P, T], I32, "tab%d" % a, AT_TAB[a]) for a in range(K_PASSES)]
@@ -170,6 +172,8 @@ def tile_list_draft_tree_sketch_kernel(tc, tab_words, tab_scales, offs, w1_words
         inv_raw = tile([P, H_PASSES, PACK], F32, "inv_raw")
         nc.vector.reciprocal(inv_raw[:], gains)
         nc.scalar.mul(half_one[:, 0:1], gains[:, H_PASSES - 1, 1:2], 0.5)
+        nc.scalar.mul(half_own[:, 0:1], gains[:, H_PASSES - 1, 0:1], 0.5)
+        nc.vector.tensor_scalar_mul(weights[ON_SCALAR - 1], strength[:], half_own[:, 0:1])
         nc.scalar.mul(half_gain[:], gains, 0.5)
         weigh(ON_SCALAR)
         deal_rows(scales, rows, nc.sync)
@@ -178,7 +182,7 @@ def tile_list_draft_tree_sketch_kernel(tc, tab_words, tab_scales, offs, w1_words
         nc.sync.dma_start(w1_rest[:], w1_i32[:, :, PASS // 2 : H // 2])
         for t in range(0, PACK, 2):
             order_w1(0, w1_first[:], nc.scalar.copy, t, t + 2)
-        for r in range(ON_SCALAR):
+        for r in range(ON_SCALAR - 1):
             weigh(r)
         order_scales(rows_rest[:], w1s_raw[:, PASS:H])
         deal_rows(scales_rest, rows_rest, nc.sync)

@@ -239,7 +239,8 @@ def tile_list_draft_tree_sketch_kernel(tc, tab_words, tab_scales, offs, w1_words
                 stop=True,
             )
         gather_words(0, 1, 0, BANK)
-        gather_words(1, 0, 0, BANK)
+        gather_words(1, 0, 0, BANK // 2)
+        gather_words(1, 0, BANK // 2, BANK)
         gather_words(1, 1, 0, BANK - P)
         gather_words(1, 1, BANK - P, BANK)
         load_ws(0)
@@ -248,8 +249,9 @@ def tile_list_draft_tree_sketch_kernel(tc, tab_words, tab_scales, offs, w1_words
         nc.vector.tensor_scalar(inv_gain[:], inv_raw[:], LARGEST, -LARGEST, ALU.min, ALU.max)
         order_w1(2, w1_rest[:, :, PASS // 2 : PASS], nc.vector.tensor_copy, 0, PACK)
         load_ws(2)
-        project_part(0, 0, 0, BANK)
-        project_part(1, 0, 0, BANK)
+        for lo in (0, BANK // 2):
+            for r in range(2):
+                project_part(r, 0, lo, lo + BANK // 2)
         project_part(0, 1, 0, BANK - P)
         project_part(0, 1, BANK - P, BANK)
         project_part(1, 1, 0, BANK)

from contextlib import ExitStack

import concourse.mybir as mybir

K, T, S, H, SLOTS, N = 1024, 2048, 1024, 1536, 512, 768
FLOPS = 2 * K * H * S + 2 * H * N * SLOTS

F32 = mybir.dt.float32
BF16 = mybir.dt.bfloat16
I32 = mybir.dt.int32
U32 = mybir.dt.uint32
U16 = mybir.dt.uint16
U8 = mybir.dt.uint8
FP8X4 = mybir.dt.float8_e4m3fn_x4
FP4X4 = mybir.dt.float4_e2m1fn_x4
ACT = mybir.ActivationFunctionType
ALU = mybir.AluOpType

P = 128
PACK = 4
PASS = P * PACK
K_PASSES = K // PASS
H_PASSES = H // PASS
SLICES = H_PASSES * PACK
LIST = 16
BANK = 512
BANKS = 8
H_BANKS = 7
HALF = SLOTS // 2
LATE = SLOTS // 4
EARLY = SLOTS - LATE
RUN = 4
QUADRANT = 32
SCALE_ROWS = 4
ROWS_AT = P - K_PASSES * 16
W1_ROWS_AT = QUADRANT
PADDED = 8
WS_PIECE = 384
WARM_UPS = (256, 256, 512, 512, 512, 512)
AHEAD = 3
LARGEST = 3.0e38

WS_BYTES = PACK * N * 4
TAB_BYTES = 4 * T
W1P_BYTES = 2 * K_PASSES * PASS
WEIGHT_BYTES = 4 * SLOTS
ON_SCALAR = 9
EDGE = 512
AT_TAB = (0, TAB_BYTES)
AT_INV = WS_BYTES + 64
AT_WS1 = 0
AT_TS_RAW = 2 * TAB_BYTES
AT_W1_FIRST = AT_TS_RAW + T
AT_W1_REST = AT_W1_FIRST + W1P_BYTES
AT_BIAS = AT_W1_REST + 2 * W1P_BYTES
AT_ROWS_REST = AT_BIAS + 128
AT_TS_PICKED = AT_ROWS_REST - EDGE
AT_HALF_LAST = AT_ROWS_REST + H - PASS
AT_HALF_ONE = AT_HALF_LAST - 64
AT_HALF_OWN = AT_HALF_ONE - 128
AT_WS2 = AT_ROWS_REST
AT_WEIGHTS = AT_WS2 + WS_BYTES
AT_ROWS = AT_WEIGHTS + SLICES * WEIGHT_BYTES
AT_WS0 = AT_ROWS
AT_WS = (AT_WS0, AT_WS1, AT_WS2)
AT_UNITS = AT_WS0 + WS_BYTES
STAGGER = 1
UNIT_BYTES = PACK * SLOTS * 4 + 128
AT_RES = AT_UNITS + 2 * UNIT_BYTES
AT_H = AT_UNITS + 4 * UNIT_BYTES
H_BYTES = 4 * S
AT_Z_EARLY = AT_H + SLICES * H_BYTES
WOVEN_ON = 3


def tile_list_draft_tree_sketch_kernel(tc, tab_words, tab_scales, offs, w1_words, w1_scales, b1, offs2, wgt, gain, ws, out):
    nc = tc.nc
    with ExitStack() as ctx:
        keep = ctx.enter_context(tc.tile_pool(name="keep", bufs=1))
        stage = ctx.enter_context(tc.tile_pool(name="stage", bufs=1))
        psum = ctx.enter_context(tc.psum_pool(name="psum", bufs=1))

        def tile(shape, dtype, name):
            return keep.tile(shape, dtype, name=name, align_bytes=64)

        def staged(shape, dtype, name, offset):
            return stage.tile(shape, dtype, name=name, align_bytes=64, offset=offset)

        live = tile([P, S // LIST], U16, "live")
        picks = tile([P, SLOTS // LIST], U16, "picks")
        ts_raw = staged([P, T], U8, "ts_raw", AT_TS_RAW)
        w1s_raw = tile([P, H], U8, "w1s_raw")
        ts_picked = staged([P, S], U8, "ts_picked", AT_TS_PICKED)
        rows = staged([P, S + PASS], U8, "rows", AT_ROWS)
        scales = tile([P, K_PASSES, S + PASS], U8, "scales")
        scales_rest = tile([P, K_PASSES, H - PASS], U8, "scales_rest")
        half_one = staged([P, 32], F32, "half_one", AT_HALF_ONE)
        rows_rest = staged([P, H - PASS], U8, "rows_rest", AT_ROWS_REST)
        half_own = staged([P, 32], F32, "half_own", AT_HALF_OWN)
        half_last = staged([P, SLICES - ON_SCALAR - 1], F32, "half_last", AT_HALF_LAST)
        w1p = {}
        tab = [staged([P, T], I32, "tab%d" % a, AT_TAB[a]) for a in range(K_PASSES)]
        v = [[tile([P, BANK], U32, "v%d_%d" % (a, j)) for j in range(2)] for a in range(K_PASSES)]
        ws_raw = {}
        ws_bf = {}
        ws_q = [tile([P, N], U32, "ws_q%d" % b) for b in range(H_PASSES)]
        ws_s = {}
        h = [staged([P, S], F32, "h%d" % r, AT_H + H_BYTES * r) for r in range(SLICES)]
        gains_pad = tile([P, H_PASSES, PADDED], F32, "gains")
        bias_pad = staged([P, H_PASSES, PADDED], F32, "bias", AT_BIAS)
        gains = gains_pad[:, :, 0:PACK]
        bias = bias_pad[:, :, 0:PACK]
        strength = tile([P, SLOTS], F32, "strength")
        half_gain = tile([P, H_PASSES, PACK], F32, "half_gain")
        inv_gain = staged([P, H_PASSES, PACK], F32, "inv_gain", AT_INV)
        weights = [staged([P, SLOTS], F32, "weights%d" % r, AT_WEIGHTS + WEIGHT_BYTES * r)[:] for r in range(SLICES)]

        nc.vector.memset(ts_raw[0:ROWS_AT, :].bitcast(I32), 0)
        nc.gpsimd.memset(w1s_raw[0:W1_ROWS_AT, :].bitcast(I32), 0)
        nc.vector.memset(w1s_raw[2 * QUADRANT : P, :].bitcast(I32), 0)
        nc.vector.memset(scales[:].rearrange("p a c -> p (a c)").bitcast(I32), 0)
        nc.gpsimd.memset(scales_rest[:].rearrange("p a c -> p (a c)").bitcast(I32), 0)

        w1_i32 = w1_words.bitcast(I32).rearrange("a p c -> p a c")

        def load_scale_rows(dst, src, at):
            nc.sync.dma_start(dst[at : at + QUADRANT, :].bitcast(I32), src.bitcast(I32).rearrange("a j c -> j a c"))

        w1_first = staged([P, K_PASSES, PASS // 2], I32, "w1_first", AT_W1_FIRST)
        nc.sync.dma_start(live[:], offs)
        load_scale_rows(ts_raw, tab_scales, ROWS_AT)
        load_scale_rows(w1s_raw, w1_scales, W1_ROWS_AT)
        nc.sync.dma_start(gains, gain.rearrange("(b p t) -> p b t", p=P, t=PACK))
        nc.sync.dma_start(strength[:], wgt)
        for a in range(K_PASSES):
            nc.sync.dma_start(tab[a][:], tab_words[a].rearrange("p t i -> p (t i)").bitcast(I32))
        nc.sync.dma_start(w1_first[:], w1_i32[:, :, 0 : PASS // 2])
        nc.sync.dma_start(picks[:], offs2)

        def order_scales(dst, src):
            nc.gpsimd.tensor_copy(dst.rearrange("p (b t m) -> p t b m", t=PACK, m=P), src.rearrange("p (b m t) -> p t b m", t=PACK, m=P))

        def deal_rows(dst, src, queue):
            per_quadrant = K_PASSES * SCALE_ROWS
            for q in (0, 2, 1, 3):
                queue.dma_start(
                    dst[QUADRANT * q : QUADRANT * q + SCALE_ROWS, :, :].rearrange("p a c -> p (a c)").bitcast(I32),
                    src[W1_ROWS_AT + per_quadrant * q : W1_ROWS_AT + per_quadrant * (q + 1), :].bitcast(I32),
                )

        def order_w1(b, src, copy, lo, hi, at=None):
            shape, name = [P, K_PASSES, 2 * P * (hi - lo)], "w1p%d_%d" % (b, lo)
            ordered = tile(shape, U8, name) if at is None else staged(shape, U8, name, at)
            for t in range(lo, hi):
                w1p[PACK * b + t] = ordered[:, :, 2 * P * (t - lo) : 2 * P * (t - lo + 1)]
            copy(
                ordered[:].bitcast(U16).rearrange("p a (t m) -> p a t m", m=P),
                src.bitcast(U16).rearrange("p a (m t) -> p a t m", t=PACK)[:, :, lo:hi, :],
            )

        def weigh(r):
            b, t = divmod(r, PACK)
            if r < ON_SCALAR:
                nc.scalar.activation(weights[r], strength[:], ACT.Identity, scale=half_gain[:, b, t : t + 1])
            else:
                half = half_one[:, 0:1] if r == ON_SCALAR else half_last[:, r - ON_SCALAR - 1 : r - ON_SCALAR]
                nc.gpsimd.tensor_scalar(weights[r], strength[:], half, 0.0, ALU.mult, ALU.add)

        nc.vector.tensor_copy(ts_picked[:], ts_raw[:].indirect(live[:]))
        order_scales(rows[:, S : S + PASS], w1s_raw[:, 0:PASS])
        nc.vector.tensor_copy(rows[W1_ROWS_AT : W1_ROWS_AT + QUADRANT, 0:S].bitcast(I32), ts_picked[ROWS_AT:P, :].bitcast(I32))
        inv_raw = tile([P, H_PASSES, PACK], F32, "inv_raw")
        nc.vector.reciprocal(inv_raw[:], gains)
        nc.scalar.mul(half_one[:, 0:1], gains[:, H_PASSES - 1, 1:2], 0.5)
        nc.scalar.mul(half_own[:, 0:1], gains[:, H_PASSES - 1, 0:1], 0.5)
        nc.vector.tensor_scalar_mul(weights[ON_SCALAR - 1], strength[:], half_own[:, 0:1])
        nc.scalar.mul(half_gain[:], gains, 0.5)
        weigh(ON_SCALAR)
        deal_rows(scales, rows, nc.sync)
        nc.sync.dma_start(bias, b1.rearrange("(b p t) -> p b t", p=P, t=PACK))
        w1_rest = staged([P, K_PASSES, (H - PASS) // 2], I32, "w1_rest", AT_W1_REST)
        nc.sync.dma_start(w1_rest[:], w1_i32[:, :, PASS // 2 : H // 2])
        for t in range(0, PACK, 2):
            order_w1(0, w1_first[:], nc.scalar.copy, t, t + 2)
        for r in range(ON_SCALAR - 1):
            weigh(r)
        order_scales(rows_rest[:], w1s_raw[:, PASS:H])
        deal_rows(scales_rest, rows_rest, nc.sync)
        nc.gpsimd.tensor_scalar(half_last[:], gains[:, H_PASSES - 1, 2:PACK], 0.5, 0.0, ALU.mult, ALU.add)
        for r in range(ON_SCALAR + 1, SLICES):
            weigh(r)

        def load_ws(b):
            ws_raw[b] = staged([P, PACK, N], F32, "ws_raw%d" % b, AT_WS[b])
            nc.sync.dma_start(ws_raw[b][:], ws[PASS * b : PASS * (b + 1), :].rearrange("(p t) n -> p t n", t=PACK))

        def gather_words(a, j, lo, hi):
            entries = live[:, (BANK * j + lo) // LIST : (BANK * j + hi) // LIST]
            nc.vector.tensor_copy(v[a][j][:, lo:hi], tab[a][:].bitcast(U32).indirect(entries))

        sums = []

        def project_part(r, j, lo, hi):
            b, t = divmod(r, PACK)
            bank = len(sums) % H_BANKS
            sums.append(bank)
            acc = psum.tile([P, hi - lo], F32, name="acc", tag="bank%d" % bank)
            cols = slice(BANK * j + lo, BANK * j + hi)
            passes = list(range(K_PASSES)) if r == 0 else list(reversed(range(K_PASSES)))
            cuts = [lo, lo + BANK // 2, hi] if hi - lo == BANK - P else [lo, hi]
            for a in passes:
                for x, y in zip(cuts, cuts[1:]):
                    nc.tensor.matmul_mx(
                        acc[:, x - lo : y - lo],
                        lhsT=w1p[r][:, a, :].bitcast(FP4X4),
                        lhsT_scale=scales[:, a, S + P * r : S + P * (r + 1)] if b == 0 else scales_rest[:, a, P * (r - PACK) : P * (r - PACK + 1)],
                        rhs=v[a][j][:, x:y].bitcast(FP8X4),
                        rhs_scale=scales[:, a, BANK * j + x : BANK * j + y],
                        start=(a == passes[0] and x == lo),
                        stop=(a == passes[-1] and y == hi),
                    )
            nc.scalar.activation(h[r][:, cols], acc[:], ACT.Identity, bias=bias[:, b, t : t + 1])

        def project(r):
            for j in range(2):
                project_part(r, j, 0, BANK)

        gather_words(0, 0, 0, BANK // 2)
        gather_words(0, 0, BANK // 2, BANK)
        warm = psum.tile([P, BANK], F32, name="warm", tag="bank%d" % (BANKS - 1))
        for n in WARM_UPS:
            nc.tensor.matmul_mx(
                warm[:, 0:n],
                lhsT=w1s_raw[:, 0 : 2 * P].bitcast(FP4X4),
                lhsT_scale=w1s_raw[:, 0:P],
                rhs=v[0][0][:, 0:n].bitcast(FP8X4),
                rhs_scale=w1s_raw[:, 0:n],
                start=True,
                stop=True,
            )
        gather_words(0, 1, 0, BANK)
        gather_words(1, 0, 0, BANK // 2)
        gather_words(1, 0, BANK // 2, BANK)
        gather_words(1, 1, 0, BANK - P)
        gather_words(1, 1, BANK - P, BANK)
        load_ws(0)
        load_ws(1)
        order_w1(1, w1_rest[:, :, 0 : PASS // 2], nc.vector.tensor_copy, 0, PACK)
        nc.vector.tensor_scalar(inv_gain[:], inv_raw[:], LARGEST, -LARGEST, ALU.min, ALU.max)
        order_w1(2, w1_rest[:, :, PASS // 2 : PASS], nc.vector.tensor_copy, 0, PACK)
        load_ws(2)
        for lo in (0, BANK // 2):
            for r in range(2):
                project_part(r, 0, lo, lo + BANK // 2)
        project_part(0, 1, 0, BANK - P)
        project_part(0, 1, BANK - P, BANK)
        project_part(1, 1, 0, BANK)
        for r in range(2, AHEAD):
            project(r)

        def piece(b, i):
            return slice(WS_PIECE * i, WS_PIECE * (i + 1) if b == 1 or i == 0 else N - P)

        def weave(dst, src, copy):
            copy(dst.rearrange("p (c i) t -> p c t i", i=RUN), src.rearrange("p t (c i) -> p c t i", i=RUN))

        def weave_ws(b, i, copy):
            cols = piece(b, i)
            if b == 0:
                ws_bf[b, i] = staged([P, cols.stop - cols.start, PACK], BF16, "ws_bf0_%d" % i, AT_H + H_BYTES * (WOVEN_ON + i))
            else:
                ws_bf[b, i] = tile([P, cols.stop - cols.start, PACK], BF16, "ws_bf%d_%d" % (b, i))
            if (b, i) == (0, 1):
                weave(ws_bf[b, i][:, 0:P, :], ws_raw[b][:, :, cols.start : cols.start + P], copy)
            else:
                weave(ws_bf[b, i][:], ws_raw[b][:, :, cols], copy)

        def quantize_ws(b, i):
            cols = piece(b, i)
            if (b, i) == (0, 0):
                ws_s[b] = staged([P, N], U8, "ws_s0", AT_WEIGHTS + WEIGHT_BYTES * (WOVEN_ON + 1))
            elif i == 0:
                ws_s[b] = tile([P, N], U8, "ws_s%d" % b)
            nc.vector.quantize_mx(ws_q[b][:, cols].bitcast(FP8X4), ws_s[b][:, cols], ws_bf[b, i][:].rearrange("p n t -> p (n t)"))

        last_bf = staged([P, 2, P, PACK], BF16, "last_bf", AT_Z_EARLY)
        last_q = tile([P, 2 * P], U32, "last_q")
        last_s = tile([P, 2 * P], U8, "last_s")

        def stationary(b, n):
            if n == N // P - 1 and b != 1:
                cols = slice(P * (b // 2), P * (b // 2 + 1))
                return last_q[:, cols], last_s[:, cols]
            cols = slice(P * n, P * (n + 1))
            return ws_q[b][:, cols], ws_s[b][:, cols]

        units = [(0, 0, SLOTS), (1, 0, SLOTS), (2, 0, EARLY), (2, EARLY, LATE)]
        unit_at = [0, 2 * UNIT_BYTES, 0, 0]
        ux = {}
        th = {}
        z = [tile([P, w, PACK], BF16, "z%d" % u) for u, (b, c, w) in enumerate(units[:-2])]
        z.append(staged([P, EARLY, PACK], BF16, "z_early", AT_Z_EARLY))
        z.append(staged([P, LATE, PACK], BF16, "z_last", AT_RES + 4 * EARLY * (N // P - 1)))
        z_q = [tile([P, w], U32, "z_q%d" % u) for u, (b, c, w) in enumerate(units)]
        z_s = [tile([P, w], U8, "z_s%d" % u) for u, (b, c, w) in enumerate(units)]

        def pick(u, t):
            b, c, w = units[u]
            if t == 0:
                ux[u] = staged([P, PACK, w + STAGGER], F32, "ux%d" % u, AT_UNITS + unit_at[u])
                th[u] = staged([P, PACK, w + STAGGER], F32, "th%d" % u, AT_UNITS + unit_at[u] + PACK * w * 4 + 64)
            looked_up = h[PACK * b + t][:].indirect(picks[:, c // LIST : (c + w) // LIST])
            nc.vector.tensor_tensor(ux[u][:, t, 0:w], looked_up, weights[PACK * b + t][:, c : c + w], ALU.mult)

        def gate(u, t):
            b, c, w = units[u]
            nc.scalar.activation(th[u][:, t, 0:w], ux[u][:, t, 0:w], ACT.Tanh, scale=inv_gain[:, b, t : t + 1])

        def weave_z(u, lo, hi):
            nc.vector.scalar_tensor_tensor(
                z[u][:, lo:hi, :],
                th[u][:, :, lo:hi].rearrange("p t m -> p m t"),
                3.0,
                ux[u][:, :, lo:hi].rearrange("p t m -> p m t"),
                ALU.add,
                ALU.mult,
            )

        def quantize_z(u, lo, hi):
            nc.vector.quantize_mx(z_q[u][:, lo:hi].bitcast(FP8X4), z_s[u][:, lo:hi], z[u][:, lo:hi, :].rearrange("p m t -> p (m t)"))

        parts = [(0, EARLY, 1), (EARLY, LATE, 3)]
        widths = [(HALF, LATE), (LATE,)]
        scores = {}

        def score(part, b, tiles):
            c, w, per_bank = parts[part]
            u = b if b < H_PASSES - 1 else b + part
            for n in tiles:
                g, e = divmod(n, per_bank)
                opens = (part, g) not in scores
                if opens:
                    scores[part, g] = psum.tile([P, per_bank, w], F32, name="score", tag="bank%d" % (H_BANKS if not scores else (len(sums) + len(scores) - 1) % H_BANKS))
                done = 0
                for width in widths[part]:
                    lo = c - units[u][1] + done
                    nc.tensor.matmul_mx(
                        scores[part, g][:, e, done : done + width],
                        lhsT=stationary(b, n)[0].bitcast(FP8X4),
                        lhsT_scale=stationary(b, n)[1],
                        rhs=z_q[u][:, lo : lo + width].bitcast(FP8X4),
                        rhs_scale=z_s[u][:, lo : lo + width],
                        start=(opens and done == 0),
                        stop=(b == H_PASSES - 1 and e == per_bank - 1 and done + width == w),
                    )
                    done += width

        def store(part, g, copy):
            c, w, per_bank = parts[part]
            out_rows = per_bank * P
            at = AT_RES + 4 * (c * (N // P) + g * per_bank * w)
            res = staged([P, per_bank, w], F32, "res%d_%d" % (part, g), at)
            copy(res[:], scores[part, g][:])
            nc.sync.dma_start(out[out_rows * g : out_rows * (g + 1), c : c + w].rearrange("(e p) m -> p e m", p=P), res[:])

        steps = [(u, t) for u in range(len(units)) for t in range(PACK)]
        last_projected = SLICES - 1 - AHEAD
        pieces = N // WS_PIECE
        weave_steps = [WOVEN_ON, WOVEN_ON + 1, 6, 9]
        score_steps = [last_projected, 3 * PACK - 1]
        last_pass, last_unit = H_PASSES - 1, len(units) - 1
        for s, (u, t) in enumerate(steps[:-PACK]):
            pick(u, t)
            if s <= last_projected:
                project(s + AHEAD)
            if s > 0:
                gate(*steps[s - 1])
            if s == len(steps) - PACK - 1:
                gate(u, t)
            if s in weave_steps:
                b, i = divmod(weave_steps.index(s), pieces)
                weave_ws(b, i, nc.vector.tensor_copy if b == 0 else nc.scalar.copy)
            if u > 0 and t == 1:
                for lo in (0, HALF):
                    weave_z(u - 1, lo, lo + HALF)
                for lo in (0, HALF):
                    quantize_z(u - 1, lo, lo + HALF)
            if s == last_projected - 1:
                weave(ws_bf[0, 1][:, P : 2 * P, :], ws_raw[0][:, :, WS_PIECE + P : N - P], nc.scalar.copy)
            if s == last_projected:
                quantize_ws(0, 1)
            if s - 1 in weave_steps and s - 1 != WOVEN_ON + 1:
                quantize_ws(*divmod(weave_steps.index(s - 1), pieces))
            if s in score_steps:
                for part in range(len(parts)):
                    score(part, score_steps.index(s), range(N // P - (s == score_steps[0])))

        tiles = N // P
        for i in range(pieces):
            weave_ws(last_pass, i, nc.scalar.copy)
        weave_z(last_unit - 1, 0, EARLY)
        weave(last_bf[:, 0], ws_raw[0][:, :, N - P : N], nc.scalar.copy)
        for t in range(PACK):
            pick(last_unit, t)
            if t == 0:
                quantize_z(last_unit - 1, 0, EARLY)
                quantize_ws(last_pass, 0)
                score(0, last_pass, range(tiles // 2))
            gate(last_unit, t)
            if t == 0:
                store(0, 0, nc.scalar.copy)
        weave(last_bf[:, 1], ws_raw[last_pass][:, :, N - P : N], nc.vector.tensor_copy)
        quantize_ws(last_pass, 1)
        nc.vector.quantize_mx(last_q[:].bitcast(FP8X4), last_s[:], last_bf[:].rearrange("p b n t -> p (b n t)"))
        for part in range(len(parts)):
            score(part, 0, [tiles - 1])
        score(0, last_pass, range(tiles // 2, tiles))
        weave_z(last_unit, 0, LATE)
        quantize_z(last_unit, 0, LATE)
        score(1, last_pass, range(tiles))
        for g in range(1, tiles):
            store(0, g, nc.vector.tensor_copy if g == tiles - 1 else nc.scalar.copy)
        store(1, 0, nc.vector.tensor_copy)
        store(1, 1, nc.scalar.copy)
